import numpy as np, ml_dtypes
CORES = [48,51,52,55]
N = 4
BF = ml_dtypes.bfloat16
def gentries(a):
    return np.ascontiguousarray(a.reshape(8, 16, -1).transpose(0, 2, 1)).reshape(8, -1)
def gtable(e):
    e = np.asarray(e); return np.ascontiguousarray(e.reshape(8, -1, 16).transpose(0, 2, 1)).reshape(128, -1).astype(np.int32)
W, K, L, T = 4608, 1024, 1, 3
TOP, NEG, EMPTY = 255, 9, 16
def parts(rng):
    j = rng.integers(0, W, (N, 8, 16, W), dtype=np.int32)
    x = rng.integers(0, 16, (N, 8, N, L, K)); x = np.where(rng.random(x.shape) < 0.125, EMPTY, x)
    return j, x, rng.integers(0, 16, (N, 8, K)), rng.integers(0, W, (N, 8, T, K))
def coef(rng, drift):
    c = drift + 50.0 * rng.standard_normal((N, 8, 1, W), dtype=np.float32) + 40.0 * rng.standard_normal((N, 8, 16, W), dtype=np.float32)
    return np.minimum(np.maximum(np.rint(c), -128), 127)
def pack(j, c, x, y, a):
    return {"jm": np.ascontiguousarray(j.reshape(N, 128, W)).astype(np.int32), "cf": (np.ascontiguousarray(c.reshape(N, 128, W)).astype(np.float32) + 0.0).astype(BF),
            "lt": np.ascontiguousarray(x.reshape(N, 8, N * L * K)).astype(np.float32).astype(BF), "y0": np.ascontiguousarray(y).astype(np.float32).astype(BF),
            "st": np.stack([gtable(q.reshape(8, T * K)) for q in a])}
def setup_inputs(rng):
    j, x, y, a = parts(rng)
    return pack(j, coef(rng, rng.choice(np.array([5.0, 15.0, 30.0, 45.0]), (N, 8, 1, 1))), x, y, a)
def setup_inputs_ties(rng):
    j, x, y, a = parts(rng); n = rng.choice(np.array([4, 6, 7, 8, 9]), (N, 8, 1, W))
    o = np.argsort(rng.random((N, 8, 16, W)), axis=2); c = np.where(o < n, -1, (rng.random(o.shape) < 0.8).astype(np.int64))
    p = rng.permutation(16)[:, None]
    c[:, 0] = np.where(p < 8, -1, 1); c[:, 1] = np.where(p < 9, -1, 1); c[:, 2] = np.where(p < 8, -1, 0)
    return pack(j, c, x, y, a)
def setup_inputs_clip(rng):
    j, x, y, a = parts(rng); s = np.where(rng.random((N, 8, 1, W)) < 0.75, 1, -1)
    c = s * rng.integers(100, 128, (N, 8, 16, W)); c = np.where(rng.random(c.shape) < 0.1, -c, c)
    c[:, 1::2, :5] = -np.abs(c[:, 1::2, :5]) - 1
    r = int(rng.integers(0, N)); x[:, 6, r] = rng.integers(0, 16, (N, L, K)); e = 127 // L
    for d in range(N):
        q = (r + d) % N; c[q, 6] = 1; c[q, 6, 1:8] = -1
        c[q, 6, 8] = -1 if d == 3 else 0
        c[q, 6, 0] = (-128, e, e, 255 - 2 * L * e)[d] if d < 4 else 0
    return pack(j, c, x, y, a)
def setup_inputs_gaps(rng):
    j, x, y, a = parts(rng); x = np.where(rng.random(x.shape) < 0.5, EMPTY, x)
    x[:, 0] = EMPTY; x[:, 1:4] = rng.integers(0, 16, (N, 3, N, L, K))
    for q in range(N):
        for s in range(N):
            if q != s: x[q, 2, s] = EMPTY
            if q != (s - 1) % N: x[q, 3, s] = EMPTY
    c = coef(rng, 20.0); r = int(rng.integers(0, N))
    c[r, 0] = -rng.integers(1, 129, (16, W)); c[r, 1] = -128; c[r, 1, 8:] += (rng.random(W) < 0.5).astype(np.float32)
    x[r, 1, r, 1:] = EMPTY
    return pack(j, c, x, y, a)
def setup_inputs_alike(rng):
    j, x, y, a = parts(rng)
    j[:, ::2] = rng.choice(np.array([0, W - 1, W // 2, 5], np.int32), (N, 4, 16, W)); j[:, 1] = np.arange(W)
    j[:, 6] = rng.integers(0, W, (N, 1, 1))
    x[:, 3] = rng.integers(0, 16, (N, 1, 1, 1)); y[:, 3] = rng.integers(0, 16, (N, 1))
    a[:, 2] = rng.integers(0, W, (N, 1, 1)); a[:, 5] = rng.choice(np.array([0, W - 1]), (N, T, K))
    c = coef(rng, 25.0); r = int(rng.integers(0, N)); c[r] = np.minimum(np.abs(c[r]), 127)
    return pack(j, c, x, y, a)
def setup_inputs_spread(rng):
    j, x, y, a = parts(rng)
    j = np.minimum((W * rng.random(j.shape) ** 3).astype(np.int64), W - 1); a = np.minimum((W * rng.random(a.shape) ** 3).astype(np.int64), W - 1)
    c = np.exp2(8.0 * rng.random((N, 8, 1, W))) * (0.5 * rng.standard_normal((N, 8, 16, W)) + 0.25)
    x = np.minimum((17 * rng.random(x.shape) ** 2).astype(np.int64), EMPTY); y = np.minimum((16 * rng.random(y.shape) ** 2).astype(np.int64), 15)
    return pack(j, np.minimum(np.maximum(np.rint(c), -128), 127), x, y, a)
def check_inputs(d):
    bad = []
    for k, lo, hi in (("jm", 0, W - 1), ("cf", -128, 127), ("lt", 0, 16), ("y0", 0, 15), ("st", 0, W - 1)):
        a = np.asarray(d[k]).astype(np.float32)
        if not (np.all(a == np.floor(a)) and np.min(a) >= lo and np.max(a) <= hi): bad.append("range of " + k)
        if np.any(np.signbit(a) & (a == 0)): bad.append("-0.0 in " + k)
    return bad
def reference(jm, cf, lt, y0, st):
    J = jm.astype(np.int64).reshape(N, 8, 16, W); C = cf.astype(np.float32).astype(np.int64).reshape(N, 8, 16, W)
    x = lt.astype(np.float32).astype(np.int64).reshape(N, 8, N, L, K); y = y0.astype(np.float32).astype(np.int64)
    start = np.stack([gentries(a) for a in st]).astype(np.int64).reshape(N, 8, T, K)
    new = np.full((N, 8, T, K), EMPTY, np.int64); v = np.zeros((N, 8, 16, K), np.int64); g = np.arange(8)[:, None]
    for t in range(T):
        for s in range(N):
            b = J[s][g, y[s], start[s, :, t]]; u = np.take_along_axis(C[s], b[:, None, :], 2)
            live = np.ones((8, K), bool)
            for d in range(N):
                q = (s + d) % N
                slots = [new[s, :, i] for i in range(t - 1, -1, -1)] if d == 0 else []
                for z in slots + [x[q, :, s, l] for l in range(L)]:
                    go = live & (z < EMPTY)
                    b = np.where(go, J[q][g, np.minimum(z, 15), b], b)
                    w = np.minimum(np.maximum(u + np.take_along_axis(C[q], b[:, None, :], 2), -TOP), TOP)
                    u = np.where(go[:, None, :], w, u)
                    hit = go & (np.add.reduce((u < 0).astype(np.int64), axis=1) >= NEG)
                    z[hit] = EMPTY; live = live & ~hit
            new[s, :, t] = np.where(live, y[s], EMPTY)
            y[s] = np.argmax(u, axis=1)
            v[s] = u
    return {"yl": x.reshape(N, 8, N * L * K).astype(np.float32).astype(BF), "yi": new.reshape(N, 8, T * K).astype(np.float32).astype(BF), "yv": v.reshape(N, 128, K).astype(np.float32).astype(BF)}

@@ -1,0 +1,556 @@
+from concourse.mybir import AluOpType as A, ActivationFunctionType as F
+
+N, K, TW, W = 4, 1024, 3, 4608
+HALF = K // 2
+NC = K // 16
+SH = 16
+WIN = SH + 5120
+PH = 2048
+OFF = float(SH + PH)
+FLAG = -16384.0
+BYSCALAR = {(2, -2): (0, 1), (2, -1): (0, 1), (2, 0): (0, 1), (2, 1): (1,)}
+SIGNV = ((TW - 1, N - 1),)
+NU, NF, NB, NH = 40, 64, 64, 30
+
+SCRATCH = {
+    "jint": ("sbuf", [128, W], "int32"), "jw": ("sbuf", [128, WIN], "float32"),
+    "cw": ("sbuf", [128, WIN], "bfloat16"), "cw3": ("sbuf", [128, WIN], "bfloat16"), "cst": ("sbuf", [128, 512], "bfloat16"),
+    "ltn": ("sbuf", [8, N * K], "bfloat16"), "y0n": ("sbuf", [8, K], "bfloat16"),
+    "sti": ("sbuf", [128, TW * NC], "int32"), "sta": ("sbuf", [128, TW * NC], "float32"),
+    "stb": ("sbuf", [128, TW * NC], "float32"), "stu": ("sbuf", [128, TW * NC], "uint16"),
+    "eb": ("sbuf", [128, 2048], "bfloat16"), "blk": ("sbuf", [128, 128], "bfloat16"),
+    "idb": ("sbuf", [128, 128], "bfloat16"), "idn": ("sbuf", [128, 128], "bfloat16"), "idm": ("sbuf", [128, 128], "bfloat16"),
+    "hx": ("sbuf", [128, 128], "bfloat16"), "gx": ("sbuf", [8, 2048], "bfloat16"), "bc8": ("sbuf", [8, 128], "bfloat16"),
+    "pidx": ("sbuf", [128, 1], "int32"), "pxi": ("sbuf", [128, 1], "int32"), "xcol": ("sbuf", [128, 1], "float32"),
+    "negx": ("sbuf", [128, 1], "float32"), "ecol": ("sbuf", [128, 1], "float32"),
+    "jl0": ("sbuf", [128, NC], "float32"), "jl": ("sbuf", [128, NC], "float16"),
+    "dl": ("sbuf", [128, HALF], "float32"), "ha": ("sbuf", [128, HALF], "bfloat16"),
+    "lu": ("sbuf", [128, NC * NU], "uint16"), "lf": ("sbuf", [128, NC * NF], "float32"),
+    "lb": ("sbuf", [128, NC * NB], "bfloat16"), "lh": ("sbuf", [128, NC * NH], "float16"),
+    "l0n": ("sbuf", [128, NC * N], "bfloat16"), "zn0": ("sbuf", [128, NC * N], "bfloat16"), "absn": ("sbuf", [128, NC * N], "float32"),
+    "mi": ("sbuf", [128, 32 * 4], "int32"),
+    "js1": ("sbuf", [128, K], "float32"), "js2": ("sbuf", [128, K], "float32"),
+}
+BANKS = ("xa0", "xa1", "xc", "kt0", "kt1", "nt0", "nt1", "ms")
+for _i in BANKS:
+    SCRATCH[_i] = ("psum", [128, 512], "float32")
+for _i in range(N):
+    SCRATCH["mk%d" % _i] = ("sbuf", [128, K], "bfloat16")
+for _i in range(3):
+    SCRATCH["mt%d" % _i] = ("sbuf", [128, HALF], "bfloat16")
+    SCRATCH["md%d" % _i] = ("sbuf", [128, K], "float16")
+    for _n in ("v", "tm", "sg"):
+        SCRATCH[_n + str(_i)] = ("sbuf", [128, K], "bfloat16")
+for _i in range(7):
+    SCRATCH["no%d" % _i] = ("sbuf", [8, K], "bfloat16")
+for _i in range(2):
+    SCRATCH["my%d" % _i] = ("sbuf", [128, K], "bfloat16")
+    SCRATCH["yn%d" % _i] = ("sbuf", [8, K], "bfloat16")
+    SCRATCH["gh%d" % _i] = ("sbuf", [128, HALF], "bfloat16")
+    SCRATCH["run%d" % _i] = ("sbuf", [128, HALF], "float32")
+    SCRATCH["bz%d" % _i] = ("sbuf", [128, HALF], "bfloat16")
+    SCRATCH["hs%d" % _i] = ("sbuf", [128, HALF], "bfloat16")
+SEMAPHORES = ["vq", "sq", "pq", "gq", "snt", "rcw"] + ["ld%d" % i for i in range(10)] + ["st%d" % i for i in range(8)]
+for _d in range(1, N):
+    SCRATCH["zi%d" % _d] = ("sbuf", [128, NC], "bfloat16")
+    SEMAPHORES.append("rzi%d" % _d)
+for _t in range(TW):
+    SCRATCH["bh%d" % _t] = ("sbuf", [128, NC], "float16")
+    SEMAPHORES.append("rh%d" % _t)
+    for _d in range(1, N):
+        _x = "%d%d" % (_t, _d)
+        SCRATCH["br" + _x] = ("sbuf", [128, NC], "uint16")
+        SCRATCH["fr" + _x] = ("sbuf", [128, NC], "bfloat16")
+        SEMAPHORES += ["rb" + _x, "rf" + _x]
+        if _d < N - 1:
+            SCRATCH["cg" + _x] = ("sbuf", [128, 2 * (SH + HALF)], "bfloat16")
+            SCRATCH["cs" + _x] = ("sbuf", [128, SH + K], "bfloat16")
+            SEMAPHORES += ["rc%s0" % _x, "rc%s1" % _x]
+
+
+def add(pl, eng, cost, reads, writes, fn, sem=None, lat=0.0, inc=None, after=None, kind="c"):
+    tasks, last, rd = pl["tasks"], pl["last"], pl["rd"]
+    i = len(tasks)
+    deps = set(last[k] for k in list(reads) + list(writes) if k in last)
+    for k in reads:
+        if k in BANKS:
+            deps |= set(j for j in rd.get(k, []) if tasks[j]["eng"] != eng)
+    for k in writes:
+        deps |= set(rd.get(k, []))
+    for k in reads:
+        rd.setdefault(k, []).append(i)
+    for k in writes:
+        last[k] = i
+        rd[k] = []
+    deps.discard(i)
+    tdeps = deps if after is None else deps | set([after])
+    tasks.append({"eng": eng, "cost": cost, "deps": sorted(deps), "tdeps": sorted(tdeps), "fn": fn, "sem": sem, "lat": lat,
+                  "inc": inc, "kind": kind})
+    return i
+
+
+def order(tasks):
+    n = len(tasks)
+    succ = [[] for _ in range(n)]
+    for i in range(n):
+        for j in tasks[i]["tdeps"]:
+            succ[j].append(i)
+    pri = [0.0] * n
+    own = [0.0] * n
+    for i in range(n - 1, -1, -1):
+        pri[i] = max([pri[j] for j in succ[i]] + [0.0]) + tasks[i]["cost"] + tasks[i]["lat"]
+        own[i] = 1e6 - i if "first" in tasks[i] else pri[i]
+    left = [len(tasks[i]["tdeps"]) for i in range(n)]
+    rt = [0.0] * n
+    todo = [i for i in range(n) if left[i] == 0]
+    busy = {}
+    start = [0.0] * n
+    while todo:
+        i = max(todo, key=lambda a: (own[a], -a))
+        todo.remove(i)
+        e, c = tasks[i]["eng"], tasks[i]["cost"]
+        s = rt[i]
+        if e != "R":
+            b = busy.setdefault(e, [])
+            k = 0
+            while k < len(b) and b[k][1] <= s:
+                k += 1
+            while k < len(b) and b[k][0] < s + c:
+                s = max(s, b[k][1])
+                k += 1
+            b.insert(k, (s, s + c))
+        start[i] = s
+        for j in succ[i]:
+            left[j] -= 1
+            rt[j] = max(rt[j], s + c + tasks[i]["lat"] + (0.03 if tasks[j]["eng"] == e else 0.08))
+            if left[j] == 0:
+                todo.append(j)
+    return sorted(range(n), key=lambda a: (start[a], a))
+
+
+def emit(g, T, tasks):
+    seq = order(tasks)
+    pos = dict((a, b) for b, a in enumerate(seq))
+    q = {"V": g.vector, "S": g.scalar, "P": g.tensor, "G": g, "Y": g.sync}
+    qsem = {"V": "vq", "S": "sq", "P": "pq", "G": "gq"}
+    count = {}
+    known = dict((e, {}) for e in q)
+    tok = {}
+    know = {}
+    for i in seq:
+        t = tasks[i]
+        e = t["eng"]
+        if e == "R":
+            tok[i] = (t["sem"], t["inc"])
+            know[i] = {t["sem"]: t["inc"]}
+            continue
+        kn = known[e]
+        for j in sorted(t["deps"], key=lambda a: -pos[a]):
+            s, v = tok[j]
+            if kn.get(s, 0) >= v:
+                continue
+            q[e].wait_ge(T.sem[s], v)
+            for s2 in know[j]:
+                kn[s2] = max(kn.get(s2, 0), know[j][s2])
+        ins = t["fn"]()
+        if t["kind"] == "c":
+            s = qsem[e]
+            for x in ins:
+                x.then_inc(T.sem[s], 1)
+            count[s] = count.get(s, 0) + len(ins)
+        elif t["kind"] == "d":
+            s = t["sem"]
+            ins[0].then_inc(T.sem[s], 16)
+            count[s] = 16
+        else:
+            s = "snt"
+            count[s] = count.get(s, 0) + t["inc"]
+        tok[i] = (s, count[s])
+        know[i] = dict(kn)
+        know[i][s] = count[s]
+    for s in count:
+        if known["G"].get(s, 0) < count[s]:
+            g.wait_ge(T.sem[s], count[s])
+
+
+def rank_program(g, core, T, topo):
+    rank = T.rank_of(core)
+    if rank is None:
+        return
+    pl = {"tasks": [], "last": {}, "rd": {}}
+    vec, sca, ten, syn = g.vector, g.scalar, g.tensor, g.sync
+    cores = T.cores
+    used = {}
+
+    def take(kind):
+        used[kind] = used.get(kind, -1) + 1
+        return used[kind]
+
+    def new(buf):
+        n = take(buf)
+        t = T[buf]
+        return (t[:, NC * n:NC * n + NC], "%s.%d" % (buf, n), [t[:, NC * n + 32 * h:NC * n + 32 * h + 32] for h in range(2)])
+
+    def rot(kind, n=3):
+        return kind + str(take(kind) % n)
+
+    def vts(out, ok, in0, ik, s1, s2, op0, op1, cost=0.08, more=()):
+        args = (out, in0, s1, s2, op0) if op1 is None else (out, in0, s1, s2, op0, op1)
+        return add(pl, "V", cost, [ik] + list(more), [ok], lambda: [vec.tensor_scalar(*args)])
+
+    def vtt(out, ok, a, ak, b, bk, op, cost=0.08):
+        return add(pl, "V", cost, [ak, bk], [ok], lambda: [vec.tensor_tensor(out, a, b, op)])
+
+    def vcp(out, ok, a, ak, cost=0.08):
+        return add(pl, "V", cost, [ak], [ok], lambda: [vec.tensor_copy(out, a)])
+
+    def act(out, ok, in_, reads, func, cost, **kw):
+        return add(pl, "S", cost, reads, [ok], lambda: [sca.activation(out, in_, func, **kw)])
+
+    def scan(out, ok, d0, d0k, d1, d1k, op0, op1, cost):
+        return add(pl, "V", cost, [d0k, d1k], [ok], lambda: [vec.tensor_tensor_scan(out, d0, d1, 0.0, op0, op1)])
+
+    def mm(group, reads, writes, cost):
+        return add(pl, "P", cost, reads, writes, lambda: [ten.matmul(*x) for x in group])
+
+    def memset(ap, key, c, cost=0.08):
+        return add(pl, "V", cost, [], [key], lambda: [vec.memset(ap, c)])
+
+    def send(out, in_, sem, to, reads, key, lat, bulk=False):
+        dst = cores[to]
+        rid, pid, _ = topo.addr(dst)
+        en = topo.engines(core, dst)
+        en = en[1::2] if bulk else en[0::2]
+        n = len(en)
+        m = sum(1 << x for x in en)
+        i = add(pl, "G", 0.4, reads, [], lambda: [g.remote_dma(out, in_, T.sem[sem], T.sem.snt, pid, rid, m)], inc=n, kind="r")
+        return lambda: add(pl, "R", 0.0, [], key, None, sem=sem, inc=n, after=i, lat=lat)
+
+    def load(eng, out, in_, key, lat):
+        qq = syn if eng == "Y" else sca
+        i = add(pl, eng, 0.1, [], [key], lambda: [qq.dma_start(out, in_)], sem="ld%d" % take("ld"), lat=lat, kind="d")
+        pl["tasks"][i]["first"] = True
+
+    def store(out, in_, reads):
+        add(pl, "Y", 0.1, reads, [], lambda: [syn.dma_start(out, in_)], sem="st%d" % take("st"), lat=2.0, kind="d")
+
+    def halves(k):
+        return [k + ".0", k + ".1"]
+
+    HS = [slice(0, HALF), slice(HALF, K)]
+
+    load("S", T.y0n[:], T.y0[:], "y0n", 3.0)
+    load("S", T.sti[:], T.st[:], "sti", 3.2)
+    load("S", T.ltn[:], T.lt[:], "ltn", 5.0)
+    at = 2.0
+    for p in range(5):
+        a, b = 1024 * p, min(W, 1024 * p + 1024)
+        at += (b - a) * 512 / 2.2e5
+        load("Y", T.jint[:, a:b], T.jm[:, a:b], "jint%d" % p, at)
+    load("Y", T.cst[:], T.cf[:, 4096:W], "cst", at + 0.9)
+    load("Y", T.cw[:, SH:SH + 4096], T.cf[:, 0:4096], "cwa", at + 5.4)
+
+    def gsel(ap, key, pat, op, base, cm, cost=0.42, after=None):
+        return add(pl, "G", cost, [key], [key], lambda: [g.affine_select(ap, ap, pat, op, 0.0, base, cm)], after=after)
+    memset(T.idb[:], "idb", 1.0, 0.15)
+    memset(T.blk[:], "blk", 1.0, 0.15)
+    memset(T.bc8[:], "bc8", 1.0, 0.15)
+    memset(T.eb[:], "eb", 0.0, 0.9)
+    memset(T.gx[:], "gx", 1.0, 0.9)
+    memset(T.hx[:], "hx", -1.0 / 1024.0, 0.15)
+    add(pl, "G", 0.14, [], ["pidx"], lambda: [g.iota(T.pidx[:], [[1, 1]], 0, 1)])
+    gsel(T.blk[:], "blk", [[-16, 8], [0, 16]], A.is_ge, 0, 1)
+    i = gsel(T.blk[:], "blk", [[16, 8], [0, 16]], A.is_ge, 15, -1)
+    gsel(T.bc8[:], "bc8", [[-1, 8], [0, 16]], A.is_equal, 0, 1)
+    i = gsel(T.idb[:], "idb", [[-1, 128]], A.is_equal, 0, 1, 0.42, i)
+    add(pl, "G", 0.25, [], ["jl0"], lambda: [g.iota(T.jl0[:], [[0, 2], [16, NC // 2]], -PH, 0, allow_small_or_imprecise_dtypes=True)])
+    gsel(T.hx[:], "hx", [[-1, 16], [-16, 8]], A.is_equal, 0, 1, 0.42, i)
+    gsel(T.gx[:], "gx", [[1, 16], [-16, 8], [-1, 16]], A.is_equal, 0, 16, 3.6, i)
+
+    add(pl, "V", 0.06, ["pidx"], ["pxi"], lambda: [vec.tensor_scalar(T.pxi[:], T.pidx[:], 15, None, A.bitwise_and)])
+    vcp(T.xcol[:], "xcol", T.pxi[:], "pxi")
+    vts(T.negx[:], "negx", T.xcol[:], "xcol", -1.0, None, A.mult, None)
+    vts(T.ecol[:], "ecol", T.xcol[:], "xcol", -1.0 / 16.0, 15.0 / 16.0, A.mult, A.add)
+    vts(T.jl[:], "jl", T.jl0[:], "jl0", T.xcol[:, 0:1], None, A.add, None, more=["xcol"])
+    add(pl, "S", 1.3, ["blk"], ["eb"],
+        lambda: [sca.activation(T.eb[:, 128 * x + x:128 * x + 128:16], T.blk[:, x:128:16], F.Copy) for x in range(16)])
+    vts(T.idn[:], "idn", T.idb[:], "idb", -1.0, None, A.mult, None, 0.12)
+    vts(T.idm[:], "idm", T.idb[:], "idb", -0.5, None, A.mult, None, 0.12)
+    memset(T.dl[:], "dl", 1.0 / 16.0, 0.45)
+    memset(T.dl[:, 0:HALF:16], "dl", -1000.0)
+    memset(T.ha[:], "ha", 1.0, 0.3)
+    memset(T.ha[:, 0:HALF:16], "ha", 0.0)
+    memset(T.bz0[:], "bz0", 0.0, 0.3)
+    memset(T.bz1[:], "bz1", 0.0, 0.3)
+    memset(T.jw[:, 0:SH], "jwz", 0.0)
+    memset(T.jw[:, SH + 4096:WIN], "jwu", 0.0, 0.9)
+    memset(T.cw[:, 0:SH], "cwz", 0.0)
+    memset(T.cw[:, SH + 4096:WIN], "cwu", 0.0, 0.5)
+    for t in range(TW):
+        for d in range(1, N - 1):
+            x = "%d%d" % (t, d)
+            memset(T["cg" + x][:, 0:SH], "cgz" + x, 0.0)
+            memset(T["cs" + x][:, HALF:HALF + SH], "csz" + x, 0.0)
+
+    for h in range(2):
+        nt = "nt%d" % h
+        mm([(T[nt][:, 0:HALF], T.bc8[:], T.y0n[:, HS[h]], True, True)], ["bc8", "y0n"], [nt], 0.35)
+        vts(T.my0[:, HS[h]], "my0.%d" % h, T[nt][:, 0:HALF], nt, T.xcol[:, 0:1], None, A.is_equal, None, 0.5, ["xcol"])
+    mm([(T.ms[:, 0:256], T.gx[:, 128 * r:128 * r + 128], T.ltn[:, r:N * K:16], r == 0, r == 15) for r in range(16)],
+       ["gx", "ltn"], ["ms"], 2.5)
+    vts(T.zn0[:], "zn0", T.ms[:, 0:256], "ms", 15.5, FLAG, A.is_ge, A.mult, 0.25)
+    vts(T.absn[:], "absn", T.ms[:, 0:256], "ms", 15.5, None, A.is_ge, None, 0.25)
+    vts(T.l0n[:], "l0n", T.ms[:, 0:256], "ms", -1024.0, None, A.mult, None, 0.25)
+    for d in range(N):
+        for h in range(2):
+            bk = ("xa0", "xa1", "xc")[take("mb") % 3]
+            mt = rot("mt")
+            c = ((rank - d) % N) * K + HALF * h
+            mm([(T[bk][:, 0:HALF], T.bc8[:], T.ltn[:, c:c + HALF], True, True)], ["bc8", "ltn"], [bk], 0.35)
+            act(T[mt][:], mt, T[bk][:, 0:HALF], [bk, "negx"], F.Abs, 0.5, bias=T.negx[:, 0:1])
+            act(T["mk%d" % d][:, HS[h]], "mk%d.%d" % (d, h), T[mt][:], [mt], F.Relu, 0.5, bias=1.0, scale=-1.0)
+    for d in range(1, N):
+        s = (rank - d) % N
+        send(T["zi%d" % d][:], T.zn0[:, NC * s:NC * s + NC], "rzi%d" % d, s, ["zn0"], ["zi%d" % d], 2.0)()
+
+    vts(T.sta[:], "sta", T.sti[:], "sti", 2.0, -4096.0, A.mult, A.add, 0.2)
+    vtt(T.stb[:], "stb", T.sti[:], "sti", T.sta[:], "sta", A.max, 0.35)
+    vts(T.stu[:], "stu", T.stb[:], "stb", float(SH), None, A.add, None, 0.2)
+    for p in range(9):
+        bk = "kt%d" % (p % 2)
+        a = 512 * p
+        src, ik = T.jint[:, a:a + 512], "jint%d" % (p // 2)
+        vts(T[bk][:], bk, src, ik, 4096.0, -6144.0, A.max, A.add, 0.48)
+        out, ok = (T.jw[:, SH + a:SH + a + 512], "jw%d" % p) if p < 8 else (T.jw[:, SH + 4096:WIN:2], "jwu")
+        vtt(out, ok, src, ik, T[bk][:], bk, A.add, 0.48)
+    JW = ["jwz", "jwu"] + ["jw%d" % p for p in range(8)]
+    act(T.cw[:, SH + 4096:WIN:2], "cwu", T.cst[:], ["cst"], F.Copy, 0.48)
+    CW = ["cwz", "cwu", "cwa"]
+    send(T.cw3[:], T.cw[:], "rcw", (rank + 1) % N, CW, ["cw3"], 9.0, True)()
+
+    def summed(md, keep=None):
+        bk = rot("xa", 2)
+        x = T[bk][:, 0:NC]
+        grp = [(x, T.eb[:, 128 * r:128 * r + 128], T[md][:, r:K:16], r == 0, r == 15 and keep is None) for r in range(16)]
+        if keep is not None:
+            grp.append((x, T.idb[:], keep[0], False, True))
+        mm(grp, ["eb", "idb"] + halves(md) + ([keep[1]] if keep is not None else []), [bk], 0.65)
+        return x, bk
+
+    def image(lst, lk, mask, mkeys, keep=None):
+        md = rot("md")
+        add(pl, "V", 1.65, JW + [lk] + mkeys, halves(md), lambda: [vec.tensor_tensor(T[md][:], T.jw[:].indirect(lst), mask[:], A.mult)])
+        return summed(md, keep)
+
+    for t in range(1, TW):
+        for h in range(2):
+            c = NC * t + 32 * h
+            act(T["js%d" % t][:, HS[h]], "js%d.%d" % (t, h), T.jw[:].indirect(T.stu[:, c:c + 32]), JW + ["stu"], F.Identity, 0.86)
+
+    def start(t):
+        if t == 0:
+            return image(T.stu[:, 0:NC], "stu", T.my0, halves("my0"))
+        md = rot("md")
+        for h in range(2):
+            kt = "kt%d" % h
+            vtt(T[md][:, HS[h]], "%s.%d" % (md, h), T["js%d" % t][:, HS[h]], "js%d.%d" % (t, h), T[kt][:], kt, A.mult, 0.53)
+        x = summed(md)
+        if t < TW - 1:
+            for h in range(2):
+                act(T["my%d" % t][:, HS[h]], "my%d.%d" % (t, h), T["kt%d" % h][:], ["kt%d" % h], F.Copy, 0.57)
+        return x
+
+    def tolist(x, xk):
+        l = new("lu")
+        vts(l[0], l[1], x, xk, OFF, 0.0, A.add, A.max)
+        return l
+
+    def bslot(lst, lk, mask, mkeys, absent, present, prev, want, wantl):
+        if prev is None:
+            prev = new("lf")
+            vts(prev[0], prev[1], lst, lk, -OFF, None, A.add, None)
+        if present is None:
+            k = new("lh")
+            vtt(k[0], k[1], prev[0], prev[1], absent[0], absent[1], A.mult)
+            x = image(lst, lk, mask, mkeys, k)
+            l = tolist(x[0], x[1]) if wantl else None
+            b = None
+            if want:
+                b = new("lh")
+                vcp(b[0], b[1], x[0], x[1])
+            return b, l
+        k, a, b = new("lf"), new("lf"), new("lh")
+        vtt(k[0], k[1], prev[0], prev[1], absent[0], absent[1], A.mult)
+        x = image(lst, lk, mask, mkeys)
+        vtt(a[0], a[1], x[0], x[1], present[0], present[1], A.mult)
+        vtt(b[0], b[1], a[0], a[1], k[0], k[1], A.add)
+        return b, tolist(b[0], b[1]) if wantl else None
+
+    def flags(z, zk):
+        n, p = new("lf"), new("lf")
+        act(n[0], n[1], z, [zk], F.Copy, 0.15, scale=1.0 / FLAG)
+        act(p[0], p[1], z, [zk], F.Identity, 0.15, bias=1.0, scale=-1.0 / FLAG)
+        return n, p
+
+    def gather_c(out, okeys, l):
+        for h in range(2):
+            act(out[h], okeys[h], T.cw[:].indirect(l[2][h]), CW + [l[1]], F.Identity, 0.86)
+
+    def vslot(v, base, zn, dead, wins, wkeys, at):
+        u = T.xc[:, NC:2 * NC]
+        grp = [(u, T.idb[:], base[0], True, False), (u, T.idb[:], zn[0], False, dead is None)]
+        dk = [] if dead is None else [dead[1]]
+        if dead is not None:
+            grp.append((u, T.idb[:], dead[0], False, True))
+        mm(grp, ["idb", base[1], zn[1]] + dk, ["xc"], 0.1)
+        l = tolist(u, "xc")
+        tm, nv = rot("tm"), rot("v")
+        sg = "sg" + tm[2:]
+        for h in range(2):
+            c = HS[h]
+            vk, tk, sk, nk = ["%s.%d" % (x, h) for x in (v, tm, sg, nv)]
+            vi, src, srk, cl = T[v][:, c], T[tm][:, c], tk, 0.28
+            if h in BYSCALAR.get(at, ()):
+                gh = rot("gh", 2)
+                act(T[gh][:], gh, wins[h].indirect(l[2][h]), wkeys(h) + [l[1]], F.Identity, 0.85)
+                src, srk, cl = T["kt%d" % h][:], "kt%d" % h, 0.55
+                mm([(src, T.idb[:], vi, True, False), (src, T.idb[:], T[gh][:], False, True)], ["idb", vk, gh], [srk], 0.5)
+            else:
+                add(pl, "V", 0.83, wkeys(h) + [l[1], vk], [tk],
+                    lambda src=src, h=h, vi=vi: [vec.tensor_tensor(src, wins[h].indirect(l[2][h]), vi, A.add)])
+            if h and at in SIGNV:
+                vts(T[sg][:, c], sk, src, srk, 0.0, 0.5, A.is_ge, A.subtract, 0.28)
+            else:
+                act(T[sg][:, c], sk, src, [srk], F.Sign, 0.57, bias=0.5)
+            vts(T[nv][:, c], nk, src, srk, 255.0, -255.0, A.min, A.max, cl)
+        o = T.xc[:, 0:NC]
+        grp = [(o, T.idm[:], zn[0], True, False)]
+        if dead is not None:
+            grp.append((o, T.idb[:], dead[0], False, False))
+        grp += [(o, T.eb[:, 128 * r:128 * r + 128], T[sg][:, r:K:16], False, r == 15) for r in range(16)]
+        mm(grp, ["idm", "idb", zn[1], "eb"] + halves(sg) + dk, ["xc"], 0.7)
+        nd, nz = new("lb"), new("lb")
+        vts(nd[0], nd[1], o, "xc", -0.25, FLAG, A.is_le, A.mult)
+        if dead is None:
+            vtt(nz[0], nz[1], zn[0], zn[1], nd[0], nd[1], A.add)
+        elif at == (TW - 1, N - 1):
+            zd = new("lb")
+            vtt(zd[0], zd[1], zn[0], zn[1], dead[0], dead[1], A.subtract)
+            vtt(nz[0], nz[1], zd[0], zd[1], nd[0], nd[1], A.add)
+        else:
+            q = T.ms[:, 0:NC]
+            mm([(q, T.idb[:], zn[0], True, False), (q, T.idn[:], dead[0], False, False), (q, T.idb[:], nd[0], False, True)],
+               ["idb", "idn", zn[1], dead[1], nd[1]], ["ms"], 0.1)
+            act(nz[0], nz[1], q, ["ms"], F.Copy, 0.15)
+        return nv, nd, nz
+
+    def ylist(rows, keys, a, b):
+        l = new("lb")
+        mm([(T.ms[:, 0:NC], T.gx[:, 128 * r:128 * r + 128], rows[:, r:K:16], r == 0, r == 15) for r in range(16)],
+           ["gx"] + keys, ["ms"], 0.7)
+        vts(l[0], l[1], T.ms[:, 0:NC], "ms", a, b, A.mult, A.add)
+        return l
+
+    def letters(y, yk, z, zk, out, oc, bank="nt"):
+        f = new("lb")
+        vtt(f[0], f[1], y, yk, z, zk, A.min)
+        no = rot("no", 7)
+        for h in range(2):
+            nt = bank + str(h)
+            mm([(T[nt][0:8, r:512:16], T.hx[:, 8 * r:8 * r + 8], f[2][h], True, True) for r in range(16)], ["hx", f[1]], [nt], 0.4)
+            if h:
+                vcp(T[no][:, HS[h]], no + ".1", T[nt][0:8, :], nt, 0.55)
+            else:
+                act(T[no][:, HS[h]], no + ".0", T[nt][0:8, :], [nt], F.Copy, 0.57)
+        store(out[:, oc:oc + K], T[no][:], halves(no))
+
+    zn = [(T.zn0[:, NC * rank:NC * rank + NC], "zn0")] + [(T["zi%d" % d][:], "zi%d" % d) for d in range(1, N)]
+    res = []
+    ys = [ylist(T.y0n, ["y0n"], -1024.0, 0.0)]
+    for t in range(TW):
+        x = start(t)
+        l = lstart = tolist(x[0], x[1])
+        todo = [(T["my%d" % i], halves("my%d" % i), res[i]) for i in range(t - 1, -1, -1)] + [(T.mk0, halves("mk0"), zn[0])]
+        chain = []
+        prev = None
+        for mask, mkeys, z in todo:
+            n, p = flags(z[0], z[1]) if t else ((T.absn[:, NC * rank:NC * rank + NC], "absn"), None)
+            prev, l = bslot(l[0], l[1], mask, mkeys, n, p, prev, True, True)
+            chain.append(prev)
+        arrive = send(T["br%d1" % t][:], l[0], "rb%d1" % t, (rank + 1) % N, [l[1]], ["br%d1" % t], 1.9)
+        v = rot("v")
+        gather_c([T[v][:, HS[0]], T[v][:, HS[1]]], halves(v), lstart)
+        dead = None
+        for j in range(len(todo)):
+            v, dead, nz = vslot(v, chain[j], todo[j][2], dead, [T.cw[:], T.cw[:]], lambda h: CW, (t, -j))
+            if j < t:
+                res[t - 1 - j] = nz
+            else:
+                zn[0] = nz
+        pend = []
+        for d in range(1, N):
+            x = "%d%d" % (t, d)
+            arrive()
+            home = (rank - d) % N
+            n, p = flags(T["fr%d%d" % (t - 1, d)][:], "fr%d%d" % (t - 1, d)) if t else ((T.absn[:, NC * home:NC * home + NC], "absn"), None)
+            lastd = d == N - 1
+            b, l = bslot(T["br" + x][:], "br" + x, T["mk%d" % d], halves("mk%d" % d), n, p, None, lastd, not lastd)
+            if lastd:
+                pend.append(send(T["bh%d" % t][:], b[0], "rh%d" % t, home, [b[1]], ["bh%d" % t], 1.9))
+                continue
+            k = "%d%d" % (t, d + 1)
+            arrive = send(T["br" + k][:], l[0], "rb" + k, (rank + 1) % N, [l[1]], ["br" + k], 1.9)
+            cs, cg, ck, ak = T["cs" + x], T["cg" + x], halves("cs" + x), halves("cg" + x)
+            gather_c([cs[:, 0:HALF], cs[:, SH + HALF:SH + K]], ck, l)
+            if d == N - 2:
+                pend.append(send(cg[:, SH:SH + HALF], cs[:, 0:HALF], "rc%s0" % x, home, ck[:1], ak[:1], 2.6, True))
+                pend.append(send(cg[:, SH + HALF:2 * (SH + HALF)], cs[:, HALF:SH + K], "rc%s1" % x, home, [ck[1], "csz" + x], ak[1:], 2.6, True))
+            else:
+                pend.append(send(cg[:, SH:2 * (SH + HALF)], cs[:], "rc%s0" % x, home, ck + ["csz" + x], ak, 3.0, True))
+        for f in pend:
+            f()
+        for d in range(1, N):
+            x = "%d%d" % (t, d)
+            if d == N - 1:
+                v, dead, nz = vslot(v, (T["bh%d" % t][:], "bh%d" % t), zn[d], dead, [T.cw3[:], T.cw3[:]], lambda h: ["cw3"], (t, d))
+            else:
+                cg = T["cg" + x]
+                v, dead, nz = vslot(v, (T.jl[:], "jl"), zn[d], dead, [cg[:, 0:SH + HALF], cg[:, SH + HALF:2 * (SH + HALF)]],
+                                    lambda h, x=x: ["cgz" + x if h == 0 else "cg%s.1" % x, "cg%s.%d" % (x, h)], (t, d))
+            zn[d] = nz
+            send(T["fr" + x][:], nz[0], "rf" + x, (rank + d) % N, [nz[1]], ["fr" + x], 2.0)()
+        res.append(dead)
+        if t < TW - 1:
+            yn = "yn%d" % t
+            for h in range(2):
+                kt, nt, ru = "kt%d" % h, "nt%d" % h, "run%d" % h
+                c0 = HALF * h
+                mm([(T[kt][:, 128 * k:128 * k + 128], T[v][:, c0 + 128 * k:c0 + 128 * k + 128], T.idb[:], True, True) for k in range(4)],
+                   ["%s.%d" % (v, h), "idb"], [kt], 0.35)
+                scan(T[ru][:], ru, T.dl[:], "dl", T[kt][:], kt, A.add, A.max, 0.5)
+                q = 2 * t + h
+                mi, bz, hs = T.mi[:, 32 * q:32 * q + 32], T["bz%d" % h], T["hs%d" % h]
+                vts(mi, "mi%d" % q, T[ru][:, 15:HALF:16], ru, -15.0 / 32.0, None, A.add, None)
+                vtt(bz[:, 0:HALF:16], "bz%d" % h, T[ru][:, 15:HALF:16], ru, mi, "mi%d" % q, A.subtract)
+                scan(hs[:], "hs%d" % h, T.ha[:], "ha", bz[:], "bz%d" % h, A.mult, A.add, 0.3)
+                mm([(T[kt][:, 128 * k:128 * k + 128], hs[:, 128 * k:128 * k + 128], T.idb[:], True, True) for k in range(4)],
+                   ["hs%d" % h, "idb"], [kt], 0.35)
+                vts(T[kt][:], kt, T[kt][:], kt, T.ecol[:, 0:1], None, A.is_equal, None, 0.5, ["ecol"])
+                mm([(T[nt][0:8, 128 * k:128 * k + 128], bz[:, 128 * k:128 * k + 128:16], T.idb[:], True, True) for k in range(4)],
+                   ["bz%d" % h, "idb"], [nt], 0.35)
+                act(T[yn][:, HS[h]], "%s.%d" % (yn, h), T[nt][0:8, :], [nt], F.Copy, 0.57)
+            ys.append(ylist(T[yn], halves(yn), 16384.0, -15360.0))
+
+    store(T.yv[:], T[v][:], halves(v))
+
+    def yl_out(d, bank="nt"):
+        s = (rank - d) % N
+        z = zn[0] if d == 0 else (T["fr%d%d" % (TW - 1, d)][:], "fr%d%d" % (TW - 1, d))
+        letters(T.l0n[:, NC * s:NC * s + NC], "l0n", z[0], z[1], T.yl, s * K, bank)
+
+    def yi_out(t):
+        letters(ys[t][0], ys[t][1], res[t][0], res[t][1], T.yi, t * K)
+    for f, a in ((yi_out, 1), (yi_out, 0), (yl_out, 0), (yl_out, 1), (yl_out, 2), (yi_out, 2)):
+        f(a)
+    yl_out(N - 1, "kt")
+    emit(g, T, pl["tasks"])

@@ -1,71 +1,81 @@
 from concourse.mybir import AluOpType as A, ActivationFunctionType as F
+from concourse.bass import DstId, RemoteDMATransfer
 
 N, K, TW, W = 4, 1024, 3, 4608
-HALF = K // 2
 NC = K // 16
 SH = 16
 WIN = SH + 5120
 PH = 2048
 OFF = float(SH + PH)
-FLAG = -16384.0
-BYSCALAR = {(2, -2): (0, 1), (2, -1): (0, 1), (2, 0): (0, 1), (2, 1): (1,)}
-SIGNV = ((TW - 1, N - 1),)
-NU, NF, NB, NH = 40, 64, 64, 30
+D = 5152
+PRM = {
+    "parts": (32, 32),
+    "remc": ((0, 1), (0, 2)),
+    "sums": {},
+    "sum0": "B", "nd": "S", "xs": "S", "start": "G", "dual": False, "lists16": (1, 2), "lag": 3.0,
+    "f": 1.15, "g": 1.56, "hop": 2.3, "mk": "SSSS", "my0": "S", "cwait": 2, "iota": 5152, "copyat": 0, "jwait": 1, "cge": ("even", "odd", "odd"),
+    "pe": 0.5, "issue": 0.4, "sync": 0.1, "alpha": 6.0, "nudge": (), "dma": 1.0,
+    "jp": [(4096, W), (0, 1024), (1024, 2048), (2048, 3072), (3072, 3584), (3584, 4096)], "copies": (3, 2, 1),
+}
+PRM.update({'sum0': 'A', 'alpha': 15, 'f': 1.1, 'hop': 2.3, 'copyat': 0, 'sums': {(2, 0): 'B', (0, 0): 'D', (2, 2): 'C', (1, 2): 'D'},
+            'xs3': 'V', 'iota': 1288, 'remc': ((0, 1), (0, 2), (1, 1), (2, 1)), "lists16": ()})
+PARTS = PRM["parts"]
+NP = len(PARTS)
+PM = 16 * max(PARTS)
+NU, NF, NB, NH, NRU, NRF, NRB = 44, 24, 48, 24, 10, 10, 8
 
 SCRATCH = {
-    "jint": ("sbuf", [128, W], "int32"), "jw": ("sbuf", [128, WIN], "float32"),
-    "cw": ("sbuf", [128, WIN], "bfloat16"), "cw3": ("sbuf", [128, WIN], "bfloat16"), "cst": ("sbuf", [128, 512], "bfloat16"),
+    "jint": ("sbuf", [128, W], "int32"), "jw": ("sbuf", [128, 2 * D], "float32"),
+    "cst": ("sbuf", [128, 512], "bfloat16"),
     "ltn": ("sbuf", [8, N * K], "bfloat16"), "y0n": ("sbuf", [8, K], "bfloat16"),
-    "sti": ("sbuf", [128, TW * NC], "int32"), "sta": ("sbuf", [128, TW * NC], "float32"),
-    "stb": ("sbuf", [128, TW * NC], "float32"), "stu": ("sbuf", [128, TW * NC], "uint16"),
-    "eb": ("sbuf", [128, 2048], "bfloat16"), "blk": ("sbuf", [128, 128], "bfloat16"),
-    "idb": ("sbuf", [128, 128], "bfloat16"), "idn": ("sbuf", [128, 128], "bfloat16"), "idm": ("sbuf", [128, 128], "bfloat16"),
-    "hx": ("sbuf", [128, 128], "bfloat16"), "gx": ("sbuf", [8, 2048], "bfloat16"), "bc8": ("sbuf", [8, 128], "bfloat16"),
-    "pidx": ("sbuf", [128, 1], "int32"), "pxi": ("sbuf", [128, 1], "int32"), "xcol": ("sbuf", [128, 1], "float32"),
-    "negx": ("sbuf", [128, 1], "float32"), "ecol": ("sbuf", [128, 1], "float32"),
+    "ltl": ("sbuf", [128, N * NC], "bfloat16"), "y0l": ("sbuf", [128, NC], "bfloat16"),
+    "li": ("sbuf", [128, 5 * NC], "bfloat16"), "zi": ("sbuf", [128, 5 * NC], "bfloat16"), "z0": ("sbuf", [128, NC], "bfloat16"),
+    "sti": ("sbuf", [128, 192], "int32"), "sta": ("sbuf", [128, 192], "float32"), "stb": ("sbuf", [128, 192], "float32"),
+    "stx": ("sbuf", [128, 224], "float32"), "sty": ("sbuf", [128, 192], "float32"), "stz": ("sbuf", [128, 224], "float32"),
+    "smi": ("sbuf", [128, 192], "int32"), "smf": ("sbuf", [128, 192], "float32"), "stu": ("sbuf", [128, 192], "uint16"),
+    "eb": ("sbuf", [128, 2048], "bfloat16"), "ebx": ("sbuf", [128, 2048], "bfloat16"), "blk": ("sbuf", [128, 128], "bfloat16"),
+    "idf": ("sbuf", [128, 128], "float32"), "bc8": ("sbuf", [8, 128], "bfloat16"),
+    "pidx": ("sbuf", [128, 1], "int32"), "pxi": ("sbuf", [128, 1], "int32"),
     "jl0": ("sbuf", [128, NC], "float32"), "jl": ("sbuf", [128, NC], "float16"),
-    "dl": ("sbuf", [128, HALF], "float32"), "ha": ("sbuf", [128, HALF], "bfloat16"),
+    "pm0": ("sbuf", [128, NC], "float32"), "pm": ("sbuf", [128, NC], "uint16"),
+    "dl": ("sbuf", [128, PM], "float32"), "ha": ("sbuf", [128, PM], "bfloat16"),
     "lu": ("sbuf", [128, NC * NU], "uint16"), "lf": ("sbuf", [128, NC * NF], "float32"),
     "lb": ("sbuf", [128, NC * NB], "bfloat16"), "lh": ("sbuf", [128, NC * NH], "float16"),
-    "l0n": ("sbuf", [128, NC * N], "bfloat16"), "zn0": ("sbuf", [128, NC * N], "bfloat16"), "absn": ("sbuf", [128, NC * N], "float32"),
-    "mi": ("sbuf", [128, 32 * 4], "int32"),
-    "js1": ("sbuf", [128, K], "float32"), "js2": ("sbuf", [128, K], "float32"),
+    "ru": ("sbuf", [128, NC * NRU], "uint16"), "rf": ("sbuf", [128, NC * NRF], "float32"),
+    "rb": ("sbuf", [128, NC * NRB], "bfloat16"), "rh": ("sbuf", [128, NC * NRF], "float16"),
+    "mi": ("sbuf", [128, NC * 2], "int32"),
+    "ol": ("sbuf", [128, NC * 7], "bfloat16"), "lo": ("sbuf", [128, NC * 3], "bfloat16"),
+    "tmf": ("sbuf", [128, K], "bfloat16"), "vo": ("sbuf", [128, K], "bfloat16"),
 }
-BANKS = ("xa0", "xa1", "xc", "kt0", "kt1", "nt0", "nt1", "ms")
+for _i in ("xcol", "x16", "ecol", "mb1", "mb2"):
+    SCRATCH[_i] = ("sbuf", [128, 1], "float32")
+for _i in ("idb", "idn", "idm", "idh", "idg"):
+    SCRATCH[_i] = ("sbuf", [128, 128], "bfloat16")
+BANKS = ["xa0", "xa1", "xc0", "xc1", "kt0", "kt1", "ms0", "ms1"]
 for _i in BANKS:
     SCRATCH[_i] = ("psum", [128, 512], "float32")
 for _i in range(N):
+    if any((_t, _i) not in PRM["remc"] for _t in range(TW)):
+        SCRATCH["cw%d" % _i] = ("sbuf", [128, WIN], "bfloat16")
     SCRATCH["mk%d" % _i] = ("sbuf", [128, K], "bfloat16")
-for _i in range(3):
-    SCRATCH["mt%d" % _i] = ("sbuf", [128, HALF], "bfloat16")
-    SCRATCH["md%d" % _i] = ("sbuf", [128, K], "float16")
-    for _n in ("v", "tm", "sg"):
-        SCRATCH[_n + str(_i)] = ("sbuf", [128, K], "bfloat16")
-for _i in range(7):
-    SCRATCH["no%d" % _i] = ("sbuf", [8, K], "bfloat16")
-for _i in range(2):
+for _i in range(TW):
     SCRATCH["my%d" % _i] = ("sbuf", [128, K], "bfloat16")
-    SCRATCH["yn%d" % _i] = ("sbuf", [8, K], "bfloat16")
-    SCRATCH["gh%d" % _i] = ("sbuf", [128, HALF], "bfloat16")
-    SCRATCH["run%d" % _i] = ("sbuf", [128, HALF], "float32")
-    SCRATCH["bz%d" % _i] = ("sbuf", [128, HALF], "bfloat16")
-    SCRATCH["hs%d" % _i] = ("sbuf", [128, HALF], "bfloat16")
-SEMAPHORES = ["vq", "sq", "pq", "gq", "snt", "rcw"] + ["ld%d" % i for i in range(10)] + ["st%d" % i for i in range(8)]
-for _d in range(1, N):
-    SCRATCH["zi%d" % _d] = ("sbuf", [128, NC], "bfloat16")
-    SEMAPHORES.append("rzi%d" % _d)
-for _t in range(TW):
-    SCRATCH["bh%d" % _t] = ("sbuf", [128, NC], "float16")
-    SEMAPHORES.append("rh%d" % _t)
-    for _d in range(1, N):
-        _x = "%d%d" % (_t, _d)
-        SCRATCH["br" + _x] = ("sbuf", [128, NC], "uint16")
-        SCRATCH["fr" + _x] = ("sbuf", [128, NC], "bfloat16")
-        SEMAPHORES += ["rb" + _x, "rf" + _x]
-        if _d < N - 1:
-            SCRATCH["cg" + _x] = ("sbuf", [128, 2 * (SH + HALF)], "bfloat16")
-            SCRATCH["cs" + _x] = ("sbuf", [128, SH + K], "bfloat16")
-            SEMAPHORES += ["rc%s0" % _x, "rc%s1" % _x]
+for _i in range(3):
+    for _n in ("v", "mt"):
+        SCRATCH[_n + str(_i)] = ("sbuf", [128, K], "bfloat16")
+for _i in range(2):
+    SCRATCH["md%d" % _i] = ("sbuf", [128, K], "float16")
+    if PRM["start"] != "G":
+        SCRATCH["js%d" % (_i + 1)] = ("sbuf", [128, K], "float32")
+    for _n in ("tm", "sg", "gh"):
+        SCRATCH[_n + str(_i)] = ("sbuf", [128, K], "bfloat16")
+for _n, _d in (("run", "float32"), ("bz", "bfloat16"), ("hs", "bfloat16")):
+    SCRATCH[_n] = ("sbuf", [128, K], _d)
+for _t, _d in PRM["remc"]:
+    SCRATCH["cg%d%d" % (_t, _d)] = ("sbuf", [128, K + NP * SH], "bfloat16")
+    SCRATCH["cs%d%d" % (_t, _d)] = ("sbuf", [128, K], "bfloat16")
+SEMAPHORES = ["vq", "sq", "pq", "gq", "snt"] + ["ld%d" % i for i in range(20)] + ["st%d" % i for i in range(10)]
+SEMAPHORES += ["r%d" % i for i in range(90)]
 
 
 def add(pl, eng, cost, reads, writes, fn, sem=None, lat=0.0, inc=None, after=None, kind="c"):
@@ -83,9 +93,9 @@ def add(pl, eng, cost, reads, writes, fn, sem=None, lat=0.0, inc=None, after=Non
         last[k] = i
         rd[k] = []
     deps.discard(i)
-    tdeps = deps if after is None else deps | set([after])
+    tdeps = deps if after is None else deps | set(after)
     tasks.append({"eng": eng, "cost": cost, "deps": sorted(deps), "tdeps": sorted(tdeps), "fn": fn, "sem": sem, "lat": lat,
-                  "inc": inc, "kind": kind})
+                  "inc": inc, "kind": kind, "bias": pl["bias"], "name": str(list(writes) or list(reads))})
     return i
 
 
@@ -95,41 +105,78 @@ def order(tasks):
     for i in range(n):
         for j in tasks[i]["tdeps"]:
             succ[j].append(i)
+    edge = [[(j, tasks[i]["cost"] + (0.0 if i in tasks[j].get("soft", ()) else tasks[i]["lat"])
+              + (0.0 if tasks[j]["eng"] == "R" else 0.06 if tasks[j]["eng"] == tasks[i]["eng"] else PRM["sync"])) for j in succ[i]]
+            for i in range(n)]
     pri = [0.0] * n
-    own = [0.0] * n
-    for i in range(n - 1, -1, -1):
-        pri[i] = max([pri[j] for j in succ[i]] + [0.0]) + tasks[i]["cost"] + tasks[i]["lat"]
-        own[i] = 1e6 - i if "first" in tasks[i] else pri[i]
-    left = [len(tasks[i]["tdeps"]) for i in range(n)]
-    rt = [0.0] * n
-    todo = [i for i in range(n) if left[i] == 0]
-    busy = {}
-    start = [0.0] * n
-    while todo:
-        i = max(todo, key=lambda a: (own[a], -a))
-        todo.remove(i)
-        e, c = tasks[i]["eng"], tasks[i]["cost"]
-        s = rt[i]
-        if e != "R":
-            b = busy.setdefault(e, [])
-            k = 0
-            while k < len(b) and b[k][1] <= s:
-                k += 1
-            while k < len(b) and b[k][0] < s + c:
-                s = max(s, b[k][1])
-                k += 1
-            b.insert(k, (s, s + c))
-        start[i] = s
+    left = [len(t["tdeps"]) for t in tasks]
+    topo = [i for i in range(n) if left[i] == 0]
+    for i in topo:
         for j in succ[i]:
             left[j] -= 1
-            rt[j] = max(rt[j], s + c + tasks[i]["lat"] + (0.03 if tasks[j]["eng"] == e else 0.08))
             if left[j] == 0:
-                todo.append(j)
-    return sorted(range(n), key=lambda a: (start[a], a))
+                topo.append(j)
+    for i in reversed(topo):
+        pri[i] = max([pri[j] + c for j, c in edge[i]] + [tasks[i]["cost"] + tasks[i]["lat"]])
+    own = [1e6 - i if "first" in tasks[i] else pri[i] + tasks[i]["bias"] for i in range(n)]
+    for seed in PRM["nudge"]:
+        nudge(own, seed)
+    seq, start = run_list(tasks, edge, own, PRM["alpha"])
+    PRM["span"] = (max(start), max(pri))
+    PRM["dbg"] = (tasks, start, pri, succ, edge, own)
+    return seq
+
+
+def nudge(own, seed):
+    x = seed * 7919 + 13
+    for _ in range(12):
+        x = (x * 1103515245 + 12345) % 2147483648
+        a = (x >> 8) % len(own)
+        x = (x * 1103515245 + 12345) % 2147483648
+        own[a] += ((x >> 8) % 1001 - 500) / 200.0
+
+
+def run_list(tasks, edge, own, alpha):
+    n = len(tasks)
+    left = [len(tasks[i]["tdeps"]) for i in range(n)]
+    rt = [0.0] * n
+    start = [0.0] * n
+    todo = dict((e, []) for e in "RYGVSP")
+    free = dict((e, 0.0) for e in todo)
+    for i in range(n):
+        if left[i] == 0:
+            todo[tasks[i]["eng"]].append(i)
+    seq = []
+    while len(seq) < n:
+        best = None
+        for e in "RYGVSP":
+            if todo[e]:
+                s = max(free[e], min(rt[a] for a in todo[e]))
+                if best is None or s < best[0]:
+                    best = (s, e)
+        s, e = best
+        i = max(todo[e], key=lambda a: (own[a] - alpha * max(0.0, rt[a] - s), -a)) if e != "R" else min(todo[e], key=lambda a: rt[a])
+        todo[e].remove(i)
+        s = max(s, rt[i])
+        start[i] = s
+        if e != "R":
+            free[e] = s + tasks[i]["cost"]
+        seq.append(i)
+        for j, c in edge[i]:
+            left[j] -= 1
+            rt[j] = max(rt[j], s + c)
+            if left[j] == 0:
+                todo[tasks[j]["eng"]].append(j)
+    return seq, start
+
+
+SEQ = {}
 
 
 def emit(g, T, tasks):
-    seq = order(tasks)
+    if not SEQ:
+        SEQ[0] = order(tasks)
+    seq = SEQ[0]
     pos = dict((a, b) for b, a in enumerate(seq))
     q = {"V": g.vector, "S": g.scalar, "P": g.tensor, "G": g, "Y": g.sync}
     qsem = {"V": "vq", "S": "sq", "P": "pq", "G": "gq"}
@@ -177,35 +224,51 @@ def rank_program(g, core, T, topo):
     rank = T.rank_of(core)
     if rank is None:
         return
-    pl = {"tasks": [], "last": {}, "rd": {}}
+    pl = {"tasks": [], "last": {}, "rd": {}, "bias": 0.0}
     vec, sca, ten, syn = g.vector, g.scalar, g.tensor, g.sync
     cores = T.cores
     used = {}
+    FF, GG, HOP = PRM["f"] * 0.83e-3, PRM["g"], PRM["hop"]
+    C0 = [sum(PARTS[:h]) for h in range(NP)]
+    LC = [slice(C0[h], C0[h] + PARTS[h]) for h in range(NP)]
+    WC = [slice(16 * C0[h], 16 * (C0[h] + PARTS[h])) for h in range(NP)]
+
+    def el(n, c=1.0):
+        return max(64, n * c) * FF
+
+    def ga(n):
+        return 0.06 + n * GG * FF
+
+    def pe(n, c=64):
+        return n * c * PRM["pe"] * FF
 
     def take(kind):
         used[kind] = used.get(kind, -1) + 1
         return used[kind]
 
-    def new(buf):
-        n = take(buf)
-        t = T[buf]
-        return (t[:, NC * n:NC * n + NC], "%s.%d" % (buf, n), [t[:, NC * n + 32 * h:NC * n + 32 * h + 32] for h in range(2)])
+    def new(buf, h):
+        n = take((buf, h))
+        return (T[buf][:, NC * n + C0[h]:NC * n + C0[h] + PARTS[h]], "%s.%d.%d" % (buf, n, h))
 
-    def rot(kind, n=3):
-        return kind + str(take(kind) % n)
+    def rot(kind, h, n=2):
+        b = kind + str(take((kind, h)) % n)
+        return (T[b][:, WC[h]], "%s.%d" % (b, h), b)
 
-    def vts(out, ok, in0, ik, s1, s2, op0, op1, cost=0.08, more=()):
+    def part(buf, h, at=0):
+        return (T[buf][:, NC * at + C0[h]:NC * at + C0[h] + PARTS[h]], buf)
+
+    def vts(out, ok, in0, ik, s1, s2, op0, op1, cost=None, more=()):
         args = (out, in0, s1, s2, op0) if op1 is None else (out, in0, s1, s2, op0, op1)
-        return add(pl, "V", cost, [ik] + list(more), [ok], lambda: [vec.tensor_scalar(*args)])
+        return add(pl, "V", cost or el(0), [ik] + list(more), [ok], lambda: [vec.tensor_scalar(*args)])
 
-    def vtt(out, ok, a, ak, b, bk, op, cost=0.08):
-        return add(pl, "V", cost, [ak, bk], [ok], lambda: [vec.tensor_tensor(out, a, b, op)])
+    def vtt(out, ok, a, ak, b, bk, op, cost=None):
+        return add(pl, "V", cost or el(0), [ak, bk], [ok], lambda: [vec.tensor_tensor(out, a, b, op)])
 
-    def vcp(out, ok, a, ak, cost=0.08):
-        return add(pl, "V", cost, [ak], [ok], lambda: [vec.tensor_copy(out, a)])
+    def vcp(out, ok, a, ak, cost=None):
+        return add(pl, "V", cost or el(0), [ak], [ok], lambda: [vec.tensor_copy(out, a)])
 
-    def act(out, ok, in_, reads, func, cost, **kw):
-        return add(pl, "S", cost, reads, [ok], lambda: [sca.activation(out, in_, func, **kw)])
+    def act(out, ok, in_, reads, func, cost=None, **kw):
+        return add(pl, "S", cost or el(100), reads, [ok], lambda: [sca.activation(out, in_, func, **kw)])
 
     def scan(out, ok, d0, d0k, d1, d1k, op0, op1, cost):
         return add(pl, "V", cost, [d0k, d1k], [ok], lambda: [vec.tensor_tensor_scan(out, d0, d1, 0.0, op0, op1)])
@@ -213,344 +276,446 @@ def rank_program(g, core, T, topo):
     def mm(group, reads, writes, cost):
         return add(pl, "P", cost, reads, writes, lambda: [ten.matmul(*x) for x in group])
 
-    def memset(ap, key, c, cost=0.08):
-        return add(pl, "V", cost, [], [key], lambda: [vec.memset(ap, c)])
+    def lin(out, bank, terms):
+        grp = [(out, T[m][:], l[0], i == 0, i == len(terms) - 1) for i, (m, l) in enumerate(terms)]
+        cost = pe(sum(4 if m == "idf" else 1 for m, l in terms))
+        return mm(grp, [m for m, l in terms] + [l[1] for m, l in terms], [bank], cost)
 
-    def send(out, in_, sem, to, reads, key, lat, bulk=False):
-        dst = cores[to]
-        rid, pid, _ = topo.addr(dst)
+    def memset(ap, key, c, n=0):
+        return add(pl, "V", el(n), [], [key], lambda: [vec.memset(ap, c)])
+
+    def engines(dst, kind):
         en = topo.engines(core, dst)
-        en = en[1::2] if bulk else en[0::2]
-        n = len(en)
-        m = sum(1 << x for x in en)
-        i = add(pl, "G", 0.4, reads, [], lambda: [g.remote_dma(out, in_, T.sem[sem], T.sem.snt, pid, rid, m)], inc=n, kind="r")
-        return lambda: add(pl, "R", 0.0, [], key, None, sem=sem, inc=n, after=i, lat=lat)
+        return {"all": en, "even": en[0::2], "odd": en[1::2], "lo": en[:len(en) // 2], "hi": en[len(en) // 2:],
+                "q0": en[0::4], "q2": en[2::4]}[kind]
 
-    def load(eng, out, in_, key, lat):
+    def send(trs, lat, reads=(), after=None):
+        made, tot, arr = [], 0, []
+        for src, sk, kind, dsts in trs:
+            en = engines(cores[dsts[0][0] % N], kind)
+            sem = "r%d" % take("r")
+            ids = [topo.addr(cores[to % N]) for to, _, _ in dsts]
+            made.append((src, sem, ids, [o for _, o, _ in dsts], sum(1 << x for x in en)))
+            tot += len(en)
+            arr.append((sem, len(en) * len(dsts), [k for _, _, k in dsts]))
+
+        def call():
+            if len(made) == 1 and len(made[0][2]) == 1:
+                src, sem, ids, outs, m = made[0]
+                return [g.remote_dma(outs[0], src, T.sem[sem], T.sem.snt, ids[0][1], ids[0][0], m)]
+            return [g.remote_dma_fused([RemoteDMATransfer(dst_ids=[DstId(rid=a[0], pnc=a[1]) for a in ids], dma_engine_mask=m,
+                                                          remote_sem=T.sem[sem], srcs=[src], dsts=outs)
+                                        for src, sem, ids, outs, m in made], local_sem=T.sem.snt)]
+        keys = []
+        for x in trs:
+            keys += x[1] if isinstance(x[1], list) else [x[1]]
+        i = add(pl, "G", PRM["issue"], keys + list(reads), [], call, inc=tot, kind="r", after=after)
+        for sem, n, ks in arr:
+            add(pl, "R", 0.0, [], ks, None, sem=sem, inc=n, after=[i], lat=lat)
+        return i
+
+    def load(eng, out, in_, key, lat, reads=()):
         qq = syn if eng == "Y" else sca
-        i = add(pl, eng, 0.1, [], [key], lambda: [qq.dma_start(out, in_)], sem="ld%d" % take("ld"), lat=lat, kind="d")
+        i = add(pl, eng, 0.1, list(reads), [key], lambda: [qq.dma_start(out, in_)], sem="ld%d" % take("ld"), lat=lat, kind="d",
+                after=used.get(eng))
         pl["tasks"][i]["first"] = True
+        pl["tasks"][i]["soft"] = used.get(eng, [])
+        used[eng] = [i]
 
     def store(out, in_, reads):
         add(pl, "Y", 0.1, reads, [], lambda: [syn.dma_start(out, in_)], sem="st%d" % take("st"), lat=2.0, kind="d")
 
-    def halves(k):
-        return [k + ".0", k + ".1"]
+    def both(k):
+        return ["%s.%d" % (k, h) for h in range(NP)]
 
-    HS = [slice(0, HALF), slice(HALF, K)]
+    load("S", T.sti[:], T.st[:], "sti", 2.4)
+    load("S", T.y0n[:], T.y0[:], "y0n", 2.4)
+    def letters(eng, d, lat, reads=()):
+        s = (rank - d) % N
+        load(eng, T.ltl[:, NC * d:NC * d + NC], T.lt[:, K * s:K * s + K], "ltl%d" % d, lat, reads)
+    letters("S", 1, 2.8)
+    load("S", T.ltn[:], T.lt[:], "ltn", 3.2)
+    JP = PRM["jp"]
+    at, base, land = 3.2, 0.0, []
+    for p, (a, b) in enumerate(JP):
+        at += (b - a) * 512 / 2.0e5 * PRM["dma"]
+        land.append(at)
+        if p == PRM["jwait"]:
+            base = 2.5
+        load("Y", T.jint[:, a:b], T.jm[:, a:b], "jint%d" % p, at - base, ["sti"] if p == PRM["jwait"] else [])
+    cwait = ["jint%d" % PRM["cwait"]]
+    base = land[PRM["cwait"]]
+    for k, d in enumerate((0, 2, 3)):
+        letters("Y", d, at + 0.4 * (k + 2) - base, cwait)
+    load("Y", T.cst[:], T.cf[:, 4096:W], "cst", at + 2.5 - base)
+    load("Y", T.cw0[:, SH:SH + 4096], T.cf[:, 0:4096], "cwa", at + 2.0 + 5.3 * PRM["dma"] - base)
+    load("Y", T.y0l[:], T.y0[:], "y0l", 3.0, ["cwa"])
 
-    load("S", T.y0n[:], T.y0[:], "y0n", 3.0)
-    load("S", T.sti[:], T.st[:], "sti", 3.2)
-    load("S", T.ltn[:], T.lt[:], "ltn", 5.0)
-    at = 2.0
-    for p in range(5):
-        a, b = 1024 * p, min(W, 1024 * p + 1024)
-        at += (b - a) * 512 / 2.2e5
-        load("Y", T.jint[:, a:b], T.jm[:, a:b], "jint%d" % p, at)
-    load("Y", T.cst[:], T.cf[:, 4096:W], "cst", at + 0.9)
-    load("Y", T.cw[:, SH:SH + 4096], T.cf[:, 0:4096], "cwa", at + 5.4)
+    def lic(i, b="li"):
+        return T[b][:, NC * i:NC * i + NC]
+    send([(T.ltl[:, NC:2 * NC], "ltl1", "all", [(rank - 1, lic(0), "li0")])], at - 3.0)
+    send([(T.ltl[:, 2 * NC:3 * NC], "ltl2", "even", [(rank - 1, lic(3), "li3"), (rank - 2, lic(1), "li1")]),
+          (T.ltl[:, 3 * NC:4 * NC], "ltl3", "odd", [(rank - 1, lic(4), "li4"), (rank - 3, lic(2), "li2")])], 5.0)
+    vts(lic(0, "zi"), "zi0", lic(0), "li0", 15.5, -float(D), A.is_ge, A.mult)
+    add(pl, "V", el(128), ["li%d" % i for i in range(1, 5)], ["zi"],
+        lambda: [vec.tensor_scalar(T.zi[:, NC:5 * NC], T.li[:, NC:5 * NC], 15.5, -float(D), A.is_ge, A.mult)])
+    vts(T.z0[:], "z0", T.ltl[:, 0:NC], "ltl0", 15.5, -float(D), A.is_ge, A.mult)
 
-    def gsel(ap, key, pat, op, base, cm, cost=0.42, after=None):
-        return add(pl, "G", cost, [key], [key], lambda: [g.affine_select(ap, ap, pat, op, 0.0, base, cm)], after=after)
-    memset(T.idb[:], "idb", 1.0, 0.15)
-    memset(T.blk[:], "blk", 1.0, 0.15)
-    memset(T.bc8[:], "bc8", 1.0, 0.15)
-    memset(T.eb[:], "eb", 0.0, 0.9)
-    memset(T.gx[:], "gx", 1.0, 0.9)
-    memset(T.hx[:], "hx", -1.0 / 1024.0, 0.15)
-    add(pl, "G", 0.14, [], ["pidx"], lambda: [g.iota(T.pidx[:], [[1, 1]], 0, 1)])
-    gsel(T.blk[:], "blk", [[-16, 8], [0, 16]], A.is_ge, 0, 1)
-    i = gsel(T.blk[:], "blk", [[16, 8], [0, 16]], A.is_ge, 15, -1)
+    def gsel(ap, key, pat, op, base, cm):
+        return add(pl, "G", 0.42, [key], [key], lambda: [g.affine_select(ap, ap, pat, op, 0.0, base, cm)])
+
+    def giota(ap, key, pat, base, cm, n, fl=True):
+        kw = {"allow_small_or_imprecise_dtypes": True} if fl else {}
+        return add(pl, "G", 0.13 + 2 * n * FF, [], [key], lambda: [g.iota(ap, pat, base, cm, **kw)])
+    memset(T.blk[:], "blk", 1.0)
+    memset(T.bc8[:], "bc8", 1.0)
+    memset(T.idb[:], "idb", 1.0)
+    memset(T.eb[:], "eb", 0.0, 1024)
+    giota(T.pidx[:], "pidx", [[1, 1]], 0, 1, 1, False)
     gsel(T.bc8[:], "bc8", [[-1, 8], [0, 16]], A.is_equal, 0, 1)
-    i = gsel(T.idb[:], "idb", [[-1, 128]], A.is_equal, 0, 1, 0.42, i)
-    add(pl, "G", 0.25, [], ["jl0"], lambda: [g.iota(T.jl0[:], [[0, 2], [16, NC // 2]], -PH, 0, allow_small_or_imprecise_dtypes=True)])
-    gsel(T.hx[:], "hx", [[-1, 16], [-16, 8]], A.is_equal, 0, 1, 0.42, i)
-    gsel(T.gx[:], "gx", [[1, 16], [-16, 8], [-1, 16]], A.is_equal, 0, 16, 3.6, i)
+    gsel(T.blk[:], "blk", [[-16, 8], [0, 16]], A.is_ge, 0, 1)
+    gsel(T.blk[:], "blk", [[16, 8], [0, 16]], A.is_ge, 15, -1)
+    gsel(T.idb[:], "idb", [[-1, 128]], A.is_equal, 0, 1)
+    giota(T.smi[:], "smi", [[16, 12], [0, 16]], 0, 1, 192, False)
+    giota(T.jl0[:], "jl0", [[16, NC]], -PH, 0, NC)
+    giota(T.pm0[:], "pm0", [[1, 16], [256, 4]], 0, 0, NC)
+    JW = ["jwz", "jwu", "jwv"] + ["jw%d" % p for p in range(8)]
+    nio = PRM["iota"]
+    for a in range(0, nio, 1288):
+        b = min(nio, a + 1288)
+        giota(T.jw[:, D + a:D + b], "jwi%d" % a, [[1, b - a]], a - int(OFF), 0, b - a)
+        JW.append("jwi%d" % a)
+    for a in range(nio, D, 1288):
+        act(T.jw[:, D + a:D + a + 1288], "jwi%d" % a, T.jw[:, D:D + 1288], ["jwi0"], F.Identity, el(1288), bias=float(a))
+        JW.append("jwi%d" % a)
 
-    add(pl, "V", 0.06, ["pidx"], ["pxi"], lambda: [vec.tensor_scalar(T.pxi[:], T.pidx[:], 15, None, A.bitwise_and)])
+    add(pl, "V", el(0), ["pidx"], ["pxi"], lambda: [vec.tensor_scalar(T.pxi[:], T.pidx[:], 15, None, A.bitwise_and)])
     vcp(T.xcol[:], "xcol", T.pxi[:], "pxi")
-    vts(T.negx[:], "negx", T.xcol[:], "xcol", -1.0, None, A.mult, None)
+    vts(T.x16[:], "x16", T.xcol[:], "xcol", 16.0, None, A.mult, None)
     vts(T.ecol[:], "ecol", T.xcol[:], "xcol", -1.0 / 16.0, 15.0 / 16.0, A.mult, A.add)
-    vts(T.jl[:], "jl", T.jl0[:], "jl0", T.xcol[:, 0:1], None, A.add, None, more=["xcol"])
-    add(pl, "S", 1.3, ["blk"], ["eb"],
+    vts(T.mb2[:], "mb2", T.xcol[:], "xcol", 14.5, 0.5, A.is_ge, A.mult)
+    vtt(T.mb1[:], "mb1", T.xcol[:], "xcol", T.mb2[:], "mb2", A.add)
+    vts(T.mb1[:], "mb1", T.mb1[:], "mb1", -1.0, None, A.mult, None)
+    vts(T.mb2[:], "mb2", T.mb2[:], "mb2", 1.0, None, A.add, None)
+    for h in range(NP):
+        vts(T.jl[:, LC[h]], "jl", T.jl0[:, 0:PARTS[h]], "jl0", T.xcol[:, 0:1], None, A.add, None, more=["xcol"])
+    vts(T.pm[:], "pm", T.pm0[:], "pm0", T.x16[:, 0:1], None, A.add, None, more=["x16"])
+    add(pl, "S", 16 * el(80), ["blk"], ["eb"],
         lambda: [sca.activation(T.eb[:, 128 * x + x:128 * x + 128:16], T.blk[:, x:128:16], F.Copy) for x in range(16)])
-    vts(T.idn[:], "idn", T.idb[:], "idb", -1.0, None, A.mult, None, 0.12)
-    vts(T.idm[:], "idm", T.idb[:], "idb", -0.5, None, A.mult, None, 0.12)
-    memset(T.dl[:], "dl", 1.0 / 16.0, 0.45)
-    memset(T.dl[:, 0:HALF:16], "dl", -1000.0)
-    memset(T.ha[:], "ha", 1.0, 0.3)
-    memset(T.ha[:, 0:HALF:16], "ha", 0.0)
-    memset(T.bz0[:], "bz0", 0.0, 0.3)
-    memset(T.bz1[:], "bz1", 0.0, 0.3)
+    for a in range(0, 2048, 256):
+        act(T.ebx[:, a:a + 256], "ebx%d" % a, T.eb[:, a:a + 256], ["eb", "xcol"], F.Copy, el(256), scale=T.xcol[:, 0:1])
+    for m, c in (("idn", -1.0), ("idm", -0.5), ("idh", D / 2.0), ("idg", -D / 2.0), ("idf", 1.0)):
+        act(T[m][:], m, T.idb[:], ["idb"], F.Copy, el(128), scale=c)
+    memset(T.dl[:], "dl", 1.0 / 16.0, PM)
+    memset(T.dl[:, 0:PM:16], "dl", -1000.0)
+    memset(T.ha[:], "ha", 1.0, PM / 2)
+    memset(T.ha[:, 0:PM:16], "ha", 0.0)
+    add(pl, "V", el(512), [], both("bz"), lambda: [vec.memset(T.bz[:], 0.0)])
     memset(T.jw[:, 0:SH], "jwz", 0.0)
-    memset(T.jw[:, SH + 4096:WIN], "jwu", 0.0, 0.9)
-    memset(T.cw[:, 0:SH], "cwz", 0.0)
-    memset(T.cw[:, SH + 4096:WIN], "cwu", 0.0, 0.5)
-    for t in range(TW):
-        for d in range(1, N - 1):
-            x = "%d%d" % (t, d)
-            memset(T["cg" + x][:, 0:SH], "cgz" + x, 0.0)
-            memset(T["cs" + x][:, HALF:HALF + SH], "csz" + x, 0.0)
+    memset(T.jw[:, SH + 4096:D], "jwv", 0.0, 1040)
+    memset(T.cw0[:, 0:SH], "cwz", 0.0)
+    memset(T.cw0[:, SH + 4096:WIN], "cwu", 0.0, 512)
+    memset(T.stx[:, 0:16], "stx0", 0.0)
+    memset(T.stx[:, 208:224], "stx1", 0.0)
+    for t, d in PRM["remc"]:
+        for h in range(NP):
+            a = 16 * C0[h] + SH * h
+            memset(T["cg%d%d" % (t, d)][:, a:a + SH], "cgz%d%d.%d" % (t, d, h), 0.0)
 
-    for h in range(2):
-        nt = "nt%d" % h
-        mm([(T[nt][:, 0:HALF], T.bc8[:], T.y0n[:, HS[h]], True, True)], ["bc8", "y0n"], [nt], 0.35)
-        vts(T.my0[:, HS[h]], "my0.%d" % h, T[nt][:, 0:HALF], nt, T.xcol[:, 0:1], None, A.is_equal, None, 0.5, ["xcol"])
-    mm([(T.ms[:, 0:256], T.gx[:, 128 * r:128 * r + 128], T.ltn[:, r:N * K:16], r == 0, r == 15) for r in range(16)],
-       ["gx", "ltn"], ["ms"], 2.5)
-    vts(T.zn0[:], "zn0", T.ms[:, 0:256], "ms", 15.5, FLAG, A.is_ge, A.mult, 0.25)
-    vts(T.absn[:], "absn", T.ms[:, 0:256], "ms", 15.5, None, A.is_ge, None, 0.25)
-    vts(T.l0n[:], "l0n", T.ms[:, 0:256], "ms", -1024.0, None, A.mult, None, 0.25)
+    def onehot(rows, rk, c0, out, eng):
+        for h in range(NP):
+            bk = ("kt0", "kt1", "ms0", "ms1")[take("mb") % 4]
+            n = PARTS[h]
+            mm([(T[bk][:, r:16 * n:16], T.bc8[:], rows[:, c0 + NC * r + C0[h]:c0 + NC * r + C0[h] + n], True, True) for r in range(16)],
+               ["bc8", rk], [bk], pe(16))
+            o, ok = T[out][:, WC[h]], "%s.%d" % (out, h)
+            if eng == "V":
+                vts(o, ok, T[bk][:, 0:16 * n], bk, 15.0, T.xcol[:, 0:1], A.min, A.is_equal, el(16 * n), ["xcol"])
+            else:
+                mt = rot("mt", h, 3)
+                act(mt[0], mt[1], T[bk][:, 0:16 * n], [bk, "mb1"], F.Abs, el(16 * n), bias=T.mb1[:, 0:1])
+                act(o, ok, mt[0], [mt[1], "mb2"], F.Relu, el(16 * n), bias=T.mb2[:, 0:1], scale=-1.0)
+    onehot(T.y0n, "y0n", 0, "my0", PRM["my0"])
     for d in range(N):
-        for h in range(2):
-            bk = ("xa0", "xa1", "xc")[take("mb") % 3]
-            mt = rot("mt")
-            c = ((rank - d) % N) * K + HALF * h
-            mm([(T[bk][:, 0:HALF], T.bc8[:], T.ltn[:, c:c + HALF], True, True)], ["bc8", "ltn"], [bk], 0.35)
-            act(T[mt][:], mt, T[bk][:, 0:HALF], [bk, "negx"], F.Abs, 0.5, bias=T.negx[:, 0:1])
-            act(T["mk%d" % d][:, HS[h]], "mk%d.%d" % (d, h), T[mt][:], [mt], F.Relu, 0.5, bias=1.0, scale=-1.0)
+        onehot(T.ltn, "ltn", K * ((rank - d) % N), "mk%d" % d, PRM["mk"][d])
+
+    vts(T.sta[:], "sta", T.sti[:], "sti", 2.0, -4096.0, A.mult, A.add, el(192))
+    vtt(T.stb[:], "stb", T.sti[:], "sti", T.sta[:], "sta", A.max, el(384))
+    add(pl, "S", 12 * el(80), ["stb"], ["stx"],
+        lambda: [sca.activation(T.stx[:, 16 + 16 * b:32 + 16 * b], T.stb[:, NC * (b // 4) + b % 4:NC * (b // 4) + NC:4], F.Copy) for b in range(12)])
+    add(pl, "V", el(192), ["stx"], ["sty"], lambda: [vec.transpose(T.sty[:], T.stx[:, 16:208])])
+    add(pl, "V", el(224), ["stx", "stx0", "stx1"], ["stz"], lambda: [vec.transpose(T.stz[:], T.stx[:])])
+    add(pl, "V", el(192), ["smi"], ["smi"], lambda: [vec.tensor_scalar(T.smi[:], T.smi[:], 16, None, A.bitwise_and)])
+    vts(T.smf[:], "smf", T.smi[:], "smi", 0.0, None, A.is_equal, None, el(192))
+    vtt(T.sta[:], "sta", T.sty[:], "sty", T.stz[:, 16:208], "stz", A.subtract, el(384))
+    vtt(T.sty[:], "sty", T.sta[:], "sta", T.smf[:], "smf", A.mult, el(384))
+    vtt(T.sta[:], "sta", T.sty[:], "sty", T.stz[:, 16:208], "stz", A.add, el(384))
+    vts(T.stu[:], "stu", T.sta[:], "sta", float(SH), None, A.add, None, el(192))
+
+    for p, (a0, b0) in enumerate(JP):
+        for a in range(a0, b0, 512):
+            bk = ("xa0", "xa1", "xc0", "xc1")[take("jb") % 4]
+            src, ik = T.jint[:, a:a + 512], "jint%d" % p
+            vts(T[bk][:], bk, src, ik, 4096.0, -6144.0, A.max, A.add, el(512))
+            if a < 4096:
+                vtt(T.jw[:, SH + a:SH + a + 512], "jw%d" % (a // 512), src, ik, T[bk][:], bk, A.add, el(512))
+            else:
+                add(pl, "V", el(512), [ik, bk], ["jwu", "jwv"],
+                    lambda src=src, bk=bk: [vec.tensor_tensor(T.jw[:, SH + 4096:WIN:2], src, T[bk][:], A.add)])
+    act(T.cw0[:, SH + 4096:WIN:2], "cwu", T.cst[:], ["cst"], F.Copy, el(512))
+    CW = ["cwz", "cwu", "cwa"]
+    need = [d for d in PRM["copies"] if any((t, d) not in PRM["remc"] for t in range(TW))]
+    bulk = []
+
+    def copies(after):
+        for k, d in enumerate(need):
+            after = [send([(T.cw0[:], CW, "odd", [(rank - d, T["cw%d" % d][:], "cw%d" % d)])], 2.0 + 12.0 * PRM["dma"] * (k + 1), after=after)]
+    copies([])
+    copytasks = [i for i, x in enumerate(pl["tasks"]) if x["kind"] == "r"][-len(need)]
+
+    ND = PRM["nd"]
+    DP, DN, DC = ("idh", "idg", -D / 2.0) if ND == "S" else ("idb", "idn", 0.0)
+    finals = {}
+
+    def words(h):
+        n, nw = PARTS[h], 16 * PARTS[h]
+        xa, xc, kt, ms = ["%s%d" % (b, h % 2) for b in ("xa", "xc", "kt", "ms")]
+
+        def tolist(x, xk, c=0.0):
+            l = new("lu", h)
+            vts(l[0], l[1], x, xk, OFF + c, 0.0, A.add, A.max)
+            return l
+
+        def summed(md, nxt):
+            x = T[xa][:, 0:n]
+            b, w0 = T[md[2]], 16 * C0[h]
+            grp = [(x, T.idn[:], nxt[0], True, False)] if nxt else []
+            grp += [(x, T.eb[:, 128 * r:128 * r + 128], b[:, w0 + r:w0 + nw:16], r == 0 and not nxt, r == 15) for r in range(16)]
+            mm(grp, ["eb", md[1]] + (["idn", nxt[1]] if nxt else []), [xa], pe(17))
+            return x
+
+        def image(l, mask, nxt):
+            md = rot("md", h)
+            add(pl, "V", ga(nw), JW + [l[1], "%s.%d" % (mask, h)], [md[1]],
+                lambda: [vec.tensor_tensor(md[0], T.jw[:].indirect(l[0]), T[mask][:, WC[h]], A.mult)])
+            return summed(md, nxt)
+
+        def keep(x, nxt, eng):
+            if eng == "S":
+                b = new("lf", h)
+                act(b[0], b[1], x, [xa], F.Copy)
+                return b, [("idf", b)] + ([("idb", nxt)] if nxt else [])
+            b = new("lh", h)
+            if nxt:
+                vtt(b[0], b[1], x, xa, nxt[0], nxt[1], A.add)
+            else:
+                vcp(b[0], b[1], x, xa)
+            return b, [("idb", b)]
+
+        def gather_c(out, l):
+            act(out[0], out[1], T.cw0[:].indirect(l[0]), CW + [l[1]], F.Identity, ga(nw))
+
+        def letter(y, terms, c, at):
+            q = T[ms][:, 0:n]
+            lin(q, ms, [("idb", y)] + terms)
+            o = (T.ol[:, NC * at + C0[h]:NC * at + C0[h] + n], "ol%d.%d" % (at, h)) if at is not None else new("lb", h)
+            vts(o[0], o[1], q, ms, c, 16.0, A.add, A.min)
+            return o
+
+        def vslot(v, base, zn, dead, win, wkeys, at, out):
+            last = at == (TW - 1, N - 1)
+            u = T[xc][:, 0:n]
+            dt, dc = ([(DP, dead)], DC) if dead else ([], 0.0)
+            if last:
+                lc = letter(out[0], [("idn", zn)], 0.0, None)
+                yc = letter(out[2], [(DN, dead)], -DC, None)
+            lin(u, xc, base + [("idb", zn)] + dt)
+            l = tolist(u, xc, dc)
+            how = "A" if last else PRM["sums"].get(at, PRM["sum0"])
+            sg, nv = rot("sg", h), None if last else rot("v", h, 3)
+            if how in "BC":
+                gh = rot("gh", h)
+                act(gh[0], gh[1], win.indirect(l[0]), wkeys + [l[1]], F.Identity, ga(nw))
+                src = (T[kt][:, 0:nw], kt)
+                mm([(src[0], T.idb[:], v[0], True, False), (src[0], T.idb[:], gh[0], False, True)], ["idb", v[1], gh[1]], [kt], pe(2, nw))
+                cl = el(nw)
+            else:
+                src = (T.tmf[:, WC[h]], "tmf.%d" % h) if last else rot("tm", h)
+                add(pl, "V", ga(nw), wkeys + [l[1], v[1]], [src[1]], lambda: [vec.tensor_tensor(src[0], win.indirect(l[0]), v[0], A.add)])
+                cl = el(nw, 0.5)
+            if how in "AB" and not (last and h == NP - 1):
+                act(sg[0], sg[1], src[0], [src[1]], F.Sign, el(nw), bias=0.5)
+            elif how != "C":
+                vts(sg[0], sg[1], src[0], src[1], 0.0, 0.5, A.is_ge, A.subtract, el(nw, 0.5))
+            if nv:
+                vts(nv[0], nv[1], src[0], src[1], 255.0, -255.0, A.min, A.max, cl)
+            if how == "C":
+                vts(sg[0], sg[1], nv[0], nv[1], 0.0, 0.5, A.is_ge, A.subtract, el(nw, 0.5))
+            o = T[xc][:, n:2 * n]
+            b, w0 = T[sg[2]], 16 * C0[h]
+            grp = [(o, T.idm[:], zn[0], True, False)]
+            if dead:
+                grp.append((o, T[DN if last else DP][:], dead[0], False, False))
+            grp += [(o, T.eb[:, 128 * r:128 * r + 128], b[:, w0 + r:w0 + nw:16], False, r == 15) for r in range(16)]
+            mm(grp, ["idm", DP, DN, zn[1], "eb", sg[1]] + ([dead[1]] if dead else []), [xc], pe(18))
+            if last:
+                x = new("lb", h)
+                vts(x[0], x[1], o, xc, -0.25 + dc, 16.0, A.is_le, A.mult)
+                for a, i in ((lc, out[1]), (yc, out[3])):
+                    vtt(T.ol[:, NC * i + C0[h]:NC * i + C0[h] + n], "ol%d.%d" % (i, h), x[0], x[1], a[0], a[1], A.max)
+                return None, None, None
+            nd = new("lb", h)
+            if ND == "S":
+                act(nd[0], nd[1], o, [xc], F.Sign, bias=0.25 + dc)
+            else:
+                vts(nd[0], nd[1], o, xc, -0.25, -float(D), A.is_le, A.mult)
+            if out:
+                letter(out[0], [("idn", zn), (DN, nd)] + dt, dc - DC, out[1])
+                return nv, nd, None
+            nz = new("lb", h)
+            q = T[ms][:, 0:n]
+            lin(q, ms, [("idb", zn), (DP, nd)] + ([(DN, dead)] if dead else []))
+            act(nz[0], nz[1], q, [ms], F.Identity, bias=DC - dc)
+            return nv, nd, nz
+
+        zn = [part("z0", h), (part("zi", h)[0], "zi0")] + [part("zi", h, d - 1) for d in range(2, N)]
+        nf = [None, part("zi", h, 3), part("zi", h, 4), None]
+        lts = [(T.ltl[:, LC[h]], "ltl0")] + [(T.li[:, NC * i + C0[h]:NC * i + C0[h] + n], "li%d" % i) for i in range(3)]
+        res = []
+        ys = [part("y0l", h)]
+        for t in range(TW):
+            le = "all" if t in PRM["lists16"] else "even"
+            todo = [("my%d" % i, res[i], (ys[i], 4 + i)) for i in range(t - 1, -1, -1)] + [("mk0", zn[0], (lts[0], 0))]
+            stl = (T.stu[:, NC * t + C0[h]:NC * t + C0[h] + n], "stu")
+            if t == 0 or PRM["start"] == "G":
+                x = image(stl, "my%d" % t, todo[0][1])
+            else:
+                md = rot("md", h)
+                vtt(md[0], md[1], T["js%d" % t][:, WC[h]], "js%d.%d" % (t, h), T[kt][:, 0:nw], kt, A.mult, el(nw))
+                x = summed(md, todo[0][1])
+                act(T["my%d" % t][:, WC[h]], "my%d.%d" % (t, h), T[kt][:, 0:nw], [kt], F.Copy, el(nw))
+            l = tolist(x, xa)
+            chain = [keep(x, todo[0][1], PRM["xs"])[1]]
+            for j in range(len(todo)):
+                nxt = todo[j + 1][1] if j < t else zn[1]
+                x = image(l, todo[j][0], nxt)
+                l = tolist(x, xa)
+                chain.append(keep(x, nxt, PRM["xs"])[1])
+            br = new("ru", h)
+            send([(l[0], l[1], le, [(rank + 1, br[0], br[1])])], HOP)
+            if t:
+                q, my, w0 = T[ms][:, 0:n], T["my%d" % t], 16 * C0[h]
+                mm([(q, T.ebx[:, 128 * r:128 * r + 128], my[:, w0 + r:w0 + nw:16], r == 0, r == 15) for r in range(16)],
+                   ["ebx%d" % a for a in range(0, 2048, 256)] + ["my%d.%d" % (t, h)], [ms], pe(16))
+                y = new("lb", h)
+                act(y[0], y[1], q, [ms], F.Copy)
+                ys.append(y)
+            if t + 1 < TW and PRM["start"] != "G":
+                c = NC * (t + 1) + C0[h]
+                act(T["js%d" % (t + 1)][:, WC[h]], "js%d.%d" % (t + 1, h), T.jw[:].indirect(T.stu[:, c:c + n]), JW + ["stu"], F.Identity, ga(nw))
+            home = {}
+            for d in range(1, N):
+                x = image(br, "mk%d" % d, nf[d])
+                rem = (t, d) in PRM["remc"]
+                if d < N - 1:
+                    l = tolist(x, xa)
+                    br = new("ru", h)
+                    to = [(rank + 1, br[0], br[1])]
+                    if PRM["dual"] and not rem:
+                        a, b = new("ru", h), new("lf", h)
+                        to.append((rank - d, a[0], a[1]))
+                    send([(l[0], l[1], le, to)], HOP)
+                    if PRM["dual"] and not rem:
+                        vts(b[0], b[1], a[0], a[1], -OFF, None, A.add, None)
+                        home[d] = [("idf", b), ("idb", zn[d + 1])]
+                        continue
+                b, terms = keep(x, nf[d], PRM["xs"] if d < N - 1 else PRM.get("xs3", PRM["xs"]))
+                if rem:
+                    u = T[xa][:, n:2 * n]
+                    lin(u, xa, terms)
+                    l = tolist(u, xa)
+                    nm = "%d%d" % (t, d)
+                    cs = (T["cs" + nm][:, WC[h]], "cs%s.%d" % (nm, h))
+                    gather_c(cs, l)
+                    a = 16 * C0[h] + SH * (h + 1)
+                    bulk.append((t, d, send([(cs[0], cs[1], PRM["cge"][t], [(rank - d, T["cg" + nm][:, a:a + nw], "cg%s.%d" % (nm, h))])],
+                                            HOP + (0.6 if PRM["cge"][t] == "all" else 1.2))))
+                else:
+                    a = new("rf" if terms[0][0] == "idf" else "rh", h)
+                    send([(b[0], b[1], le, [(rank - d, a[0], a[1])])], HOP)
+                    home[d] = [(terms[0][0], a)] + ([("idb", zn[d + 1])] if len(terms) > 1 else [])
+            u = T[xc][:, 0:n]
+            lin(u, xc, chain[0])
+            l = tolist(u, xc)
+            v = rot("v", h, 3)
+            gather_c(v, l)
+            dead = None
+            fin = t == TW - 1
+            for j in range(len(todo)):
+                v, dead, nz = vslot(v, chain[j + 1], todo[j][1], dead, T.cw0[:], CW, (t, j - t), todo[j][2] if fin else None)
+                if j < t:
+                    res[t - 1 - j] = nz
+                else:
+                    zn[0] = nz
+            for d in range(1, N):
+                out = ((lts[d], d) + ((ys[t], 4 + t) if d == N - 1 else ())) if fin else None
+                if d in home:
+                    v, dead, nz = vslot(v, home[d], zn[d], dead, T["cw%d" % d][:], ["cw%d" % d], (t, d), out)
+                else:
+                    nm = "%d%d" % (t, d)
+                    a = 16 * C0[h] + SH * h
+                    v, dead, nz = vslot(v, [("idb", part("jl", h))], zn[d], dead, T["cg" + nm][:, a:a + SH + nw],
+                                        ["cgz%s.%d" % (nm, h), "cg%s.%d" % (nm, h)], (t, d), out)
+                zn[d] = nz
+            if fin:
+                break
+            nf = [None, new("rb", h), new("rb", h), None]
+            send([(zn[2][0], zn[2][1], "even", [(rank + 1, nf[1][0], nf[1][1])]),
+                  (zn[3][0], zn[3][1], "odd" if t in PRM["lists16"] else "even", [(rank + 2, nf[2][0], nf[2][1])])][0:2]
+                 if t in PRM["lists16"] else
+                 [(zn[2][0], zn[2][1], "q0", [(rank + 1, nf[1][0], nf[1][1])]), (zn[3][0], zn[3][1], "q2", [(rank + 2, nf[2][0], nf[2][1])])],
+                 HOP + 0.5)
+            if ND == "S":
+                r = new("lb", h)
+                act(r[0], r[1], dead[0], [dead[1]], F.Identity, scale=D / 2.0, bias=DC)
+                res.append(r)
+            else:
+                res.append(dead)
+            w0, nb = 16 * C0[h], nw // 128
+            vb = T[v[2]]
+            ru, rk, bzk, hsk = T.run[:, WC[h]], "run.%d" % h, "bz.%d" % h, "hs.%d" % h
+            mm([(T[kt][:, 128 * k:128 * k + 128], vb[:, w0 + 128 * k:w0 + 128 * k + 128], T.idb[:], True, True) for k in range(nb)],
+               [v[1], "idb"], [kt], pe(nb, 128))
+            scan(ru, rk, T.dl[:, 0:nw], "dl", T[kt][:, 0:nw], kt, A.add, A.max, el(nw))
+            mi, mk_ = T.mi[:, NC * t + C0[h]:NC * t + C0[h] + n], "mi%d.%d" % (t, h)
+            top = T.run[:, w0 + 15:w0 + nw:16]
+            vts(mi, mk_, top, rk, -15.0 / 32.0, None, A.add, None)
+            vtt(T.bz[:, w0:w0 + nw:16], bzk, top, rk, mi, mk_, A.subtract)
+            scan(T.hs[:, WC[h]], hsk, T.ha[:, 0:nw], "ha", T.bz[:, WC[h]], bzk, A.mult, A.add, el(nw, 0.5))
+            mm([(T[kt][:, 128 * k:128 * k + 128], T.hs[:, w0 + 128 * k:w0 + 128 * k + 128], T.idb[:], True, True) for k in range(nb)],
+               [hsk, "idb"], [kt], pe(nb, 128))
+            if PRM["start"] == "G":
+                vts(T["my%d" % (t + 1)][:, WC[h]], "my%d.%d" % (t + 1, h), T[kt][:, 0:nw], kt, T.ecol[:, 0:1], None, A.is_equal, None, el(nw), ["ecol"])
+            else:
+                vts(T[kt][:, 0:nw], kt, T[kt][:, 0:nw], kt, T.ecol[:, 0:1], None, A.is_equal, None, el(nw), ["ecol"])
+
+    for h in range(NP):
+        pl["bias"] = PRM["lag"] * (NP - 1 - h)
+        words(h)
+    pl["bias"] = 0.0
+    if PRM["copyat"]:
+        pl["tasks"][copytasks]["tdeps"] += [b for t, d, b in bulk if (t, d) == PRM["copyat"]]
+
+    def olc(b, i):
+        return T[b][:, NC * i:NC * i + NC]
+    add(pl, "V", ga(K), both("tmf") + both("ol3") + ["pm"], ["vo"], lambda: [vec.tensor_scalar(T.vo[:], T.tmf[:].indirect(T.pm[:]), 255.0, -255.0, A.min, A.max)])
+    send([(olc("ol", d), both("ol%d" % d), ("even", "odd")[d - 1], [(rank + d, olc("lo", d - 1), "lo%d" % d)]) for d in (1, 2)], HOP)
+    send([(olc("ol", 3), both("ol3"), "all", [(rank + 3, olc("lo", 2), "lo3")])], HOP)
+    for t in range(TW):
+        store(T.yi[:, K * t:K * t + K], olc("ol", 4 + t), both("ol%d" % (4 + t)))
+    store(T.yl[:, K * rank:K * rank + K], olc("ol", 0), both("ol0"))
+    store(T.yv[:], T.vo[:], ["vo"])
     for d in range(1, N):
         s = (rank - d) % N
-        send(T["zi%d" % d][:], T.zn0[:, NC * s:NC * s + NC], "rzi%d" % d, s, ["zn0"], ["zi%d" % d], 2.0)()
-
-    vts(T.sta[:], "sta", T.sti[:], "sti", 2.0, -4096.0, A.mult, A.add, 0.2)
-    vtt(T.stb[:], "stb", T.sti[:], "sti", T.sta[:], "sta", A.max, 0.35)
-    vts(T.stu[:], "stu", T.stb[:], "stb", float(SH), None, A.add, None, 0.2)
-    for p in range(9):
-        bk = "kt%d" % (p % 2)
-        a = 512 * p
-        src, ik = T.jint[:, a:a + 512], "jint%d" % (p // 2)
-        vts(T[bk][:], bk, src, ik, 4096.0, -6144.0, A.max, A.add, 0.48)
-        out, ok = (T.jw[:, SH + a:SH + a + 512], "jw%d" % p) if p < 8 else (T.jw[:, SH + 4096:WIN:2], "jwu")
-        vtt(out, ok, src, ik, T[bk][:], bk, A.add, 0.48)
-    JW = ["jwz", "jwu"] + ["jw%d" % p for p in range(8)]
-    act(T.cw[:, SH + 4096:WIN:2], "cwu", T.cst[:], ["cst"], F.Copy, 0.48)
-    CW = ["cwz", "cwu", "cwa"]
-    send(T.cw3[:], T.cw[:], "rcw", (rank + 1) % N, CW, ["cw3"], 9.0, True)()
-
-    def summed(md, keep=None):
-        bk = rot("xa", 2)
-        x = T[bk][:, 0:NC]
-        grp = [(x, T.eb[:, 128 * r:128 * r + 128], T[md][:, r:K:16], r == 0, r == 15 and keep is None) for r in range(16)]
-        if keep is not None:
-            grp.append((x, T.idb[:], keep[0], False, True))
-        mm(grp, ["eb", "idb"] + halves(md) + ([keep[1]] if keep is not None else []), [bk], 0.65)
-        return x, bk
-
-    def image(lst, lk, mask, mkeys, keep=None):
-        md = rot("md")
-        add(pl, "V", 1.65, JW + [lk] + mkeys, halves(md), lambda: [vec.tensor_tensor(T[md][:], T.jw[:].indirect(lst), mask[:], A.mult)])
-        return summed(md, keep)
-
-    for t in range(1, TW):
-        for h in range(2):
-            c = NC * t + 32 * h
-            act(T["js%d" % t][:, HS[h]], "js%d.%d" % (t, h), T.jw[:].indirect(T.stu[:, c:c + 32]), JW + ["stu"], F.Identity, 0.86)
-
-    def start(t):
-        if t == 0:
-            return image(T.stu[:, 0:NC], "stu", T.my0, halves("my0"))
-        md = rot("md")
-        for h in range(2):
-            kt = "kt%d" % h
-            vtt(T[md][:, HS[h]], "%s.%d" % (md, h), T["js%d" % t][:, HS[h]], "js%d.%d" % (t, h), T[kt][:], kt, A.mult, 0.53)
-        x = summed(md)
-        if t < TW - 1:
-            for h in range(2):
-                act(T["my%d" % t][:, HS[h]], "my%d.%d" % (t, h), T["kt%d" % h][:], ["kt%d" % h], F.Copy, 0.57)
-        return x
-
-    def tolist(x, xk):
-        l = new("lu")
-        vts(l[0], l[1], x, xk, OFF, 0.0, A.add, A.max)
-        return l
-
-    def bslot(lst, lk, mask, mkeys, absent, present, prev, want, wantl):
-        if prev is None:
-            prev = new("lf")
-            vts(prev[0], prev[1], lst, lk, -OFF, None, A.add, None)
-        if present is None:
-            k = new("lh")
-            vtt(k[0], k[1], prev[0], prev[1], absent[0], absent[1], A.mult)
-            x = image(lst, lk, mask, mkeys, k)
-            l = tolist(x[0], x[1]) if wantl else None
-            b = None
-            if want:
-                b = new("lh")
-                vcp(b[0], b[1], x[0], x[1])
-            return b, l
-        k, a, b = new("lf"), new("lf"), new("lh")
-        vtt(k[0], k[1], prev[0], prev[1], absent[0], absent[1], A.mult)
-        x = image(lst, lk, mask, mkeys)
-        vtt(a[0], a[1], x[0], x[1], present[0], present[1], A.mult)
-        vtt(b[0], b[1], a[0], a[1], k[0], k[1], A.add)
-        return b, tolist(b[0], b[1]) if wantl else None
-
-    def flags(z, zk):
-        n, p = new("lf"), new("lf")
-        act(n[0], n[1], z, [zk], F.Copy, 0.15, scale=1.0 / FLAG)
-        act(p[0], p[1], z, [zk], F.Identity, 0.15, bias=1.0, scale=-1.0 / FLAG)
-        return n, p
-
-    def gather_c(out, okeys, l):
-        for h in range(2):
-            act(out[h], okeys[h], T.cw[:].indirect(l[2][h]), CW + [l[1]], F.Identity, 0.86)
-
-    def vslot(v, base, zn, dead, wins, wkeys, at):
-        u = T.xc[:, NC:2 * NC]
-        grp = [(u, T.idb[:], base[0], True, False), (u, T.idb[:], zn[0], False, dead is None)]
-        dk = [] if dead is None else [dead[1]]
-        if dead is not None:
-            grp.append((u, T.idb[:], dead[0], False, True))
-        mm(grp, ["idb", base[1], zn[1]] + dk, ["xc"], 0.1)
-        l = tolist(u, "xc")
-        tm, nv = rot("tm"), rot("v")
-        sg = "sg" + tm[2:]
-        for h in range(2):
-            c = HS[h]
-            vk, tk, sk, nk = ["%s.%d" % (x, h) for x in (v, tm, sg, nv)]
-            vi, src, srk, cl = T[v][:, c], T[tm][:, c], tk, 0.28
-            if h in BYSCALAR.get(at, ()):
-                gh = rot("gh", 2)
-                act(T[gh][:], gh, wins[h].indirect(l[2][h]), wkeys(h) + [l[1]], F.Identity, 0.85)
-                src, srk, cl = T["kt%d" % h][:], "kt%d" % h, 0.55
-                mm([(src, T.idb[:], vi, True, False), (src, T.idb[:], T[gh][:], False, True)], ["idb", vk, gh], [srk], 0.5)
-            else:
-                add(pl, "V", 0.83, wkeys(h) + [l[1], vk], [tk],
-                    lambda src=src, h=h, vi=vi: [vec.tensor_tensor(src, wins[h].indirect(l[2][h]), vi, A.add)])
-            if h and at in SIGNV:
-                vts(T[sg][:, c], sk, src, srk, 0.0, 0.5, A.is_ge, A.subtract, 0.28)
-            else:
-                act(T[sg][:, c], sk, src, [srk], F.Sign, 0.57, bias=0.5)
-            vts(T[nv][:, c], nk, src, srk, 255.0, -255.0, A.min, A.max, cl)
-        o = T.xc[:, 0:NC]
-        grp = [(o, T.idm[:], zn[0], True, False)]
-        if dead is not None:
-            grp.append((o, T.idb[:], dead[0], False, False))
-        grp += [(o, T.eb[:, 128 * r:128 * r + 128], T[sg][:, r:K:16], False, r == 15) for r in range(16)]
-        mm(grp, ["idm", "idb", zn[1], "eb"] + halves(sg) + dk, ["xc"], 0.7)
-        nd, nz = new("lb"), new("lb")
-        vts(nd[0], nd[1], o, "xc", -0.25, FLAG, A.is_le, A.mult)
-        if dead is None:
-            vtt(nz[0], nz[1], zn[0], zn[1], nd[0], nd[1], A.add)
-        elif at == (TW - 1, N - 1):
-            zd = new("lb")
-            vtt(zd[0], zd[1], zn[0], zn[1], dead[0], dead[1], A.subtract)
-            vtt(nz[0], nz[1], zd[0], zd[1], nd[0], nd[1], A.add)
-        else:
-            q = T.ms[:, 0:NC]
-            mm([(q, T.idb[:], zn[0], True, False), (q, T.idn[:], dead[0], False, False), (q, T.idb[:], nd[0], False, True)],
-               ["idb", "idn", zn[1], dead[1], nd[1]], ["ms"], 0.1)
-            act(nz[0], nz[1], q, ["ms"], F.Copy, 0.15)
-        return nv, nd, nz
-
-    def ylist(rows, keys, a, b):
-        l = new("lb")
-        mm([(T.ms[:, 0:NC], T.gx[:, 128 * r:128 * r + 128], rows[:, r:K:16], r == 0, r == 15) for r in range(16)],
-           ["gx"] + keys, ["ms"], 0.7)
-        vts(l[0], l[1], T.ms[:, 0:NC], "ms", a, b, A.mult, A.add)
-        return l
-
-    def letters(y, yk, z, zk, out, oc, bank="nt"):
-        f = new("lb")
-        vtt(f[0], f[1], y, yk, z, zk, A.min)
-        no = rot("no", 7)
-        for h in range(2):
-            nt = bank + str(h)
-            mm([(T[nt][0:8, r:512:16], T.hx[:, 8 * r:8 * r + 8], f[2][h], True, True) for r in range(16)], ["hx", f[1]], [nt], 0.4)
-            if h:
-                vcp(T[no][:, HS[h]], no + ".1", T[nt][0:8, :], nt, 0.55)
-            else:
-                act(T[no][:, HS[h]], no + ".0", T[nt][0:8, :], [nt], F.Copy, 0.57)
-        store(out[:, oc:oc + K], T[no][:], halves(no))
-
-    zn = [(T.zn0[:, NC * rank:NC * rank + NC], "zn0")] + [(T["zi%d" % d][:], "zi%d" % d) for d in range(1, N)]
-    res = []
-    ys = [ylist(T.y0n, ["y0n"], -1024.0, 0.0)]
-    for t in range(TW):
-        x = start(t)
-        l = lstart = tolist(x[0], x[1])
-        todo = [(T["my%d" % i], halves("my%d" % i), res[i]) for i in range(t - 1, -1, -1)] + [(T.mk0, halves("mk0"), zn[0])]
-        chain = []
-        prev = None
-        for mask, mkeys, z in todo:
-            n, p = flags(z[0], z[1]) if t else ((T.absn[:, NC * rank:NC * rank + NC], "absn"), None)
-            prev, l = bslot(l[0], l[1], mask, mkeys, n, p, prev, True, True)
-            chain.append(prev)
-        arrive = send(T["br%d1" % t][:], l[0], "rb%d1" % t, (rank + 1) % N, [l[1]], ["br%d1" % t], 1.9)
-        v = rot("v")
-        gather_c([T[v][:, HS[0]], T[v][:, HS[1]]], halves(v), lstart)
-        dead = None
-        for j in range(len(todo)):
-            v, dead, nz = vslot(v, chain[j], todo[j][2], dead, [T.cw[:], T.cw[:]], lambda h: CW, (t, -j))
-            if j < t:
-                res[t - 1 - j] = nz
-            else:
-                zn[0] = nz
-        pend = []
-        for d in range(1, N):
-            x = "%d%d" % (t, d)
-            arrive()
-            home = (rank - d) % N
-            n, p = flags(T["fr%d%d" % (t - 1, d)][:], "fr%d%d" % (t - 1, d)) if t else ((T.absn[:, NC * home:NC * home + NC], "absn"), None)
-            lastd = d == N - 1
-            b, l = bslot(T["br" + x][:], "br" + x, T["mk%d" % d], halves("mk%d" % d), n, p, None, lastd, not lastd)
-            if lastd:
-                pend.append(send(T["bh%d" % t][:], b[0], "rh%d" % t, home, [b[1]], ["bh%d" % t], 1.9))
-                continue
-            k = "%d%d" % (t, d + 1)
-            arrive = send(T["br" + k][:], l[0], "rb" + k, (rank + 1) % N, [l[1]], ["br" + k], 1.9)
-            cs, cg, ck, ak = T["cs" + x], T["cg" + x], halves("cs" + x), halves("cg" + x)
-            gather_c([cs[:, 0:HALF], cs[:, SH + HALF:SH + K]], ck, l)
-            if d == N - 2:
-                pend.append(send(cg[:, SH:SH + HALF], cs[:, 0:HALF], "rc%s0" % x, home, ck[:1], ak[:1], 2.6, True))
-                pend.append(send(cg[:, SH + HALF:2 * (SH + HALF)], cs[:, HALF:SH + K], "rc%s1" % x, home, [ck[1], "csz" + x], ak[1:], 2.6, True))
-            else:
-                pend.append(send(cg[:, SH:2 * (SH + HALF)], cs[:], "rc%s0" % x, home, ck + ["csz" + x], ak, 3.0, True))
-        for f in pend:
-            f()
-        for d in range(1, N):
-            x = "%d%d" % (t, d)
-            if d == N - 1:
-                v, dead, nz = vslot(v, (T["bh%d" % t][:], "bh%d" % t), zn[d], dead, [T.cw3[:], T.cw3[:]], lambda h: ["cw3"], (t, d))
-            else:
-                cg = T["cg" + x]
-                v, dead, nz = vslot(v, (T.jl[:], "jl"), zn[d], dead, [cg[:, 0:SH + HALF], cg[:, SH + HALF:2 * (SH + HALF)]],
-                                    lambda h, x=x: ["cgz" + x if h == 0 else "cg%s.1" % x, "cg%s.%d" % (x, h)], (t, d))
-            zn[d] = nz
-            send(T["fr" + x][:], nz[0], "rf" + x, (rank + d) % N, [nz[1]], ["fr" + x], 2.0)()
-        res.append(dead)
-        if t < TW - 1:
-            yn = "yn%d" % t
-            for h in range(2):
-                kt, nt, ru = "kt%d" % h, "nt%d" % h, "run%d" % h
-                c0 = HALF * h
-                mm([(T[kt][:, 128 * k:128 * k + 128], T[v][:, c0 + 128 * k:c0 + 128 * k + 128], T.idb[:], True, True) for k in range(4)],
-                   ["%s.%d" % (v, h), "idb"], [kt], 0.35)
-                scan(T[ru][:], ru, T.dl[:], "dl", T[kt][:], kt, A.add, A.max, 0.5)
-                q = 2 * t + h
-                mi, bz, hs = T.mi[:, 32 * q:32 * q + 32], T["bz%d" % h], T["hs%d" % h]
-                vts(mi, "mi%d" % q, T[ru][:, 15:HALF:16], ru, -15.0 / 32.0, None, A.add, None)
-                vtt(bz[:, 0:HALF:16], "bz%d" % h, T[ru][:, 15:HALF:16], ru, mi, "mi%d" % q, A.subtract)
-                scan(hs[:], "hs%d" % h, T.ha[:], "ha", bz[:], "bz%d" % h, A.mult, A.add, 0.3)
-                mm([(T[kt][:, 128 * k:128 * k + 128], hs[:, 128 * k:128 * k + 128], T.idb[:], True, True) for k in range(4)],
-                   ["hs%d" % h, "idb"], [kt], 0.35)
-                vts(T[kt][:], kt, T[kt][:], kt, T.ecol[:, 0:1], None, A.is_equal, None, 0.5, ["ecol"])
-                mm([(T[nt][0:8, 128 * k:128 * k + 128], bz[:, 128 * k:128 * k + 128:16], T.idb[:], True, True) for k in range(4)],
-                   ["bz%d" % h, "idb"], [nt], 0.35)
-                act(T[yn][:, HS[h]], "%s.%d" % (yn, h), T[nt][0:8, :], [nt], F.Copy, 0.57)
-            ys.append(ylist(T[yn], halves(yn), 16384.0, -15360.0))
-
-    store(T.yv[:], T[v][:], halves(v))
-
-    def yl_out(d, bank="nt"):
-        s = (rank - d) % N
-        z = zn[0] if d == 0 else (T["fr%d%d" % (TW - 1, d)][:], "fr%d%d" % (TW - 1, d))
-        letters(T.l0n[:, NC * s:NC * s + NC], "l0n", z[0], z[1], T.yl, s * K, bank)
-
-    def yi_out(t):
-        letters(ys[t][0], ys[t][1], res[t][0], res[t][1], T.yi, t * K)
-    for f, a in ((yi_out, 1), (yi_out, 0), (yl_out, 0), (yl_out, 1), (yl_out, 2), (yi_out, 2)):
-        f(a)
-    yl_out(N - 1, "kt")
+        store(T.yl[:, K * s:K * s + K], olc("lo", d - 1), ["lo%d" % d])
     emit(g, T, pl["tasks"])

@@ -15,14 +15,29 @@ PRM = {
     "sum0": "B", "nd": "S", "xs": "S", "start": "G", "dual": False, "lists16": (1, 2), "lag": 3.0,
     "f": 1.15, "g": 1.56, "hop": 2.3, "mk": "SSSS", "my0": "S", "cwait": 2, "iota": 5152, "copyat": 0, "jwait": 1, "cge": ("even", "odd", "odd"),
     "pe": 0.5, "issue": 0.4, "sync": 0.1, "alpha": 6.0, "nudge": (), "dma": 1.0,
-    "jp": [(4096, W), (0, 1024), (1024, 2048), (2048, 3072), (3072, 3584), (3584, 4096)], "copies": (3, 2, 1),
+    "jp": [(4096, W), (0, 1024), (1024, 2048), (2048, 3072), (3072, 3584), (3584, 4096)], "row": 0.04, "cp": [(0, 4096)],
+    "loads": [("S", "ltl1", 0), ("S", "sti", 0), ("S", "y0n", 0), ("S", "ltn", 0), ("Y", "jint0", 0), ("Y", "jint1", 0), ("Y", "jint2", 0),
+              ("Y", "jint3", 0), ("Y", "jint4", 0), ("Y", "jint5", 0), ("Y", "ltl0", "jint3"), ("Y", "ltl2", 0), ("Y", "ltl3", 0),
+              ("Y", "cst", 0), ("Y", "cw0", 0), ("Y", "y0l", "cwa0")],
+    "copies": [(3, 0, WIN, "odd", None), (2, 0, WIN, "odd", ("cw", 0))],
+    "nfe": (("q0", "q2"), ("q0", "q2")), "bhe": ("even", "even", "even"), "spec": (), "order": "", "liafter": None,
 }
-PRM.update({'sum0': 'A', 'alpha': 15, 'f': 1.1, 'hop': 2.3, 'copyat': 0, 'sums': {(2, 0): 'B', (0, 0): 'D', (2, 2): 'C', (1, 2): 'D'},
-            'xs3': 'V', 'iota': 1288, 'remc': ((0, 1), (0, 2), (1, 1), (2, 1)), "lists16": ()})
+PRM.update({'sum0': 'A', 'alpha': 15, 'f': 1.1, 'hop': 2.3, 'sums': {(2, 0): 'B', (0, 0): 'D', (2, 2): 'C', (1, 2): 'D'},
+            'xs3': 'V', 'iota': 1288, 'remc': ((0, 1), (0, 2), (1, 1), (2, 1)), "lists16": (),
+            "cge": dict(((0, d, h), "even") for d in (1, 2) for h in (0, 1))})
+PRM.update({'lists16': (0, 1, 2), 'cge': dict(((t, d, h), "all") for t in range(3) for d in (1, 2, 3) for h in (0, 1)), 'bhe': ('all', 'all', 'all'),
+            'nfe': (('even', 'odd'), ('even', 'odd')), 'xs': 'V',
+            'loads': [('Y', 'sti', 0), ('Y', 'y0n', 0), ('S', 'ltl1', 0), ('S', 'ltn', 0), ('S', 'ltl2', 0), ('Y', 'jint0', 0), ('Y', 'jint1', 0),
+                      ('Y', 'jint2', 0), ('Y', 'jint3', 0), ('Y', 'jint4', 0), ('Y', 'jint5', 0), ('Y', 'ltl0', 'jint3'), ('Y', 'ltl3', 0),
+                      ('Y', 'cst', 0), ('Y', 'cw0', 0), ('Y', 'cw1', ('br', 0, 1, 0)), ('Y', 'y0l', ('cg', 0, 3, 0))],
+            'jp': [(4096, 4608), (0, 1408), (1408, 2432), (2432, 3200), (3200, 3712), (3712, 4096)], 'sum0': 'A',
+            'remc': ((0, 1), (0, 2), (0, 3), (1, 1), (1, 2), (2, 1), (2, 2)), 'copies': [(3, 0, 5136, 'all', ('cg', 0, 3, 1))],
+            'cp': [(0, 2816), (2816, 4096)], 'liafter': ('br', 0, 1, 1), 'spec': (0, 1, 2), 'sums': {(2, -2): 'B', (2, 0): 'B', (1, -1): 'B'}})
+PRM["order"] = "00040J0M1t1x0N1u0206080a0c0R0e0g0i0U0L0k010503070K090b0d0f0h2h0j0Y2i0l1Q0Z0I2j121w0S1T0O130H2m1N0Q0W151y142k2l0y2n2o0P1O2s1R1Z2p0V1W1v2q2t2r190X2y1U2u1P2z250z0A2v1S2w201X2b222A232C1V2x2e1Y2D28210m2G1i290o2B0q0s242H2E2f1j2I260n0p2F1d0r0t272J2g2K2c2L1c2P2d0G0E7E2Q2R2S7F2M2V1a2a7G7H2W7K1b1f1g2X167L2Y1e311l1k2T1h7M7N2U1n7Q1o2Z300B1D1s327R0u330C0D7S347I351E7T38367J170v111C1p7O397U7P3a7V1A7X101z7Y1q0T0F1B1I7Z1r1G181F373b7W3e3x3c833f803g3y848m3h3d85881m3j863A3z3k891H3l1J8a818n3m3B3i3F3C3n3D3G3p878o823E8b8e3q3I3o3r8c3s8f3J3t1K8p3u1L8u8g3H3K8v3v3O3L8h3M3P8d8q3N8i1M8w8j3R3Q3S8r8k3w3V8D2N8x8E3W8s8y3T3X8t8G3U0w3Y8z8l8H8A8L8B403Z2O8F49418C4a8K0x8I4b8M4c4d428J8N434e444f8O8P484g8Y8Z4h908Q914j4i924m938R8X944n954k8S4o4p964l4s5397984t8T9b4q994u4r9c4v4y54459d9e9h8U9a9i9S4w4z559j9n46479f564C8V8W9k4x9g4D579T9l584E9o4H5c4F9U9r4A5d4I4B594J9m9s5e4K4G9p9t9w9u9V5a9x4L4N9W4O9y9X9z4P4Sa19v4Q4T5f4M5b9Y9A4U9C4V5ga24W5j4R9D5k9B5h9qa49E9H4Y9F9I5ma55i4Xa39Z9J4Z5n5la09K5oa850519Ga99L5s5pa6ab5t9N5qac5va75r5u529O5waa9M5z5A9Pad5B9Qae5Cafah5E5D5Nai5x5O9Rak5P5Qag5Rajal5S5yap5F5Taoaq5U5G5Mar5V5Hamatas5W5XaC60aD61aEaF6263aG66aHauaI67av5IaBan5JaJ5Y6869aK6caLaM6daP5K5Law6e6faQ5Z6i6NaRaSaVaxayaN64aO65aW6O6a6jaXaYb1bC6PaT6mazaAb26Qb36b6naUb76RbD6gb4aZ6r6o6hb06p6s6k6t6W6u6Sb56YbE6X6vb86l6T736qbbbF6xbc6w74bdbgb6bebG6y75bhb9bS6z6C766A6D6Z6EbL6F7bbfbHbNba706Gbibj6U77bm6B7cbk6V6IbnbMbT78bI6Hbobrbp71bs6J72bt7dbu7e6Kbl6LbJ797fbKbU7kbv7acF7gbV7lbObq7h7m7nbx6Mc07obPcGbw7ic1bW7j7rbyc27wbQbz7xbX7pbA7yc3c9c47qbR7zcD7sbYbZca7t7AcJcbc5bBcc7Bc6cxc7cdcEc8cecg7ucl7vcKcf7Ccmchcz7DcncycicoctcpcLcAcjcqcrckcBcscucNcvcHcMcCcOcwcPcIcQ"
 PARTS = PRM["parts"]
 NP = len(PARTS)
 PM = 16 * max(PARTS)
-NU, NF, NB, NH, NRU, NRF, NRB = 44, 24, 48, 24, 10, 10, 8
+NU, NF, NB, NH, NRU, NRF, NRB = 46, 19, 36, 19, 13, 7, 8
 
 SCRATCH = {
     "jint": ("sbuf", [128, W], "int32"), "jw": ("sbuf", [128, 2 * D], "float32"),
@@ -49,7 +64,11 @@ SCRATCH = {
 }
 for _i in ("xcol", "x16", "ecol", "mb1", "mb2"):
     SCRATCH[_i] = ("sbuf", [128, 1], "float32")
-for _i in ("idb", "idn", "idm", "idh", "idg"):
+if PRM["spec"]:
+    SCRATCH["vw"] = ("sbuf", [128, 6 * K], "bfloat16")
+SCRATCH["zz"] = ("sbuf", [128, 6 * NC], "bfloat16")
+SCRATCH["zo"] = ("sbuf", [128, 2 * NC], "bfloat16")
+for _i in ("idb", "idn", "idm", "idh", "idg", "idw"):
     SCRATCH[_i] = ("sbuf", [128, 128], "bfloat16")
 BANKS = ["xa0", "xa1", "xc0", "xc1", "kt0", "kt1", "ms0", "ms1"]
 for _i in BANKS:
@@ -61,8 +80,7 @@ for _i in range(N):
 for _i in range(TW):
     SCRATCH["my%d" % _i] = ("sbuf", [128, K], "bfloat16")
 for _i in range(3):
-    for _n in ("v", "mt"):
-        SCRATCH[_n + str(_i)] = ("sbuf", [128, K], "bfloat16")
+    SCRATCH["v" + str(_i)] = ("sbuf", [128, K], "bfloat16")
 for _i in range(2):
     SCRATCH["md%d" % _i] = ("sbuf", [128, K], "float16")
     if PRM["start"] != "G":
@@ -105,8 +123,8 @@ def order(tasks):
     for i in range(n):
         for j in tasks[i]["tdeps"]:
             succ[j].append(i)
-    edge = [[(j, tasks[i]["cost"] + (0.0 if i in tasks[j].get("soft", ()) else tasks[i]["lat"])
-              + (0.0 if tasks[j]["eng"] == "R" else 0.06 if tasks[j]["eng"] == tasks[i]["eng"] else PRM["sync"])) for j in succ[i]]
+    edge = [[(j, tasks[i]["cost"] + tasks[i]["lat"]
+              + (tasks[j]["pre"] if tasks[j]["eng"] == "R" else 0.06 if tasks[j]["eng"] == tasks[i]["eng"] else PRM["sync"])) for j in succ[i]]
             for i in range(n)]
     pri = [0.0] * n
     left = [len(t["tdeps"]) for t in tasks]
@@ -122,6 +140,9 @@ def order(tasks):
     for seed in PRM["nudge"]:
         nudge(own, seed)
     seq, start = run_list(tasks, edge, own, PRM["alpha"])
+    if len(PRM["order"]) == 2 * n:
+        ch = "0123456789abcdefghijklmnopqrstuvwxyzABCDEFGHIJKLMNOPQRSTUVWXYZ"
+        seq = [ch.index(PRM["order"][2 * i]) * 62 + ch.index(PRM["order"][2 * i + 1]) for i in range(n)]
     PRM["span"] = (max(start), max(pri))
     PRM["dbg"] = (tasks, start, pri, succ, edge, own)
     return seq
@@ -147,6 +168,7 @@ def run_list(tasks, edge, own, alpha):
         if left[i] == 0:
             todo[tasks[i]["eng"]].append(i)
     seq = []
+    dma = [0.0] * 4
     while len(seq) < n:
         best = None
         for e in "RYGVSP":
@@ -158,9 +180,13 @@ def run_list(tasks, edge, own, alpha):
         i = max(todo[e], key=lambda a: (own[a] - alpha * max(0.0, rt[a] - s), -a)) if e != "R" else min(todo[e], key=lambda a: rt[a])
         todo[e].remove(i)
         s = max(s, rt[i])
-        start[i] = s
         if e != "R":
             free[e] = s + tasks[i]["cost"]
+        else:
+            s = max([s] + [dma[c] for c in tasks[i]["cls"]])
+            for c in tasks[i]["cls"]:
+                dma[c] = s + tasks[i]["cost"]
+        start[i] = s
         seq.append(i)
         for j, c in edge[i]:
             left[j] -= 1
@@ -289,7 +315,14 @@ def rank_program(g, core, T, topo):
         return {"all": en, "even": en[0::2], "odd": en[1::2], "lo": en[:len(en) // 2], "hi": en[len(en) // 2:],
                 "q0": en[0::4], "q2": en[2::4]}[kind]
 
-    def send(trs, lat, reads=(), after=None):
+    def landing(i, sem, inc, keys, kind, rows, rb, pre, lat, rate=14.0):
+        cls = {"all": (0, 1, 2, 3), "even": (0, 2), "odd": (1, 3), "q0": (0,), "q2": (2,), "q1": (1,), "q3": (3,)}[kind]
+        dur = rows / (4.0 * len(cls)) * (PRM["row"] + rb * PRM["dma"] / (1000.0 * rate))
+        j = add(pl, "R", dur, [], keys, None, sem=sem, inc=inc, after=[i], lat=lat)
+        pl["tasks"][j]["cls"] = cls
+        pl["tasks"][j]["pre"] = pre
+
+    def send(trs, rb, name=None):
         made, tot, arr = [], 0, []
         for src, sk, kind, dsts in trs:
             en = engines(cores[dsts[0][0] % N], kind)
@@ -297,7 +330,7 @@ def rank_program(g, core, T, topo):
             ids = [topo.addr(cores[to % N]) for to, _, _ in dsts]
             made.append((src, sem, ids, [o for _, o, _ in dsts], sum(1 << x for x in en)))
             tot += len(en)
-            arr.append((sem, len(en) * len(dsts), [k for _, _, k in dsts]))
+            arr.append((sem, len(en) * len(dsts), [k for _, _, k in dsts], kind))
 
         def call():
             if len(made) == 1 and len(made[0][2]) == 1:
@@ -309,57 +342,71 @@ def rank_program(g, core, T, topo):
         keys = []
         for x in trs:
             keys += x[1] if isinstance(x[1], list) else [x[1]]
-        i = add(pl, "G", PRM["issue"], keys + list(reads), [], call, inc=tot, kind="r", after=after)
-        for sem, n, ks in arr:
-            add(pl, "R", 0.0, [], ks, None, sem=sem, inc=n, after=[i], lat=lat)
+        i = add(pl, "G", PRM["issue"], keys, [], call, inc=tot, kind="r")
+        pre = HOP - 0.7 + (3.5 if take("first") == 0 else 0.0)
+        for sem, n, ks, kind in arr:
+            landing(i, sem, n, ks, kind, 128 * len(ks), rb, pre, 0.25, 11.0 if kind == "all" else 13.0)
+        event[name] = i
         return i
 
-    def load(eng, out, in_, key, lat, reads=()):
+    def load(eng, out, in_, key, rows, rb, reads=()):
         qq = syn if eng == "Y" else sca
-        i = add(pl, eng, 0.1, list(reads), [key], lambda: [qq.dma_start(out, in_)], sem="ld%d" % take("ld"), lat=lat, kind="d",
-                after=used.get(eng))
+        sem = "ld%d" % take("ld")
+        i = add(pl, eng, 0.1, list(reads), [], lambda: [qq.dma_start(out, in_)], sem=sem, kind="d", after=used.get(eng))
         pl["tasks"][i]["first"] = True
-        pl["tasks"][i]["soft"] = used.get(eng, [])
         used[eng] = [i]
+        landing(i, sem, 16, [key], "all", rows, rb, 1.6, 0.0)
 
-    def store(out, in_, reads):
-        add(pl, "Y", 0.1, reads, [], lambda: [syn.dma_start(out, in_)], sem="st%d" % take("st"), lat=2.0, kind="d")
+    def store(out, in_, reads, rb):
+        sem = "st%d" % take("st")
+        i = add(pl, "Y", 0.1, reads, [], lambda: [syn.dma_start(out, in_)], sem=sem, kind="d")
+        landing(i, sem, 16, [], "all", 128, rb, 1.6, 0.0)
 
     def both(k):
         return ["%s.%d" % (k, h) for h in range(NP)]
 
-    load("S", T.sti[:], T.st[:], "sti", 2.4)
-    load("S", T.y0n[:], T.y0[:], "y0n", 2.4)
-    def letters(eng, d, lat, reads=()):
+    event = {}
+    late = []
+
+    def letters(eng, d, reads=()):
         s = (rank - d) % N
-        load(eng, T.ltl[:, NC * d:NC * d + NC], T.lt[:, K * s:K * s + K], "ltl%d" % d, lat, reads)
-    letters("S", 1, 2.8)
-    load("S", T.ltn[:], T.lt[:], "ltn", 3.2)
+        load(eng, T.ltl[:, NC * d:NC * d + NC], T.lt[:, K * s:K * s + K], "ltl%d" % d, 128, 128, reads)
     JP = PRM["jp"]
-    at, base, land = 3.2, 0.0, []
-    for p, (a, b) in enumerate(JP):
-        at += (b - a) * 512 / 2.0e5 * PRM["dma"]
-        land.append(at)
-        if p == PRM["jwait"]:
-            base = 2.5
-        load("Y", T.jint[:, a:b], T.jm[:, a:b], "jint%d" % p, at - base, ["sti"] if p == PRM["jwait"] else [])
-    cwait = ["jint%d" % PRM["cwait"]]
-    base = land[PRM["cwait"]]
-    for k, d in enumerate((0, 2, 3)):
-        letters("Y", d, at + 0.4 * (k + 2) - base, cwait)
-    load("Y", T.cst[:], T.cf[:, 4096:W], "cst", at + 2.5 - base)
-    load("Y", T.cw0[:, SH:SH + 4096], T.cf[:, 0:4096], "cwa", at + 2.0 + 5.3 * PRM["dma"] - base)
-    load("Y", T.y0l[:], T.y0[:], "y0l", 3.0, ["cwa"])
+    for eng, what, wait in PRM["loads"]:
+        if isinstance(wait, tuple):
+            late.append((len(pl["tasks"]), wait))
+            wait = None
+        wait = [wait] if wait else []
+        if what == "sti":
+            load(eng, T.sti[:], T.st[:], what, 128, 768, wait)
+        elif what == "y0n":
+            load(eng, T.y0n[:], T.y0[:], what, 16, 1024, wait)
+        elif what == "ltn":
+            load(eng, T.ltn[:], T.lt[:], what, 16, 4096, wait)
+        elif what == "y0l":
+            load(eng, T.y0l[:], T.y0[:], what, 128, 128, wait)
+        elif what == "cst":
+            load(eng, T.cst[:], T.cf[:, 4096:W], what, 128, 1024, wait)
+        elif what[:2] == "cw":
+            a, b = PRM["cp"][int(what[2])]
+            load(eng, T.cw0[:, SH + a:SH + b], T.cf[:, a:b], "cwa" + what[2], 128, 2 * (b - a), wait)
+        elif what[:3] == "ltl":
+            letters(eng, int(what[3]), wait)
+        else:
+            a, b = JP[int(what[4])]
+            load(eng, T.jint[:, a:b], T.jm[:, a:b], what, 128, 4 * (b - a), wait)
 
     def lic(i, b="li"):
         return T[b][:, NC * i:NC * i + NC]
-    send([(T.ltl[:, NC:2 * NC], "ltl1", "all", [(rank - 1, lic(0), "li0")])], at - 3.0)
-    send([(T.ltl[:, 2 * NC:3 * NC], "ltl2", "even", [(rank - 1, lic(3), "li3"), (rank - 2, lic(1), "li1")]),
-          (T.ltl[:, 3 * NC:4 * NC], "ltl3", "odd", [(rank - 1, lic(4), "li4"), (rank - 3, lic(2), "li2")])], 5.0)
-    vts(lic(0, "zi"), "zi0", lic(0), "li0", 15.5, -float(D), A.is_ge, A.mult)
-    add(pl, "V", el(128), ["li%d" % i for i in range(1, 5)], ["zi"],
-        lambda: [vec.tensor_scalar(T.zi[:, NC:5 * NC], T.li[:, NC:5 * NC], 15.5, -float(D), A.is_ge, A.mult)])
+    send([(T.ltl[:, NC:2 * NC], "ltl1", "even", [(rank - 1, lic(0), "li0")]),
+          (T.ltl[:, 2 * NC:3 * NC], "ltl2", "odd", [(rank - 1, lic(1), "li1")])], 128)
+    send([(T.ltl[:, 2 * NC:3 * NC], "ltl2", "even", [(rank - 2, lic(2), "li2")]),
+          (T.ltl[:, 3 * NC:4 * NC], "ltl3", "odd", [(rank - 1, lic(4), "li4"), (rank - 3, lic(3), "li3")])], 128, "li")
+    vts(T.zi[:, 0:2 * NC], "zi0", T.li[:, 0:2 * NC], "li0", 15.5, -float(D), A.is_ge, A.mult, None, ["li1"])
+    vts(T.zi[:, 2 * NC:5 * NC], "zi", T.li[:, 2 * NC:5 * NC], "li2", 15.5, -float(D), A.is_ge, A.mult, el(96), ["li3", "li4"])
     vts(T.z0[:], "z0", T.ltl[:, 0:NC], "ltl0", 15.5, -float(D), A.is_ge, A.mult)
+    if 0 in PRM["spec"]:
+        vts(T.zo[:], "zo", T.ltl[:, NC:3 * NC], "ltl1", 15.5, -float(D), A.is_ge, A.mult, None, ["ltl2"])
 
     def gsel(ap, key, pat, op, base, cm):
         return add(pl, "G", 0.42, [key], [key], lambda: [g.affine_select(ap, ap, pat, op, 0.0, base, cm)])
@@ -379,7 +426,7 @@ def rank_program(g, core, T, topo):
     giota(T.smi[:], "smi", [[16, 12], [0, 16]], 0, 1, 192, False)
     giota(T.jl0[:], "jl0", [[16, NC]], -PH, 0, NC)
     giota(T.pm0[:], "pm0", [[1, 16], [256, 4]], 0, 0, NC)
-    JW = ["jwz", "jwu", "jwv"] + ["jw%d" % p for p in range(8)]
+    JW = ["jwz", "jwu", "jwv"]
     nio = PRM["iota"]
     for a in range(0, nio, 1288):
         b = min(nio, a + 1288)
@@ -404,7 +451,7 @@ def rank_program(g, core, T, topo):
         lambda: [sca.activation(T.eb[:, 128 * x + x:128 * x + 128:16], T.blk[:, x:128:16], F.Copy) for x in range(16)])
     for a in range(0, 2048, 256):
         act(T.ebx[:, a:a + 256], "ebx%d" % a, T.eb[:, a:a + 256], ["eb", "xcol"], F.Copy, el(256), scale=T.xcol[:, 0:1])
-    for m, c in (("idn", -1.0), ("idm", -0.5), ("idh", D / 2.0), ("idg", -D / 2.0), ("idf", 1.0)):
+    for m, c in (("idn", -1.0), ("idm", -0.5), ("idh", D / 2.0), ("idg", -D / 2.0), ("idf", 1.0), ("idw", PM / 2.0)):
         act(T[m][:], m, T.idb[:], ["idb"], F.Copy, el(128), scale=c)
     memset(T.dl[:], "dl", 1.0 / 16.0, PM)
     memset(T.dl[:, 0:PM:16], "dl", -1000.0)
@@ -432,7 +479,7 @@ def rank_program(g, core, T, topo):
             if eng == "V":
                 vts(o, ok, T[bk][:, 0:16 * n], bk, 15.0, T.xcol[:, 0:1], A.min, A.is_equal, el(16 * n), ["xcol"])
             else:
-                mt = rot("mt", h, 3)
+                mt = rot("gh", h)
                 act(mt[0], mt[1], T[bk][:, 0:16 * n], [bk, "mb1"], F.Abs, el(16 * n), bias=T.mb1[:, 0:1])
                 act(o, ok, mt[0], [mt[1], "mb2"], F.Relu, el(16 * n), bias=T.mb2[:, 0:1], scale=-1.0)
     onehot(T.y0n, "y0n", 0, "my0", PRM["my0"])
@@ -455,23 +502,24 @@ def rank_program(g, core, T, topo):
     for p, (a0, b0) in enumerate(JP):
         for a in range(a0, b0, 512):
             bk = ("xa0", "xa1", "xc0", "xc1")[take("jb") % 4]
-            src, ik = T.jint[:, a:a + 512], "jint%d" % p
-            vts(T[bk][:], bk, src, ik, 4096.0, -6144.0, A.max, A.add, el(512))
+            m = min(512, b0 - a)
+            src, ik = T.jint[:, a:a + m], "jint%d" % p
+            vts(T[bk][:, 0:m], bk, src, ik, 4096.0, -6144.0, A.max, A.add, el(m))
             if a < 4096:
-                vtt(T.jw[:, SH + a:SH + a + 512], "jw%d" % (a // 512), src, ik, T[bk][:], bk, A.add, el(512))
+                JW.append("jw%d" % a)
+                vtt(T.jw[:, SH + a:SH + a + m], JW[-1], src, ik, T[bk][:, 0:m], bk, A.add, el(m))
             else:
                 add(pl, "V", el(512), [ik, bk], ["jwu", "jwv"],
                     lambda src=src, bk=bk: [vec.tensor_tensor(T.jw[:, SH + 4096:WIN:2], src, T[bk][:], A.add)])
     act(T.cw0[:, SH + 4096:WIN:2], "cwu", T.cst[:], ["cst"], F.Copy, el(512))
-    CW = ["cwz", "cwu", "cwa"]
-    need = [d for d in PRM["copies"] if any((t, d) not in PRM["remc"] for t in range(TW))]
-    bulk = []
-
-    def copies(after):
-        for k, d in enumerate(need):
-            after = [send([(T.cw0[:], CW, "odd", [(rank - d, T["cw%d" % d][:], "cw%d" % d)])], 2.0 + 12.0 * PRM["dma"] * (k + 1), after=after)]
-    copies([])
-    copytasks = [i for i, x in enumerate(pl["tasks"]) if x["kind"] == "r"][-len(need)]
+    CW = ["cwz", "cwu"] + ["cwa%d" % k for k in range(len(PRM["cp"]))]
+    CK = dict((d, []) for d in range(1, N))
+    follow = []
+    for k, (d, a, b, kind, ev) in enumerate(PRM["copies"]):
+        rd = [x for x in CW if x == "cwz" and a < SH or x == "cwu" and b > SH + 4096]
+        rd += ["cwa%d" % j for j, (p0, p1) in enumerate(PRM["cp"]) if SH + p0 < b and SH + p1 > a]
+        CK[d].append("cw%d.%d" % (d, a))
+        follow.append((send([(T.cw0[:, a:b], rd, kind, [(rank - d, T["cw%d" % d][:, a:b], CK[d][-1])])], 2 * (b - a), ("cw", k)), ev))
 
     ND = PRM["nd"]
     DP, DN, DC = ("idh", "idg", -D / 2.0) if ND == "S" else ("idb", "idn", 0.0)
@@ -522,20 +570,51 @@ def rank_program(g, core, T, topo):
             vts(o[0], o[1], q, ms, c, 16.0, A.add, A.min)
             return o
 
+        def version(k):
+            a = 6 * 16 * C0[h] + k * nw
+            return (T.vw[:, a:a + nw], "vw%d.%d" % (k, h))
+
+        def ahead(base, zn):
+            u = T[ms][:, n:2 * n]
+            lin(u, ms, base + ([("idb", zn)] if zn else []))
+            return tolist(u, ms)
+
+        def choice(deads):
+            q = T[ms][:, 0:n]
+            lin(q, ms, [("idb", part("jl", h))] + [("idw", x) for x in deads])
+            return tolist(q, ms, -SH + nw + len(deads) * nw / 2.0)
+
+        def chosen(l, m):
+            v = rot("v", h, 3)
+            a = 6 * 16 * C0[h]
+            act(v[0], v[1], T.vw[:, a:a + (m + 1) * nw].indirect(l[0]), [version(k)[1] for k in range(m + 1)] + [l[1]], F.Identity, ga(nw))
+            return v
+
         def vslot(v, base, zn, dead, win, wkeys, at, out):
             last = at == (TW - 1, N - 1)
+            spec = at[0] in PRM["spec"] and at[1] < N - 1
             u = T[xc][:, 0:n]
             dt, dc = ([(DP, dead)], DC) if dead else ([], 0.0)
             if last:
                 lc = letter(out[0], [("idn", zn)], 0.0, None)
                 yc = letter(out[2], [(DN, dead)], -DC, None)
-            lin(u, xc, base + [("idb", zn)] + dt)
-            l = tolist(u, xc, dc)
-            how = "A" if last else PRM["sums"].get(at, PRM["sum0"])
-            sg, nv = rot("sg", h), None if last else rot("v", h, 3)
+            if isinstance(base, tuple):
+                l = base
+            elif spec:
+                l = ahead(base, zn) if base else None
+            else:
+                lin(u, xc, base + [("idb", zn)] + dt)
+                l = tolist(u, xc, dc)
+            how = "A" if last else PRM["sums"].get(at + (h,), PRM["sums"].get(at, PRM["sum0"]))
+            if not base:
+                how = "B" if how in "AB" else "C"
+            sg, nv = rot("sg", h), None if last else version(at[0] + at[1] + 1) if spec else rot("v", h, 3)
             if how in "BC":
-                gh = rot("gh", h)
-                act(gh[0], gh[1], win.indirect(l[0]), wkeys + [l[1]], F.Identity, ga(nw))
+                if base:
+                    gh = rot("gh", h)
+                    act(gh[0], gh[1], win.indirect(l[0]), wkeys + [l[1]], F.Identity, ga(nw))
+                else:
+                    gh = (win, wkeys)
                 src = (T[kt][:, 0:nw], kt)
                 mm([(src[0], T.idb[:], v[0], True, False), (src[0], T.idb[:], gh[0], False, True)], ["idb", v[1], gh[1]], [kt], pe(2, nw))
                 cl = el(nw)
@@ -572,15 +651,20 @@ def rank_program(g, core, T, topo):
             if out:
                 letter(out[0], [("idn", zn), (DN, nd)] + dt, dc - DC, out[1])
                 return nv, nd, None
-            nz = new("lb", h)
+            if at[1] > 0:
+                a = 3 * (NC * at[0] + C0[h]) + n * (at[1] - 1)
+                nz = (T.zz[:, a:a + n], "zz%d%d.%d" % (at[0], at[1], h))
+            else:
+                nz = new("lb", h)
             q = T[ms][:, 0:n]
             lin(q, ms, [("idb", zn), (DP, nd)] + ([(DN, dead)] if dead else []))
             act(nz[0], nz[1], q, [ms], F.Identity, bias=DC - dc)
             return nv, nd, nz
 
-        zn = [part("z0", h), (part("zi", h)[0], "zi0")] + [part("zi", h, d - 1) for d in range(2, N)]
-        nf = [None, part("zi", h, 3), part("zi", h, 4), None]
-        lts = [(T.ltl[:, LC[h]], "ltl0")] + [(T.li[:, NC * i + C0[h]:NC * i + C0[h] + n], "li%d" % i) for i in range(3)]
+        zn = [part("z0", h), (part("zi", h)[0], "zi0")] + [part("zi", h, d) for d in range(2, N)]
+        nf = [None, (part("zi", h, 1)[0], "zi0"), part("zi", h, 4), None]
+        of = [None, part("zo", h, 0), part("zo", h, 1), None]
+        lts = [(T.ltl[:, LC[h]], "ltl0")] + [(T.li[:, NC * i + C0[h]:NC * i + C0[h] + n], "li%d" % i) for i in (0, 2, 3)]
         res = []
         ys = [part("y0l", h)]
         for t in range(TW):
@@ -595,14 +679,19 @@ def rank_program(g, core, T, topo):
                 x = summed(md, todo[0][1])
                 act(T["my%d" % t][:, WC[h]], "my%d.%d" % (t, h), T[kt][:, 0:nw], [kt], F.Copy, el(nw))
             l = tolist(x, xa)
+            spec = t in PRM["spec"]
             chain = [keep(x, todo[0][1], PRM["xs"])[1]]
+            if spec:
+                chain[0] = ahead(chain[0], None)
             for j in range(len(todo)):
                 nxt = todo[j + 1][1] if j < t else zn[1]
                 x = image(l, todo[j][0], nxt)
                 l = tolist(x, xa)
                 chain.append(keep(x, nxt, PRM["xs"])[1])
+                if spec:
+                    chain[-1] = ahead(chain[-1], todo[j][1])
             br = new("ru", h)
-            send([(l[0], l[1], le, [(rank + 1, br[0], br[1])])], HOP)
+            send([(l[0], l[1], le, [(rank + 1, br[0], br[1])])], 2 * n, ("br", t, 1, h))
             if t:
                 q, my, w0 = T[ms][:, 0:n], T["my%d" % t], 16 * C0[h]
                 mm([(q, T.ebx[:, 128 * r:128 * r + 128], my[:, w0 + r:w0 + nw:16], r == 0, r == 15) for r in range(16)],
@@ -624,7 +713,7 @@ def rank_program(g, core, T, topo):
                     if PRM["dual"] and not rem:
                         a, b = new("ru", h), new("lf", h)
                         to.append((rank - d, a[0], a[1]))
-                    send([(l[0], l[1], le, to)], HOP)
+                    send([(l[0], l[1], le, to)], 2 * n, ("br", t, d + 1, h))
                     if PRM["dual"] and not rem:
                         vts(b[0], b[1], a[0], a[1], -OFF, None, A.add, None)
                         home[d] = [("idf", b), ("idb", zn[d + 1])]
@@ -632,49 +721,66 @@ def rank_program(g, core, T, topo):
                 b, terms = keep(x, nf[d], PRM["xs"] if d < N - 1 else PRM.get("xs3", PRM["xs"]))
                 if rem:
                     u = T[xa][:, n:2 * n]
-                    lin(u, xa, terms)
+                    lin(u, xa, terms + ([("idb", of[d])] if spec and of[d] else []))
                     l = tolist(u, xa)
                     nm = "%d%d" % (t, d)
                     cs = (T["cs" + nm][:, WC[h]], "cs%s.%d" % (nm, h))
                     gather_c(cs, l)
                     a = 16 * C0[h] + SH * (h + 1)
-                    bulk.append((t, d, send([(cs[0], cs[1], PRM["cge"][t], [(rank - d, T["cg" + nm][:, a:a + nw], "cg%s.%d" % (nm, h))])],
-                                            HOP + (0.6 if PRM["cge"][t] == "all" else 1.2))))
+                    send([(cs[0], cs[1], PRM["cge"].get((t, d, h), "odd"), [(rank - d, T["cg" + nm][:, a:a + nw], "cg%s.%d" % (nm, h))])],
+                         2 * nw, ("cg", t, d, h))
                 else:
                     a = new("rf" if terms[0][0] == "idf" else "rh", h)
-                    send([(b[0], b[1], le, [(rank - d, a[0], a[1])])], HOP)
+                    send([(b[0], b[1], le if d == N - 1 else PRM["bhe"][t], [(rank - d, a[0], a[1])])],
+                         (4 if terms[0][0] == "idf" else 2) * n, ("bh", t, d, h))
                     home[d] = [(terms[0][0], a)] + ([("idb", zn[d + 1])] if len(terms) > 1 else [])
-            u = T[xc][:, 0:n]
-            lin(u, xc, chain[0])
-            l = tolist(u, xc)
-            v = rot("v", h, 3)
+            if spec:
+                l, v = chain[0], version(0)
+            else:
+                u = T[xc][:, 0:n]
+                lin(u, xc, chain[0])
+                l = tolist(u, xc)
+                v = rot("v", h, 3)
             gather_c(v, l)
             dead = None
+            deads = []
             fin = t == TW - 1
             for j in range(len(todo)):
                 v, dead, nz = vslot(v, chain[j + 1], todo[j][1], dead, T.cw0[:], CW, (t, j - t), todo[j][2] if fin else None)
+                deads.append(dead)
                 if j < t:
                     res[t - 1 - j] = nz
                 else:
                     zn[0] = nz
             for d in range(1, N):
                 out = ((lts[d], d) + ((ys[t], 4 + t) if d == N - 1 else ())) if fin else None
+                if spec and d == N - 2:
+                    pick = choice(deads)
+                if spec and d == N - 1:
+                    v = chosen(pick, len(deads))
+                nm = "%d%d" % (t, d)
+                a = 16 * C0[h] + SH * h
                 if d in home:
-                    v, dead, nz = vslot(v, home[d], zn[d], dead, T["cw%d" % d][:], ["cw%d" % d], (t, d), out)
+                    v, dead, nz = vslot(v, home[d], zn[d], dead, T["cw%d" % d][:], CK[d], (t, d), out)
+                elif spec and d < N - 1:
+                    v, dead, nz = vslot(v, None, zn[d], dead, T["cg" + nm][:, a + SH:a + SH + nw], "cg%s.%d" % (nm, h), (t, d), out)
                 else:
-                    nm = "%d%d" % (t, d)
-                    a = 16 * C0[h] + SH * h
                     v, dead, nz = vslot(v, [("idb", part("jl", h))], zn[d], dead, T["cg" + nm][:, a:a + SH + nw],
                                         ["cgz%s.%d" % (nm, h), "cg%s.%d" % (nm, h)], (t, d), out)
+                deads.append(dead)
                 zn[d] = nz
             if fin:
                 break
-            nf = [None, new("rb", h), new("rb", h), None]
-            send([(zn[2][0], zn[2][1], "even", [(rank + 1, nf[1][0], nf[1][1])]),
-                  (zn[3][0], zn[3][1], "odd" if t in PRM["lists16"] else "even", [(rank + 2, nf[2][0], nf[2][1])])][0:2]
-                 if t in PRM["lists16"] else
-                 [(zn[2][0], zn[2][1], "q0", [(rank + 1, nf[1][0], nf[1][1])]), (zn[3][0], zn[3][1], "q2", [(rank + 2, nf[2][0], nf[2][1])])],
-                 HOP + 0.5)
+            a = 3 * (NC * t + C0[h])
+            b = 4 * (NC * t + C0[h])
+            of = [None] + [(T.rb[:, b + 2 * n * i:b + 2 * n * i + n], "rb%d%d.%d" % (t, i, h)) for i in range(2)] + [None]
+            nf = [None] + [(T.rb[:, b + 2 * n * i + n:b + 2 * n * i + 2 * n], "rb%d%d.%d" % (t, i, h)) for i in range(2)] + [None]
+            if t + 1 in PRM["spec"] and ((t + 1, 1) in PRM["remc"] or (t + 1, 2) in PRM["remc"]):
+                send([(T.zz[:, a + n * i:a + n * i + 2 * n], [zn[i + 1][1], zn[i + 2][1]], PRM["nfe"][t][i],
+                       [(rank + 1 + i, T.rb[:, b + 2 * n * i:b + 2 * n * i + 2 * n], nf[i + 1][1])]) for i in range(2)], 4 * n, ("nf", t, h))
+            else:
+                send([(zn[i + 2][0], zn[i + 2][1], PRM["nfe"][t][i], [(rank + 1 + i, nf[i + 1][0], nf[i + 1][1])]) for i in range(2)],
+                     2 * n, ("nf", t, h))
             if ND == "S":
                 r = new("lb", h)
                 act(r[0], r[1], dead[0], [dead[1]], F.Identity, scale=D / 2.0, bias=DC)
@@ -703,19 +809,25 @@ def rank_program(g, core, T, topo):
         pl["bias"] = PRM["lag"] * (NP - 1 - h)
         words(h)
     pl["bias"] = 0.0
-    if PRM["copyat"]:
-        pl["tasks"][copytasks]["tdeps"] += [b for t, d, b in bulk if (t, d) == PRM["copyat"]]
+    for i, ev in follow + [(event["li"], PRM["liafter"])]:
+        if ev:
+            pl["tasks"][i]["tdeps"].append(event[ev])
+    for i, ev in late:
+        for k in ("deps", "tdeps"):
+            pl["tasks"][i][k].append(event[ev] + 1)
 
     def olc(b, i):
         return T[b][:, NC * i:NC * i + NC]
-    add(pl, "V", ga(K), both("tmf") + both("ol3") + ["pm"], ["vo"], lambda: [vec.tensor_scalar(T.vo[:], T.tmf[:].indirect(T.pm[:]), 255.0, -255.0, A.min, A.max)])
-    send([(olc("ol", d), both("ol%d" % d), ("even", "odd")[d - 1], [(rank + d, olc("lo", d - 1), "lo%d" % d)]) for d in (1, 2)], HOP)
-    send([(olc("ol", 3), both("ol3"), "all", [(rank + 3, olc("lo", 2), "lo3")])], HOP)
+    for k in range(2):
+        add(pl, "V", ga(K // 2), both("tmf") + (both("ol3") if k else []) + ["pm"], ["vo%d" % k],
+            lambda k=k: [vec.tensor_scalar(T.vo[:, 512 * k:512 * k + 512], T.tmf[:].indirect(T.pm[:, 32 * k:32 * k + 32]), 255.0, -255.0, A.min, A.max)])
+    store(T.yv[:], T.vo[:], ["vo0", "vo1"], 2048)
+    for d in range(1, N):
+        send([(olc("ol", d), both("ol%d" % d), "all", [(rank + d, olc("lo", d - 1), "lo%d" % d)])], 128)
     for t in range(TW):
-        store(T.yi[:, K * t:K * t + K], olc("ol", 4 + t), both("ol%d" % (4 + t)))
-    store(T.yl[:, K * rank:K * rank + K], olc("ol", 0), both("ol0"))
-    store(T.yv[:], T.vo[:], ["vo"])
+        store(T.yi[:, K * t:K * t + K], olc("ol", 4 + t), both("ol%d" % (4 + t)) + (["vo1"] if t == TW - 1 else []), 128)
+    store(T.yl[:, K * rank:K * rank + K], olc("ol", 0), both("ol0"), 128)
     for d in range(1, N):
         s = (rank - d) % N
-        store(T.yl[:, K * s:K * s + K], olc("lo", d - 1), ["lo%d" % d])
+        store(T.yl[:, K * s:K * s + K], olc("lo", d - 1), ["lo%d" % d], 128)
     emit(g, T, pl["tasks"])

@@ -20,7 +20,7 @@ PRM = {
               ("Y", "jint3", 0), ("Y", "jint4", 0), ("Y", "jint5", 0), ("Y", "ltl0", "jint3"), ("Y", "ltl2", 0), ("Y", "ltl3", 0),
               ("Y", "cst", 0), ("Y", "cw0", 0), ("Y", "y0l", "cwa0")],
     "copies": [(3, 0, WIN, "odd", None), (2, 0, WIN, "odd", ("cw", 0))],
-    "nfe": (("q0", "q2"), ("q0", "q2")), "bhe": ("even", "even", "even"), "spec": (), "order": "", "liafter": None,
+    "nfe": (("q0", "q2"), ("q0", "q2")), "bhe": ("even", "even", "even"), "spec": (), "order": "", "liafter": None, "ljafter": ("br", 0, 2, 1), "direct": True, "hdirect": "", "pair": (), "half": (),
 }
 PRM.update({'sum0': 'A', 'alpha': 15, 'f': 1.1, 'hop': 2.3, 'sums': {(2, 0): 'B', (0, 0): 'D', (2, 2): 'C', (1, 2): 'D'},
             'xs3': 'V', 'iota': 1288, 'remc': ((0, 1), (0, 2), (1, 1), (2, 1)), "lists16": (),
@@ -34,10 +34,16 @@ PRM.update({'lists16': (0, 1, 2), 'cge': dict(((t, d, h), "all") for t in range(
             'remc': ((0, 1), (0, 2), (0, 3), (1, 1), (1, 2), (2, 1), (2, 2)), 'copies': [(3, 0, 5136, 'all', ('cg', 0, 3, 1))],
             'cp': [(0, 2816), (2816, 4096)], 'liafter': ('br', 0, 1, 1), 'spec': (0, 1, 2), 'sums': {(2, -2): 'B', (2, 0): 'B', (1, -1): 'B'}})
 PRM["order"] = "00040J0M1t1x0N1u0206080a0c0R0e0g0i0U0L0k010503070K090b0d0f0h2h0j0Y2i0l1Q0Z0I2j121w0S1T0O130H2m1N0Q0W151y142k2l0y2n2o0P1O2s1R1Z2p0V1W1v2q2t2r190X2y1U2u1P2z250z0A2v1S2w201X2b222A232C1V2x2e1Y2D28210m2G1i290o2B0q0s242H2E2f1j2I260n0p2F1d0r0t272J2g2K2c2L1c2P2d0G0E7E2Q2R2S7F2M2V1a2a7G7H2W7K1b1f1g2X167L2Y1e311l1k2T1h7M7N2U1n7Q1o2Z300B1D1s327R0u330C0D7S347I351E7T38367J170v111C1p7O397U7P3a7V1A7X101z7Y1q0T0F1B1I7Z1r1G181F373b7W3e3x3c833f803g3y848m3h3d85881m3j863A3z3k891H3l1J8a818n3m3B3i3F3C3n3D3G3p878o823E8b8e3q3I3o3r8c3s8f3J3t1K8p3u1L8u8g3H3K8v3v3O3L8h3M3P8d8q3N8i1M8w8j3R3Q3S8r8k3w3V8D2N8x8E3W8s8y3T3X8t8G3U0w3Y8z8l8H8A8L8B403Z2O8F49418C4a8K0x8I4b8M4c4d428J8N434e444f8O8P484g8Y8Z4h908Q914j4i924m938R8X944n954k8S4o4p964l4s5397984t8T9b4q994u4r9c4v4y54459d9e9h8U9a9i9S4w4z559j9n46479f564C8V8W9k4x9g4D579T9l584E9o4H5c4F9U9r4A5d4I4B594J9m9s5e4K4G9p9t9w9u9V5a9x4L4N9W4O9y9X9z4P4Sa19v4Q4T5f4M5b9Y9A4U9C4V5ga24W5j4R9D5k9B5h9qa49E9H4Y9F9I5ma55i4Xa39Z9J4Z5n5la09K5oa850519Ga99L5s5pa6ab5t9N5qac5va75r5u529O5waa9M5z5A9Pad5B9Qae5Cafah5E5D5Nai5x5O9Rak5P5Qag5Rajal5S5yap5F5Taoaq5U5G5Mar5V5Hamatas5W5XaC60aD61aEaF6263aG66aHauaI67av5IaBan5JaJ5Y6869aK6caLaM6daP5K5Law6e6faQ5Z6i6NaRaSaVaxayaN64aO65aW6O6a6jaXaYb1bC6PaT6mazaAb26Qb36b6naUb76RbD6gb4aZ6r6o6hb06p6s6k6t6W6u6Sb56YbE6X6vb86l6T736qbbbF6xbc6w74bdbgb6bebG6y75bhb9bS6z6C766A6D6Z6EbL6F7bbfbHbNba706Gbibj6U77bm6B7cbk6V6IbnbMbT78bI6Hbobrbp71bs6J72bt7dbu7e6Kbl6LbJ797fbKbU7kbv7acF7gbV7lbObq7h7m7nbx6Mc07obPcGbw7ic1bW7j7rbyc27wbQbz7xbX7pbA7yc3c9c47qbR7zcD7sbYbZca7t7AcJcbc5bBcc7Bc6cxc7cdcEc8cecg7ucl7vcKcf7Ccmchcz7DcncycicoctcpcLcAcjcqcrckcBcscucNcvcHcMcCcOcwcPcIcQ"
+PRM["loads"][-2] = ('Y', 'cw1', ('go',))
+PRM.update({'jp': [(4096, 4608), (0, 1536), (1536, 2560), (2560, 3328), (3328, 3840), (3840, 4096)],
+            'copies': [(3, 0, 3840, 'all', ('cg', 0, 3, 1)), (3, 3840, 4480, 'all', ('br', 1, 1, 0)), (3, 4480, 5136, 'all', ('br', 1, 1, 1))],
+            'start': 'J', 'lags': (2, 1, 0), 'alpha': 20, 'f': 1.05, 'hdirect': 'V', 'pair': (), 'half': (), 'iota': 2576, 'mk': 'SSSV'})
+PRM["order"] = "00040P0Q0V0206080a0c0W0e0g1p0i0k01050M1s1t03070S0N090b0d0f0T0h1Y0j1o0R1Z0l23201q0O121C0y0L1w241d1r0U1F13210Y1a1z222529261627171b2819182a1x0X0Z1A1G1L1D1y1O111I2b0z0A1R2f2d1B2g1e1J2c101U2e2j1M2h1E1W2k1H1g1P0m2l1K0o0q2n1N0s2i2m2p0n0p2q0r0t2r2o2s2A4m0K7C7p2B9b0H2C7q2D2F1Q7r7s2G7u1S1T2H7x7v1X2L1f1i2T1h2N7w1V7A2E7y2I0B2J2t1j0G0u2M7B2O0C7D0v2P2Q1u7E2K2R152U2V147I1v7J7F1c0J7G1l347K7T7t2W7z0D1m1n7L2S2X3g7H2Z7M0E0F857O302Y35317P363h32377N7Q7U3i3j7R7V863o7W383k88333p7X8d3l873m3a3r7S89393s3n1k8e7Z3b8a7Y3t3c3u3q803d3x818f823e8b3v0I4e3w8m3y838g3z2u3A8h8c8n8i3f3B8j8o3E3F8k8p8l843G3C8q8t2v8u8r0w3H8v3J3I8w3S3K0x3T8x8y8s3D3U3L8H3V3R3W8I3X3M8z3Y3Z8A3N8G3O8X4840418J8K8L4j8M4243458B8C4k8D8N463P3Q8O47498P8Q4b988E8F8R8S4c8U4d4f8V444h4a8T4P992w8W8Y904O4D4g918Z934l9D4Q4i92962x4R2y4n9E9h4s4o9s944S4T954p974t4q4u4v9F2z9c9G4w4X9d9I4r9i9e4Y9j9H9f4U4y9k504x4V9M4W4z9J9l9a51529K4Z9g9N4A4E544B4F4G9P9n559m4H9O9o9L9p9t4C9q9u9v9T4J579Q4I9U9w9R58564K9r9V9W4L4M5d9X9S9y539x9Y595a5e9z9Z5b9A5g5f9B4N5ca260aP5haJ5k5Ua05l5ia15ma35na59C5p5oa45ya65j5za7aaa95q5A5Bab5Cac5D5Eadae5r5F5xana85sao5G5Hap5Oafaq5I5Jar5Lasag5tah5uaiamat5MajaDau655N5Pav5R5v5waxay5SaAakal5T5VaB5K5X6yaCaEaw5YaG5Z5QaH61636n6zazaF62aUaIaKaMbn6Abc6caNbo64aOaSaV6Bbp67bq6OaQ5W68aRaL6C6D6daT696e6H6a6fbsaW6E666g6I6FbDbraX6J6b6Kb1aYbtb2aZb3b4bu6P6i6h6Qb5bw6jbyb0bx6o6kbE6p6l6qbzb7b66LbF6r6Rb8bA6Sb9bd6Gbabe6mbGbf6W6MbL6t6X6sbgbH6TbM6Nbv6Y6ubIbbbO6vbN6w6Zbibh7570bPbB766UbCbjbJbk786x6V77bl71bK79bUcu72bQbV73bR7h74bSci7i7a7cbX7bbWbmbTbYc17jcvbZ7dc6c0c77k7ec2ckc8cj7f7lc3c9cwcocqcecac47mcb7nccclcfcmcxcpcycr7gcg7oc5cdcscnczchcActcB"
+PRM["order"] = "00040P0W02060Q080a0V0c0e0g0N121s0i0R0M1p0k0S01050307090b0d0f0h1Y0j1t1q0l1Z1o23201r1F240y1z0L130O210T1C22250Y1w1a162617292718281A2a1G1b190Z1D1B1x1d1I1L2d0U0z0A2b1e1y2f1J2c101U2g1O2e1M2j1H2h1W112k2i1h1E0m2l0o0q2n0s2m2p0n0p2q0r0t2r2o2s2A0K0H7p2B2C2D7q2F2t1P7r7s2G7u1g9b2H2I7v1X2L7C1u1R2E7w7x1V7A1f2N2J7y0B2T2K1j0X1Q0G0u2M1K1N7B2O1S0C7D4m2P0v2Q1T2U7E1l2R152V7I1i7F1v147G7J0J7t7K1c7T1m7z1n0D2W342S7L2X7H2Z3g7M0E0F7O85302Y35317P363h32377N7Q7U3i3j7R7V863o7W383k88333p7X0I1k8d3l873r3a7S3m89393s3n8e7Z3b8a7Y3t3c3q3u803d8b8g818f823e3x8m3y833v8c3w8h3A2u3z8n4e8i3B8o8j3f3E3F8k8p3G8l848q8t8r8u3C2v0w3H8v3J3I8w3S3D3K0x3T3L8x8y3U8H3V3W8I3X8z3Y3M8A3Z3R8G8J40418K8X8L483N8s424j433O458B8M8C4k8D8N468O47498P8Q4b3P3Q988E8F8R8S4c8U4d448V8T4h4a4O992w8W8Y904P934D914s4f9D4Q4i92969a2x4R2y4n4l9h944o4g8Z4S9E4T4p974t9s4q954u4v9F2z9c9G4w4X4U9d9I4r9i9e4Y9H9f4V9j4y509k4x9M4z9J519l4W9K524Z9g9N4E4A544F4B4G9P9n9L554H9m9o579p9t4C9q9u9O9v9T4J9Q4I9w9U9R5358564K9r9W4L4M595d9y5a9X9x9S9Y5e5b5c9V9z9Z5U5g9A5f9B4Na25h605k5la05maJa1a35na59C5p5oa45ya65zaa5ia9a75AaP5Bab5Cac5D5q5Eadae5ra85F5xan5j5sao5G5H5Oap5tafaq5J5Iar5Lasagahaiamajat5M5u5Kau656y5NaDav5P5R5Qaxakal5Say6zaA5v5waw5T5VaB5XaCaE5YaG5Z61aHaF63azbn6AaIaKaMaU66bo6cb1aN626naLbc6Bbp64aO6OaS67bqaQ5W686CaR6D6daT696e6H6a6fbsaW6E6I6g6FbtbD6JaXbr6b6Pb2aVaYb3aZb46K6i6hbu6Qb5bw6j6L6S6k6obxb0by6l6pbE6qb7bzb66rbAbFbv6Rb86T6G6m6Wbdb9bebGbabf6MbBbH6t6XbL6sbg6u6YbM6Z6NbIbCbNbbco75706v6wbi6Ubh76bJbO6Vbjcp71bk7877bl6xbKbU7279bPbQbV73bR7h74bSci7a7cbX7b7ibW7dbmbTbY7jc1bZc6c0c77k7ec2ckc8cj7lc3c9cwcqcuceca7fc47mcb7nccclcfcmcxcrcycv7gc5cgcd7ocscnczchcActcB"
 PARTS = PRM["parts"]
 NP = len(PARTS)
 PM = 16 * max(PARTS)
-NU, NF, NB, NH, NRU, NRF, NRB = 46, 19, 36, 19, 13, 7, 8
+NU, NF, NB, NH, NRU, NRF, NRB = 40, 19 if PRM["xs"] == "S" else 16 if PRM["hdirect"] else 7, 44, 4 if PRM["hdirect"] else 19, 10, 4, 8
 
 SCRATCH = {
     "jint": ("sbuf", [128, W], "int32"), "jw": ("sbuf", [128, 2 * D], "float32"),
@@ -48,7 +54,7 @@ SCRATCH = {
     "sti": ("sbuf", [128, 192], "int32"), "sta": ("sbuf", [128, 192], "float32"), "stb": ("sbuf", [128, 192], "float32"),
     "stx": ("sbuf", [128, 224], "float32"), "sty": ("sbuf", [128, 192], "float32"), "stz": ("sbuf", [128, 224], "float32"),
     "smi": ("sbuf", [128, 192], "int32"), "smf": ("sbuf", [128, 192], "float32"), "stu": ("sbuf", [128, 192], "uint16"),
-    "eb": ("sbuf", [128, 2048], "bfloat16"), "ebx": ("sbuf", [128, 2048], "bfloat16"), "blk": ("sbuf", [128, 128], "bfloat16"),
+    "eb": ("sbuf", [128, 2048], "bfloat16"), "ym": ("sbuf", [128, K], "bfloat16"), "blk": ("sbuf", [128, 128], "bfloat16"),
     "idf": ("sbuf", [128, 128], "float32"), "bc8": ("sbuf", [8, 128], "bfloat16"),
     "pidx": ("sbuf", [128, 1], "int32"), "pxi": ("sbuf", [128, 1], "int32"),
     "jl0": ("sbuf", [128, NC], "float32"), "jl": ("sbuf", [128, NC], "float16"),
@@ -66,6 +72,9 @@ for _i in ("xcol", "x16", "ecol", "mb1", "mb2"):
     SCRATCH[_i] = ("sbuf", [128, 1], "float32")
 if PRM["spec"]:
     SCRATCH["vw"] = ("sbuf", [128, 6 * K], "bfloat16")
+if PRM["pair"]:
+    SCRATCH["sp"] = ("sbuf", [128, 2 * K], "bfloat16")
+    SCRATCH["l2"] = ("sbuf", [128, 2 * NC * len(PRM["pair"])], "bfloat16")
 SCRATCH["zz"] = ("sbuf", [128, 6 * NC], "bfloat16")
 SCRATCH["zo"] = ("sbuf", [128, 2 * NC], "bfloat16")
 for _i in ("idb", "idn", "idm", "idh", "idg", "idw"):
@@ -92,7 +101,7 @@ for _n, _d in (("run", "float32"), ("bz", "bfloat16"), ("hs", "bfloat16")):
 for _t, _d in PRM["remc"]:
     SCRATCH["cg%d%d" % (_t, _d)] = ("sbuf", [128, K + NP * SH], "bfloat16")
     SCRATCH["cs%d%d" % (_t, _d)] = ("sbuf", [128, K], "bfloat16")
-SEMAPHORES = ["vq", "sq", "pq", "gq", "snt"] + ["ld%d" % i for i in range(20)] + ["st%d" % i for i in range(10)]
+SEMAPHORES = ["vq", "sq", "pq", "gq", "snt", "go"] + ["ld%d" % i for i in range(20)] + ["st%d" % i for i in range(10)]
 SEMAPHORES += ["r%d" % i for i in range(90)]
 
 
@@ -235,6 +244,9 @@ def emit(g, T, tasks):
             s = t["sem"]
             ins[0].then_inc(T.sem[s], 16)
             count[s] = 16
+        elif t["kind"] == "i":
+            s = t["sem"]
+            count[s] = 1
         else:
             s = "snt"
             count[s] = count.get(s, 0) + t["inc"]
@@ -400,10 +412,13 @@ def rank_program(g, core, T, topo):
         return T[b][:, NC * i:NC * i + NC]
     send([(T.ltl[:, NC:2 * NC], "ltl1", "even", [(rank - 1, lic(0), "li0")]),
           (T.ltl[:, 2 * NC:3 * NC], "ltl2", "odd", [(rank - 1, lic(1), "li1")])], 128)
+    send([(T.ltl[:, 3 * NC:4 * NC], "ltl3", "all", [(rank - 1, lic(4), "li4")])], 128, "li")
     send([(T.ltl[:, 2 * NC:3 * NC], "ltl2", "even", [(rank - 2, lic(2), "li2")]),
-          (T.ltl[:, 3 * NC:4 * NC], "ltl3", "odd", [(rank - 1, lic(4), "li4"), (rank - 3, lic(3), "li3")])], 128, "li")
+          (T.ltl[:, 3 * NC:4 * NC], "ltl3", "odd", [(rank - 3, lic(3), "li3")])], 128, "lj")
+    event["go"] = add(pl, "G", 0.02, [], ["go"], lambda: [g.sem_inc(T.sem.go, 1)], sem="go", kind="i", after=[event["li"]])
     vts(T.zi[:, 0:2 * NC], "zi0", T.li[:, 0:2 * NC], "li0", 15.5, -float(D), A.is_ge, A.mult, None, ["li1"])
-    vts(T.zi[:, 2 * NC:5 * NC], "zi", T.li[:, 2 * NC:5 * NC], "li2", 15.5, -float(D), A.is_ge, A.mult, el(96), ["li3", "li4"])
+    vts(T.zi[:, 2 * NC:4 * NC], "zi", T.li[:, 2 * NC:4 * NC], "li2", 15.5, -float(D), A.is_ge, A.mult, None, ["li3"])
+    vts(lic(4, "zi"), "zi4", lic(4), "li4", 15.5, -float(D), A.is_ge, A.mult)
     vts(T.z0[:], "z0", T.ltl[:, 0:NC], "ltl0", 15.5, -float(D), A.is_ge, A.mult)
     if 0 in PRM["spec"]:
         vts(T.zo[:], "zo", T.ltl[:, NC:3 * NC], "ltl1", 15.5, -float(D), A.is_ge, A.mult, None, ["ltl2"])
@@ -449,10 +464,9 @@ def rank_program(g, core, T, topo):
     vts(T.pm[:], "pm", T.pm0[:], "pm0", T.x16[:, 0:1], None, A.add, None, more=["x16"])
     add(pl, "S", 16 * el(80), ["blk"], ["eb"],
         lambda: [sca.activation(T.eb[:, 128 * x + x:128 * x + 128:16], T.blk[:, x:128:16], F.Copy) for x in range(16)])
-    for a in range(0, 2048, 256):
-        act(T.ebx[:, a:a + 256], "ebx%d" % a, T.eb[:, a:a + 256], ["eb", "xcol"], F.Copy, el(256), scale=T.xcol[:, 0:1])
     for m, c in (("idn", -1.0), ("idm", -0.5), ("idh", D / 2.0), ("idg", -D / 2.0), ("idf", 1.0), ("idw", PM / 2.0)):
-        act(T[m][:], m, T.idb[:], ["idb"], F.Copy, el(128), scale=c)
+        if m != "idf" or "S" in (PRM["xs"], PRM["xs3"]):
+            act(T[m][:], m, T.idb[:], ["idb"], F.Copy, el(128), scale=c)
     memset(T.dl[:], "dl", 1.0 / 16.0, PM)
     memset(T.dl[:, 0:PM:16], "dl", -1000.0)
     memset(T.ha[:], "ha", 1.0, PM / 2)
@@ -465,7 +479,7 @@ def rank_program(g, core, T, topo):
     memset(T.stx[:, 0:16], "stx0", 0.0)
     memset(T.stx[:, 208:224], "stx1", 0.0)
     for t, d in PRM["remc"]:
-        for h in range(NP):
+        for h in range(NP if d == N - 1 or t not in PRM["spec"] else 0):
             a = 16 * C0[h] + SH * h
             memset(T["cg%d%d" % (t, d)][:, a:a + SH], "cgz%d%d.%d" % (t, d, h), 0.0)
 
@@ -608,15 +622,21 @@ def rank_program(g, core, T, topo):
             how = "A" if last else PRM["sums"].get(at + (h,), PRM["sums"].get(at, PRM["sum0"]))
             if not base:
                 how = "B" if how in "AB" else "C"
-            sg, nv = rot("sg", h), None if last else version(at[0] + at[1] + 1) if spec else rot("v", h, 3)
+            if at in PRM["pair"] or held[0]:
+                a = 32 * C0[h] + (nw if held[0] else 0)
+                sg = (T.sp[:, a:a + nw], "sp%d.%d" % (1 if held[0] else 0, h))
+            else:
+                sg = rot("sg", h)
+            nv = None if last else version(at[0] + at[1] + 1) if spec else rot("v", h, 3)
             if how in "BC":
                 if base:
                     gh = rot("gh", h)
                     act(gh[0], gh[1], win.indirect(l[0]), wkeys + [l[1]], F.Identity, ga(nw))
+                    gh = (gh[0], [gh[1]])
                 else:
                     gh = (win, wkeys)
                 src = (T[kt][:, 0:nw], kt)
-                mm([(src[0], T.idb[:], v[0], True, False), (src[0], T.idb[:], gh[0], False, True)], ["idb", v[1], gh[1]], [kt], pe(2, nw))
+                mm([(src[0], T.idb[:], v[0], True, False), (src[0], T.idb[:], gh[0], False, True)], ["idb", v[1]] + gh[1], [kt], pe(2, nw))
                 cl = el(nw)
             else:
                 src = (T.tmf[:, WC[h]], "tmf.%d" % h) if last else rot("tm", h)
@@ -630,6 +650,26 @@ def rank_program(g, core, T, topo):
                 vts(nv[0], nv[1], src[0], src[1], 255.0, -255.0, A.min, A.max, cl)
             if how == "C":
                 vts(sg[0], sg[1], nv[0], nv[1], 0.0, 0.5, A.is_ge, A.subtract, el(nw, 0.5))
+            if at in PRM["pair"]:
+                held[0] = (zn, out, at, sg)
+                return nv, dead, None
+            if held[0]:
+                z1, out1, at1, sg1 = held[0]
+                held[0] = None
+                o, a = T[xc][:, n:3 * n], 32 * C0[h]
+                grp = [(o, T.eb[:, 128 * r:128 * r + 128], T.sp[:, a + r:a + 2 * nw:16], r == 0, False) for r in range(16)]
+                for i, z in enumerate((z1, zn)):
+                    if dead:
+                        grp.append((T[xc][:, n + n * i:2 * n + n * i], T[DP][:], dead[0], False, False))
+                    grp.append((T[xc][:, n + n * i:2 * n + n * i], T.idm[:], z[0], False, i == 1))
+                mm(grp, ["idm", DP, z1[1], zn[1], "eb", sg1[1], sg[1]] + ([dead[1]] if dead else []), [xc], pe(len(grp)))
+                i = take(("l2", h))
+                a = 2 * (NC * i + C0[h])
+                act(T.l2[:, a:a + 2 * n], "l2.%d.%d" % (i, h), o, [xc], F.Sign, bias=0.25 + dc)
+                n1, nd = (T.l2[:, a:a + n], "l2.%d.%d" % (i, h)), new("lb", h)
+                vtt(nd[0], nd[1], n1[0], n1[1], T.l2[:, a + n:a + 2 * n], n1[1], A.min)
+                held[1] = (n1, after(z1, n1, dead, at1, out1))
+                return nv, nd, after(zn, nd, n1, at, out)
             o = T[xc][:, n:2 * n]
             b, w0 = T[sg[2]], 16 * C0[h]
             grp = [(o, T.idm[:], zn[0], True, False)]
@@ -648,9 +688,13 @@ def rank_program(g, core, T, topo):
                 act(nd[0], nd[1], o, [xc], F.Sign, bias=0.25 + dc)
             else:
                 vts(nd[0], nd[1], o, xc, -0.25, -float(D), A.is_le, A.mult)
+            return nv, nd, after(zn, nd, dead, at, out)
+
+        def after(zn, nd, dead, at, out):
+            dt, dc = ([(DP, dead)], DC) if dead else ([], 0.0)
             if out:
                 letter(out[0], [("idn", zn), (DN, nd)] + dt, dc - DC, out[1])
-                return nv, nd, None
+                return None
             if at[1] > 0:
                 a = 3 * (NC * at[0] + C0[h]) + n * (at[1] - 1)
                 nz = (T.zz[:, a:a + n], "zz%d%d.%d" % (at[0], at[1], h))
@@ -659,16 +703,33 @@ def rank_program(g, core, T, topo):
             q = T[ms][:, 0:n]
             lin(q, ms, [("idb", zn), (DP, nd)] + ([(DN, dead)] if dead else []))
             act(nz[0], nz[1], q, [ms], F.Identity, bias=DC - dc)
-            return nv, nd, nz
+            return nz
+
+        held = [None, None]
 
         zn = [part("z0", h), (part("zi", h)[0], "zi0")] + [part("zi", h, d) for d in range(2, N)]
-        nf = [None, (part("zi", h, 1)[0], "zi0"), part("zi", h, 4), None]
+        nf = [None, (part("zi", h, 1)[0], "zi0"), (part("zi", h, 4)[0], "zi4"), None]
         of = [None, part("zo", h, 0), part("zo", h, 1), None]
         lts = [(T.ltl[:, LC[h]], "ltl0")] + [(T.li[:, NC * i + C0[h]:NC * i + C0[h] + n], "li%d" % i) for i in (0, 2, 3)]
         res = []
         ys = [part("y0l", h)]
+
+        def note(deads, dead, j, nz):
+            deads.append(dead)
+            both_ = [(j, nz)]
+            if held[1]:
+                deads[-2] = held[1][0]
+                both_.append((j - 1, held[1][1]))
+                held[1] = None
+            for a, z in both_:
+                if a < 0:
+                    res[-1 - a] = z
+                else:
+                    zn[a] = z
         for t in range(TW):
             le = "all" if t in PRM["lists16"] else "even"
+            if PRM.get("lags"):
+                pl["bias"] = PRM["lags"][t] * (NP - 1 - h)
             todo = [("my%d" % i, res[i], (ys[i], 4 + i)) for i in range(t - 1, -1, -1)] + [("mk0", zn[0], (lts[0], 0))]
             stl = (T.stu[:, NC * t + C0[h]:NC * t + C0[h] + n], "stu")
             if t == 0 or PRM["start"] == "G":
@@ -677,25 +738,47 @@ def rank_program(g, core, T, topo):
                 md = rot("md", h)
                 vtt(md[0], md[1], T["js%d" % t][:, WC[h]], "js%d.%d" % (t, h), T[kt][:, 0:nw], kt, A.mult, el(nw))
                 x = summed(md, todo[0][1])
-                act(T["my%d" % t][:, WC[h]], "my%d.%d" % (t, h), T[kt][:, 0:nw], [kt], F.Copy, el(nw))
+                if t < TW - 1:
+                    act(T["my%d" % t][:, WC[h]], "my%d.%d" % (t, h), T[kt][:, 0:nw], [kt], F.Copy, el(nw))
+                else:
+                    act(T.ym[:, WC[h]], "ym.%d" % h, T[kt][:, 0:nw], [kt, "xcol"], F.Copy, el(nw), scale=T.xcol[:, 0:1])
             l = tolist(x, xa)
             spec = t in PRM["spec"]
-            chain = [keep(x, todo[0][1], PRM["xs"])[1]]
-            if spec:
-                chain[0] = ahead(chain[0], None)
+
+            def clist(x, nxt, z):
+                if spec and PRM["hdirect"]:
+                    zz, b = nxt, new("lf", h)
+                    if z:
+                        zz = new("lb", h)
+                        if PRM["hdirect"] in "VS":
+                            vtt(zz[0], zz[1], z[0], z[1], nxt[0], nxt[1], A.add)
+                        else:
+                            q = T[ms][:, 0:n]
+                            lin(q, ms, [("idb", z), ("idb", nxt)])
+                            act(zz[0], zz[1], q, [ms], F.Copy)
+                    if PRM["hdirect"] == "S":
+                        act(b[0], b[1], x, [xa], F.Copy)
+                        vtt(b[0], b[1], b[0], b[1], zz[0], zz[1], A.add)
+                    else:
+                        vtt(b[0], b[1], x, xa, zz[0], zz[1], A.add)
+                    return tolist(b[0], b[1])
+                terms = keep(x, nxt, PRM["xs"])[1]
+                return ahead(terms, z) if spec else terms
+            chain = [clist(x, todo[0][1], None)]
             for j in range(len(todo)):
                 nxt = todo[j + 1][1] if j < t else zn[1]
                 x = image(l, todo[j][0], nxt)
                 l = tolist(x, xa)
-                chain.append(keep(x, nxt, PRM["xs"])[1])
-                if spec:
-                    chain[-1] = ahead(chain[-1], todo[j][1])
+                chain.append(clist(x, nxt, todo[j][1]))
             br = new("ru", h)
             send([(l[0], l[1], le, [(rank + 1, br[0], br[1])])], 2 * n, ("br", t, 1, h))
             if t:
-                q, my, w0 = T[ms][:, 0:n], T["my%d" % t], 16 * C0[h]
-                mm([(q, T.ebx[:, 128 * r:128 * r + 128], my[:, w0 + r:w0 + nw:16], r == 0, r == 15) for r in range(16)],
-                   ["ebx%d" % a for a in range(0, 2048, 256)] + ["my%d.%d" % (t, h)], [ms], pe(16))
+                q, w0 = T[ms][:, 0:n], 16 * C0[h]
+                yk = "ym.%d" % h
+                if t < TW - 1 or PRM["start"] == "G":
+                    act(T.ym[:, WC[h]], yk, T["my%d" % t][:, WC[h]], ["my%d.%d" % (t, h), "xcol"], F.Copy, el(nw), scale=T.xcol[:, 0:1])
+                mm([(q, T.eb[:, 128 * r:128 * r + 128], T.ym[:, w0 + r:w0 + nw:16], r == 0, r == 15) for r in range(16)],
+                   ["eb", yk], [ms], pe(16))
                 y = new("lb", h)
                 act(y[0], y[1], q, [ms], F.Copy)
                 ys.append(y)
@@ -703,6 +786,7 @@ def rank_program(g, core, T, topo):
                 c = NC * (t + 1) + C0[h]
                 act(T["js%d" % (t + 1)][:, WC[h]], "js%d.%d" % (t + 1, h), T.jw[:].indirect(T.stu[:, c:c + n]), JW + ["stu"], F.Identity, ga(nw))
             home = {}
+            cgk = {}
             for d in range(1, N):
                 x = image(br, "mk%d" % d, nf[d])
                 rem = (t, d) in PRM["remc"]
@@ -718,18 +802,33 @@ def rank_program(g, core, T, topo):
                         vts(b[0], b[1], a[0], a[1], -OFF, None, A.add, None)
                         home[d] = [("idf", b), ("idb", zn[d + 1])]
                         continue
-                b, terms = keep(x, nf[d], PRM["xs"] if d < N - 1 else PRM.get("xs3", PRM["xs"]))
                 if rem:
-                    u = T[xa][:, n:2 * n]
-                    lin(u, xa, terms + ([("idb", of[d])] if spec and of[d] else []))
-                    l = tolist(u, xa)
+                    if d == N - 1:
+                        l = tolist(x, xa)
+                    elif spec and PRM["direct"]:
+                        zz, b = new("lb", h), new("lf", h)
+                        vtt(zz[0], zz[1], of[d][0], of[d][1], nf[d][0], nf[d][1], A.add)
+                        vtt(b[0], b[1], x, xa, zz[0], zz[1], A.add)
+                        l = tolist(b[0], b[1])
+                    else:
+                        b, terms = keep(x, nf[d], PRM["xs"])
+                        u = T[xa][:, n:2 * n]
+                        lin(u, xa, terms + ([("idb", of[d])] if spec and of[d] else []))
+                        l = tolist(u, xa)
                     nm = "%d%d" % (t, d)
-                    cs = (T["cs" + nm][:, WC[h]], "cs%s.%d" % (nm, h))
-                    gather_c(cs, l)
-                    a = 16 * C0[h] + SH * (h + 1)
-                    send([(cs[0], cs[1], PRM["cge"].get((t, d, h), "odd"), [(rank - d, T["cg" + nm][:, a:a + nw], "cg%s.%d" % (nm, h))])],
-                         2 * nw, ("cg", t, d, h))
+                    k = 2 if (t, d) in PRM["half"] else 1
+                    num = int(l[1].split(".")[1])
+                    for i in range(k):
+                        w0, w1 = 16 * C0[h] + i * nw // k, 16 * C0[h] + (i + 1) * nw // k
+                        cs = (T["cs" + nm][:, w0:w1], "cs%s.%d.%d" % (nm, h, i))
+                        li = T.lu[:, NC * num + w0 // 16:NC * num + w1 // 16]
+                        act(cs[0], cs[1], T.cw0[:].indirect(li), CW + [l[1]], F.Identity, ga(nw // k))
+                        a = SH * (h + 1)
+                        send([(cs[0], cs[1], PRM["cge"].get((t, d, h), "odd"),
+                               [(rank - d, T["cg" + nm][:, a + w0:a + w1], "cg%s.%d.%d" % (nm, h, i))])], 2 * nw // k, ("cg", t, d, h))
+                    cgk[d] = ["cg%s.%d.%d" % (nm, h, i) for i in range(k)]
                 else:
+                    b, terms = keep(x, nf[d], PRM["xs"] if d < N - 1 else PRM.get("xs3", PRM["xs"]))
                     a = new("rf" if terms[0][0] == "idf" else "rh", h)
                     send([(b[0], b[1], le if d == N - 1 else PRM["bhe"][t], [(rank - d, a[0], a[1])])],
                          (4 if terms[0][0] == "idf" else 2) * n, ("bh", t, d, h))
@@ -747,11 +846,7 @@ def rank_program(g, core, T, topo):
             fin = t == TW - 1
             for j in range(len(todo)):
                 v, dead, nz = vslot(v, chain[j + 1], todo[j][1], dead, T.cw0[:], CW, (t, j - t), todo[j][2] if fin else None)
-                deads.append(dead)
-                if j < t:
-                    res[t - 1 - j] = nz
-                else:
-                    zn[0] = nz
+                note(deads, dead, j - t, nz)
             for d in range(1, N):
                 out = ((lts[d], d) + ((ys[t], 4 + t) if d == N - 1 else ())) if fin else None
                 if spec and d == N - 2:
@@ -763,12 +858,11 @@ def rank_program(g, core, T, topo):
                 if d in home:
                     v, dead, nz = vslot(v, home[d], zn[d], dead, T["cw%d" % d][:], CK[d], (t, d), out)
                 elif spec and d < N - 1:
-                    v, dead, nz = vslot(v, None, zn[d], dead, T["cg" + nm][:, a + SH:a + SH + nw], "cg%s.%d" % (nm, h), (t, d), out)
+                    v, dead, nz = vslot(v, None, zn[d], dead, T["cg" + nm][:, a + SH:a + SH + nw], cgk[d], (t, d), out)
                 else:
                     v, dead, nz = vslot(v, [("idb", part("jl", h))], zn[d], dead, T["cg" + nm][:, a:a + SH + nw],
-                                        ["cgz%s.%d" % (nm, h), "cg%s.%d" % (nm, h)], (t, d), out)
-                deads.append(dead)
-                zn[d] = nz
+                                        ["cgz%s.%d" % (nm, h)] + cgk[d], (t, d), out)
+                note(deads, dead, d, nz)
             if fin:
                 break
             a = 3 * (NC * t + C0[h])
@@ -809,12 +903,12 @@ def rank_program(g, core, T, topo):
         pl["bias"] = PRM["lag"] * (NP - 1 - h)
         words(h)
     pl["bias"] = 0.0
-    for i, ev in follow + [(event["li"], PRM["liafter"])]:
+    for i, ev in follow + [(event["li"], PRM["liafter"]), (event["lj"], PRM["ljafter"])]:
         if ev:
             pl["tasks"][i]["tdeps"].append(event[ev])
     for i, ev in late:
         for k in ("deps", "tdeps"):
-            pl["tasks"][i][k].append(event[ev] + 1)
+            pl["tasks"][i][k].append(event["go"] if ev == ("go",) else event[ev] + 1)
 
     def olc(b, i):
         return T[b][:, NC * i:NC * i + NC]

from concourse.mybir import AluOpType as A, ActivationFunctionType as F
from concourse.bass import DstId, RemoteDMATransfer

N, K, TW, W = 4, 1024, 3, 4608
NC = K // 16
SH = 16
WIN = SH + 5120
PH = 2048
OFF = float(SH + PH)
D = 5152
PRM = {
    "parts": (32, 32),
    "remc": ((0, 1), (0, 2)),
    "sums": {},
    "sum0": "B", "nd": "S", "xs": "S", "start": "G", "dual": False, "lists16": (1, 2), "lag": 3.0,
    "f": 1.15, "g": 1.56, "hop": 2.3, "mk": "SSSS", "my0": "S", "cwait": 2, "iota": 5152, "copyat": 0, "jwait": 1, "cge": ("even", "odd", "odd"),
    "pe": 0.5, "issue": 0.4, "sync": 0.1, "alpha": 6.0, "nudge": (), "dma": 1.0,
    "jp": [(4096, W), (0, 1024), (1024, 2048), (2048, 3072), (3072, 3584), (3584, 4096)], "row": 0.04, "cp": [(0, 4096)],
    "loads": [("S", "ltl1", 0), ("S", "sti", 0), ("S", "y0n", 0), ("S", "ltn", 0), ("Y", "jint0", 0), ("Y", "jint1", 0), ("Y", "jint2", 0),
              ("Y", "jint3", 0), ("Y", "jint4", 0), ("Y", "jint5", 0), ("Y", "ltl0", "jint3"), ("Y", "ltl2", 0), ("Y", "ltl3", 0),
              ("Y", "cst", 0), ("Y", "cw0", 0), ("Y", "y0l", "cwa0")],
    "copies": [(3, 0, WIN, "odd", None), (2, 0, WIN, "odd", ("cw", 0))],
    "nfe": (("q0", "q2"), ("q0", "q2")), "bhe": ("even", "even", "even"), "spec": (), "order": "", "liafter": None, "ljafter": ("br", 0, 2, 1), "direct": True, "hdirect": "", "pair": (), "half": (),
}
PRM.update({'sum0': 'A', 'alpha': 15, 'f': 1.1, 'hop': 2.3, 'sums': {(2, 0): 'B', (0, 0): 'D', (2, 2): 'C', (1, 2): 'D'},
            'xs3': 'V', 'iota': 1288, 'remc': ((0, 1), (0, 2), (1, 1), (2, 1)), "lists16": (),
            "cge": dict(((0, d, h), "even") for d in (1, 2) for h in (0, 1))})
PRM.update({'lists16': (0, 1, 2), 'cge': dict(((t, d, h), "all") for t in range(3) for d in (1, 2, 3) for h in (0, 1)), 'bhe': ('all', 'all', 'all'),
            'nfe': (('even', 'odd'), ('even', 'odd')), 'xs': 'V',
            'loads': [('Y', 'sti', 0), ('Y', 'y0n', 0), ('S', 'ltl1', 0), ('S', 'ltn', 0), ('S', 'ltl2', 0), ('Y', 'jint0', 0), ('Y', 'jint1', 0),
                      ('Y', 'jint2', 0), ('Y', 'jint3', 0), ('Y', 'jint4', 0), ('Y', 'jint5', 0), ('Y', 'ltl0', 'jint3'), ('Y', 'ltl3', 0),
                      ('Y', 'cst', 0), ('Y', 'cw0', 0), ('Y', 'cw1', ('br', 0, 1, 0)), ('Y', 'y0l', ('cg', 0, 3, 0))],
            'jp': [(4096, 4608), (0, 1408), (1408, 2432), (2432, 3200), (3200, 3712), (3712, 4096)], 'sum0': 'A',
            'remc': ((0, 1), (0, 2), (0, 3), (1, 1), (1, 2), (2, 1), (2, 2)), 'copies': [(3, 0, 5136, 'all', ('cg', 0, 3, 1))],
            'cp': [(0, 2816), (2816, 4096)], 'liafter': ('br', 0, 1, 1), 'spec': (0, 1, 2), 'sums': {(2, -2): 'B', (2, 0): 'B', (1, -1): 'B'}})
PRM["order"] = "00040J0M1t1x0N1u0206080a0c0R0e0g0i0U0L0k010503070K090b0d0f0h2h0j0Y2i0l1Q0Z0I2j121w0S1T0O130H2m1N0Q0W151y142k2l0y2n2o0P1O2s1R1Z2p0V1W1v2q2t2r190X2y1U2u1P2z250z0A2v1S2w201X2b222A232C1V2x2e1Y2D28210m2G1i290o2B0q0s242H2E2f1j2I260n0p2F1d0r0t272J2g2K2c2L1c2P2d0G0E7E2Q2R2S7F2M2V1a2a7G7H2W7K1b1f1g2X167L2Y1e311l1k2T1h7M7N2U1n7Q1o2Z300B1D1s327R0u330C0D7S347I351E7T38367J170v111C1p7O397U7P3a7V1A7X101z7Y1q0T0F1B1I7Z1r1G181F373b7W3e3x3c833f803g3y848m3h3d85881m3j863A3z3k891H3l1J8a818n3m3B3i3F3C3n3D3G3p878o823E8b8e3q3I3o3r8c3s8f3J3t1K8p3u1L8u8g3H3K8v3v3O3L8h3M3P8d8q3N8i1M8w8j3R3Q3S8r8k3w3V8D2N8x8E3W8s8y3T3X8t8G3U0w3Y8z8l8H8A8L8B403Z2O8F49418C4a8K0x8I4b8M4c4d428J8N434e444f8O8P484g8Y8Z4h908Q914j4i924m938R8X944n954k8S4o4p964l4s5397984t8T9b4q994u4r9c4v4y54459d9e9h8U9a9i9S4w4z559j9n46479f564C8V8W9k4x9g4D579T9l584E9o4H5c4F9U9r4A5d4I4B594J9m9s5e4K4G9p9t9w9u9V5a9x4L4N9W4O9y9X9z4P4Sa19v4Q4T5f4M5b9Y9A4U9C4V5ga24W5j4R9D5k9B5h9qa49E9H4Y9F9I5ma55i4Xa39Z9J4Z5n5la09K5oa850519Ga99L5s5pa6ab5t9N5qac5va75r5u529O5waa9M5z5A9Pad5B9Qae5Cafah5E5D5Nai5x5O9Rak5P5Qag5Rajal5S5yap5F5Taoaq5U5G5Mar5V5Hamatas5W5XaC60aD61aEaF6263aG66aHauaI67av5IaBan5JaJ5Y6869aK6caLaM6daP5K5Law6e6faQ5Z6i6NaRaSaVaxayaN64aO65aW6O6a6jaXaYb1bC6PaT6mazaAb26Qb36b6naUb76RbD6gb4aZ6r6o6hb06p6s6k6t6W6u6Sb56YbE6X6vb86l6T736qbbbF6xbc6w74bdbgb6bebG6y75bhb9bS6z6C766A6D6Z6EbL6F7bbfbHbNba706Gbibj6U77bm6B7cbk6V6IbnbMbT78bI6Hbobrbp71bs6J72bt7dbu7e6Kbl6LbJ797fbKbU7kbv7acF7gbV7lbObq7h7m7nbx6Mc07obPcGbw7ic1bW7j7rbyc27wbQbz7xbX7pbA7yc3c9c47qbR7zcD7sbYbZca7t7AcJcbc5bBcc7Bc6cxc7cdcEc8cecg7ucl7vcKcf7Ccmchcz7DcncycicoctcpcLcAcjcqcrckcBcscucNcvcHcMcCcOcwcPcIcQ"
PRM["loads"][-2] = ('Y', 'cw1', ('go',))
PRM.update({'jp': [(4096, 4608), (0, 1536), (1536, 2560), (2560, 3328), (3328, 3840), (3840, 4096)],
            'copies': [(3, 0, 3840, 'all', ('cg', 0, 3, 1)), (3, 3840, 4480, 'all', ('br', 1, 1, 0)), (3, 4480, 5136, 'all', ('br', 1, 1, 1))],
            'start': 'J', 'lags': (2, 1, 0), 'alpha': 20, 'f': 1.05, 'hdirect': 'V', 'pair': (), 'half': (), 'iota': 2576, 'mk': 'SSSV'})
PRM["order"] = "00040P0Q0V0206080a0c0W0e0g1p0i0k01050M1s1t03070S0N090b0d0f0T0h1Y0j1o0R1Z0l23201q0O121C0y0L1w241d1r0U1F13210Y1a1z222529261627171b2819182a1x0X0Z1A1G1L1D1y1O111I2b0z0A1R2f2d1B2g1e1J2c101U2e2j1M2h1E1W2k1H1g1P0m2l1K0o0q2n1N0s2i2m2p0n0p2q0r0t2r2o2s2A4m0K7C7p2B9b0H2C7q2D2F1Q7r7s2G7u1S1T2H7x7v1X2L1f1i2T1h2N7w1V7A2E7y2I0B2J2t1j0G0u2M7B2O0C7D0v2P2Q1u7E2K2R152U2V147I1v7J7F1c0J7G1l347K7T7t2W7z0D1m1n7L2S2X3g7H2Z7M0E0F857O302Y35317P363h32377N7Q7U3i3j7R7V863o7W383k88333p7X8d3l873m3a3r7S89393s3n1k8e7Z3b8a7Y3t3c3u3q803d3x818f823e8b3v0I4e3w8m3y838g3z2u3A8h8c8n8i3f3B8j8o3E3F8k8p8l843G3C8q8t2v8u8r0w3H8v3J3I8w3S3K0x3T8x8y8s3D3U3L8H3V3R3W8I3X3M8z3Y3Z8A3N8G3O8X4840418J8K8L4j8M4243458B8C4k8D8N463P3Q8O47498P8Q4b988E8F8R8S4c8U4d4f8V444h4a8T4P992w8W8Y904O4D4g918Z934l9D4Q4i92962x4R2y4n9E9h4s4o9s944S4T954p974t4q4u4v9F2z9c9G4w4X9d9I4r9i9e4Y9j9H9f4U4y9k504x4V9M4W4z9J9l9a51529K4Z9g9N4A4E544B4F4G9P9n559m4H9O9o9L9p9t4C9q9u9v9T4J579Q4I9U9w9R58564K9r9V9W4L4M5d9X9S9y539x9Y595a5e9z9Z5b9A5g5f9B4N5ca260aP5haJ5k5Ua05l5ia15ma35na59C5p5oa45ya65j5za7aaa95q5A5Bab5Cac5D5Eadae5r5F5xana85sao5G5Hap5Oafaq5I5Jar5Lasag5tah5uaiamat5MajaDau655N5Pav5R5v5waxay5SaAakal5T5VaB5K5X6yaCaEaw5YaG5Z5QaH61636n6zazaF62aUaIaKaMbn6Abc6caNbo64aOaSaV6Bbp67bq6OaQ5W68aRaL6C6D6daT696e6H6a6fbsaW6E666g6I6FbDbraX6J6b6Kb1aYbtb2aZb3b4bu6P6i6h6Qb5bw6jbyb0bx6o6kbE6p6l6qbzb7b66LbF6r6Rb8bA6Sb9bd6Gbabe6mbGbf6W6MbL6t6X6sbgbH6TbM6Nbv6Y6ubIbbbO6vbN6w6Zbibh7570bPbB766UbCbjbJbk786x6V77bl71bK79bUcu72bQbV73bR7h74bSci7i7a7cbX7bbWbmbTbYc17jcvbZ7dc6c0c77k7ec2ckc8cj7f7lc3c9cwcocqcecac47mcb7nccclcfcmcxcpcycr7gcg7oc5cdcscnczchcActcB"
PRM["order"] = "00040P0W02060Q080a0V0c0e0g0N121s0i0R0M1p0k0S01050307090b0d0f0h1Y0j1t1q0l1Z1o23201r1F240y1z0L130O210T1C22250Y1w1a162617292718281A2a1G1b190Z1D1B1x1d1I1L2d0U0z0A2b1e1y2f1J2c101U2g1O2e1M2j1H2h1W112k2i1h1E0m2l0o0q2n0s2m2p0n0p2q0r0t2r2o2s2A0K0H7p2B2C2D7q2F2t1P7r7s2G7u1g9b2H2I7v1X2L7C1u1R2E7w7x1V7A1f2N2J7y0B2T2K1j0X1Q0G0u2M1K1N7B2O1S0C7D4m2P0v2Q1T2U7E1l2R152V7I1i7F1v147G7J0J7t7K1c7T1m7z1n0D2W342S7L2X7H2Z3g7M0E0F7O85302Y35317P363h32377N7Q7U3i3j7R7V863o7W383k88333p7X0I1k8d3l873r3a7S3m89393s3n8e7Z3b8a7Y3t3c3q3u803d8b8g818f823e3x8m3y833v8c3w8h3A2u3z8n4e8i3B8o8j3f3E3F8k8p3G8l848q8t8r8u3C2v0w3H8v3J3I8w3S3D3K0x3T3L8x8y3U8H3V3W8I3X8z3Y3M8A3Z3R8G8J40418K8X8L483N8s424j433O458B8M8C4k8D8N468O47498P8Q4b3P3Q988E8F8R8S4c8U4d448V8T4h4a4O992w8W8Y904P934D914s4f9D4Q4i92969a2x4R2y4n4l9h944o4g8Z4S9E4T4p974t9s4q954u4v9F2z9c9G4w4X4U9d9I4r9i9e4Y9H9f4V9j4y509k4x9M4z9J519l4W9K524Z9g9N4E4A544F4B4G9P9n9L554H9m9o579p9t4C9q9u9O9v9T4J9Q4I9w9U9R5358564K9r9W4L4M595d9y5a9X9x9S9Y5e5b5c9V9z9Z5U5g9A5f9B4Na25h605k5la05maJa1a35na59C5p5oa45ya65zaa5ia9a75AaP5Bab5Cac5D5q5Eadae5ra85F5xan5j5sao5G5H5Oap5tafaq5J5Iar5Lasagahaiamajat5M5u5Kau656y5NaDav5P5R5Qaxakal5Say6zaA5v5waw5T5VaB5XaCaE5YaG5Z61aHaF63azbn6AaIaKaMaU66bo6cb1aN626naLbc6Bbp64aO6OaS67bqaQ5W686CaR6D6daT696e6H6a6fbsaW6E6I6g6FbtbD6JaXbr6b6Pb2aVaYb3aZb46K6i6hbu6Qb5bw6j6L6S6k6obxb0by6l6pbE6qb7bzb66rbAbFbv6Rb86T6G6m6Wbdb9bebGbabf6MbBbH6t6XbL6sbg6u6YbM6Z6NbIbCbNbbco75706v6wbi6Ubh76bJbO6Vbjcp71bk7877bl6xbKbU7279bPbQbV73bR7h74bSci7a7cbX7b7ibW7dbmbTbY7jc1bZc6c0c77k7ec2ckc8cj7lc3c9cwcqcuceca7fc47mcb7nccclcfcmcxcrcycv7gc5cgcd7ocscnczchcActcB"
PARTS = PRM["parts"]
NP = len(PARTS)
PM = 16 * max(PARTS)
NU, NF, NB, NH, NRU, NRF, NRB = 40, 19 if PRM["xs"] == "S" else 16 if PRM["hdirect"] else 7, 44, 4 if PRM["hdirect"] else 19, 10, 4, 8

SCRATCH = {
    "jint": ("sbuf", [128, W], "int32"), "jw": ("sbuf", [128, 2 * D], "float32"),
    "cst": ("sbuf", [128, 512], "bfloat16"),
    "ltn": ("sbuf", [8, N * K], "bfloat16"), "y0n": ("sbuf", [8, K], "bfloat16"),
    "ltl": ("sbuf", [128, N * NC], "bfloat16"), "y0l": ("sbuf", [128, NC], "bfloat16"),
    "li": ("sbuf", [128, 5 * NC], "bfloat16"), "zi": ("sbuf", [128, 5 * NC], "bfloat16"), "z0": ("sbuf", [128, NC], "bfloat16"),
    "sti": ("sbuf", [128, 192], "int32"), "sta": ("sbuf", [128, 192], "float32"), "stb": ("sbuf", [128, 192], "float32"),
    "stx": ("sbuf", [128, 224], "float32"), "sty": ("sbuf", [128, 192], "float32"), "stz": ("sbuf", [128, 224], "float32"),
    "smi": ("sbuf", [128, 192], "int32"), "smf": ("sbuf", [128, 192], "float32"), "stu": ("sbuf", [128, 192], "uint16"),
    "eb": ("sbuf", [128, 2048], "bfloat16"), "ym": ("sbuf", [128, K], "bfloat16"), "blk": ("sbuf", [128, 128], "bfloat16"),
    "idf": ("sbuf", [128, 128], "float32"), "bc8": ("sbuf", [8, 128], "bfloat16"),
    "pidx": ("sbuf", [128, 1], "int32"), "pxi": ("sbuf", [128, 1], "int32"),
    "jl0": ("sbuf", [128, NC], "float32"), "jl": ("sbuf", [128, NC], "float16"),
    "pm0": ("sbuf", [128, NC], "float32"), "pm": ("sbuf", [128, NC], "uint16"),
    "dl": ("sbuf", [128, PM], "float32"), "ha": ("sbuf", [128, PM], "bfloat16"),
    "lu": ("sbuf", [128, NC * NU], "uint16"), "lf": ("sbuf", [128, NC * NF], "float32"),
    "lb": ("sbuf", [128, NC * NB], "bfloat16"), "lh": ("sbuf", [128, NC * NH], "float16"),
    "ru": ("sbuf", [128, NC * NRU], "uint16"), "rf": ("sbuf", [128, NC * NRF], "float32"),
    "rb": ("sbuf", [128, NC * NRB], "bfloat16"), "rh": ("sbuf", [128, NC * NRF], "float16"),
    "mi": ("sbuf", [128, NC * 2], "int32"),
    "ol": ("sbuf", [128, NC * 7], "bfloat16"), "lo": ("sbuf", [128, NC * 3], "bfloat16"),
    "tmf": ("sbuf", [128, K], "bfloat16"), "vo": ("sbuf", [128, K], "bfloat16"),
}
for _i in ("xcol", "x16", "ecol", "mb1", "mb2"):
    SCRATCH[_i] = ("sbuf", [128, 1], "float32")
if PRM["spec"]:
    SCRATCH["vw"] = ("sbuf", [128, 6 * K], "bfloat16")
if PRM["pair"]:
    SCRATCH["sp"] = ("sbuf", [128, 2 * K], "bfloat16")
    SCRATCH["l2"] = ("sbuf", [128, 2 * NC * len(PRM["pair"])], "bfloat16")
SCRATCH["zz"] = ("sbuf", [128, 6 * NC], "bfloat16")
SCRATCH["zo"] = ("sbuf", [128, 2 * NC], "bfloat16")
for _i in ("idb", "idn", "idm", "idh", "idg", "idw"):
    SCRATCH[_i] = ("sbuf", [128, 128], "bfloat16")
BANKS = ["xa0", "xa1", "xc0", "xc1", "kt0", "kt1", "ms0", "ms1"]
for _i in BANKS:
    SCRATCH[_i] = ("psum", [128, 512], "float32")
for _i in range(N):
    if any((_t, _i) not in PRM["remc"] for _t in range(TW)):
        SCRATCH["cw%d" % _i] = ("sbuf", [128, WIN], "bfloat16")
    SCRATCH["mk%d" % _i] = ("sbuf", [128, K], "bfloat16")
for _i in range(TW):
    SCRATCH["my%d" % _i] = ("sbuf", [128, K], "bfloat16")
for _i in range(3):
    SCRATCH["v" + str(_i)] = ("sbuf", [128, K], "bfloat16")
for _i in range(2):
    SCRATCH["md%d" % _i] = ("sbuf", [128, K], "float16")
    if PRM["start"] != "G":
        SCRATCH["js%d" % (_i + 1)] = ("sbuf", [128, K], "float32")
    for _n in ("tm", "sg", "gh"):
        SCRATCH[_n + str(_i)] = ("sbuf", [128, K], "bfloat16")
for _n, _d in (("run", "float32"), ("bz", "bfloat16"), ("hs", "bfloat16")):
    SCRATCH[_n] = ("sbuf", [128, K], _d)
for _t, _d in PRM["remc"]:
    SCRATCH["cg%d%d" % (_t, _d)] = ("sbuf", [128, K + NP * SH], "bfloat16")
    SCRATCH["cs%d%d" % (_t, _d)] = ("sbuf", [128, K], "bfloat16")
SEMAPHORES = ["vq", "sq", "pq", "gq", "snt", "go"] + ["ld%d" % i for i in range(20)] + ["st%d" % i for i in range(10)]
SEMAPHORES += ["r%d" % i for i in range(90)]


def add(pl, eng, cost, reads, writes, fn, sem=None, lat=0.0, inc=None, after=None, kind="c"):
    tasks, last, rd = pl["tasks"], pl["last"], pl["rd"]
    i = len(tasks)
    deps = set(last[k] for k in list(reads) + list(writes) if k in last)
    for k in reads:
        if k in BANKS:
            deps |= set(j for j in rd.get(k, []) if tasks[j]["eng"] != eng)
    for k in writes:
        deps |= set(rd.get(k, []))
    for k in reads:
        rd.setdefault(k, []).append(i)
    for k in writes:
        last[k] = i
        rd[k] = []
    deps.discard(i)
    tdeps = deps if after is None else deps | set(after)
    tasks.append({"eng": eng, "cost": cost, "deps": sorted(deps), "tdeps": sorted(tdeps), "fn": fn, "sem": sem, "lat": lat,
                  "inc": inc, "kind": kind, "bias": pl["bias"], "name": str(list(writes) or list(reads))})
    return i


def order(tasks):
    n = len(tasks)
    succ = [[] for _ in range(n)]
    for i in range(n):
        for j in tasks[i]["tdeps"]:
            succ[j].append(i)
    edge = [[(j, tasks[i]["cost"] + tasks[i]["lat"]
              + (tasks[j]["pre"] if tasks[j]["eng"] == "R" else 0.06 if tasks[j]["eng"] == tasks[i]["eng"] else PRM["sync"])) for j in succ[i]]
            for i in range(n)]
    pri = [0.0] * n
    left = [len(t["tdeps"]) for t in tasks]
    topo = [i for i in range(n) if left[i] == 0]
    for i in topo:
        for j in succ[i]:
            left[j] -= 1
            if left[j] == 0:
                topo.append(j)
    for i in reversed(topo):
        pri[i] = max([pri[j] + c for j, c in edge[i]] + [tasks[i]["cost"] + tasks[i]["lat"]])
    own = [1e6 - i if "first" in tasks[i] else pri[i] + tasks[i]["bias"] for i in range(n)]
    for seed in PRM["nudge"]:
        nudge(own, seed)
    seq, start = run_list(tasks, edge, own, PRM["alpha"])
    if len(PRM["order"]) == 2 * n:
        ch = "0123456789abcdefghijklmnopqrstuvwxyzABCDEFGHIJKLMNOPQRSTUVWXYZ"
        seq = [ch.index(PRM["order"][2 * i]) * 62 + ch.index(PRM["order"][2 * i + 1]) for i in range(n)]
    PRM["span"] = (max(start), max(pri))
    PRM["dbg"] = (tasks, start, pri, succ, edge, own)
    return seq


def nudge(own, seed):
    x = seed * 7919 + 13
    for _ in range(12):
        x = (x * 1103515245 + 12345) % 2147483648
        a = (x >> 8) % len(own)
        x = (x * 1103515245 + 12345) % 2147483648
        own[a] += ((x >> 8) % 1001 - 500) / 200.0


def run_list(tasks, edge, own, alpha):
    n = len(tasks)
    left = [len(tasks[i]["tdeps"]) for i in range(n)]
    rt = [0.0] * n
    start = [0.0] * n
    todo = dict((e, []) for e in "RYGVSP")
    free = dict((e, 0.0) for e in todo)
    for i in range(n):
        if left[i] == 0:
            todo[tasks[i]["eng"]].append(i)
    seq = []
    dma = [0.0] * 4
    while len(seq) < n:
        best = None
        for e in "RYGVSP":
            if todo[e]:
                s = max(free[e], min(rt[a] for a in todo[e]))
                if best is None or s < best[0]:
                    best = (s, e)
        s, e = best
        i = max(todo[e], key=lambda a: (own[a] - alpha * max(0.0, rt[a] - s), -a)) if e != "R" else min(todo[e], key=lambda a: rt[a])
        todo[e].remove(i)
        s = max(s, rt[i])
        if e != "R":
            free[e] = s + tasks[i]["cost"]
        else:
            s = max([s] + [dma[c] for c in tasks[i]["cls"]])
            for c in tasks[i]["cls"]:
                dma[c] = s + tasks[i]["cost"]
        start[i] = s
        seq.append(i)
        for j, c in edge[i]:
            left[j] -= 1
            rt[j] = max(rt[j], s + c)
            if left[j] == 0:
                todo[tasks[j]["eng"]].append(j)
    return seq, start


SEQ = {}


def emit(g, T, tasks):
    if not SEQ:
        SEQ[0] = order(tasks)
    seq = SEQ[0]
    pos = dict((a, b) for b, a in enumerate(seq))
    q = {"V": g.vector, "S": g.scalar, "P": g.tensor, "G": g, "Y": g.sync}
    qsem = {"V": "vq", "S": "sq", "P": "pq", "G": "gq"}
    count = {}
    known = dict((e, {}) for e in q)
    tok = {}
    know = {}
    for i in seq:
        t = tasks[i]
        e = t["eng"]
        if e == "R":
            tok[i] = (t["sem"], t["inc"])
            know[i] = {t["sem"]: t["inc"]}
            continue
        kn = known[e]
        for j in sorted(t["deps"], key=lambda a: -pos[a]):
            s, v = tok[j]
            if kn.get(s, 0) >= v:
                continue
            q[e].wait_ge(T.sem[s], v)
            for s2 in know[j]:
                kn[s2] = max(kn.get(s2, 0), know[j][s2])
        ins = t["fn"]()
        if t["kind"] == "c":
            s = qsem[e]
            for x in ins:
                x.then_inc(T.sem[s], 1)
            count[s] = count.get(s, 0) + len(ins)
        elif t["kind"] == "d":
            s = t["sem"]
            ins[0].then_inc(T.sem[s], 16)
            count[s] = 16
        elif t["kind"] == "i":
            s = t["sem"]
            count[s] = 1
        else:
            s = "snt"
            count[s] = count.get(s, 0) + t["inc"]
        tok[i] = (s, count[s])
        know[i] = dict(kn)
        know[i][s] = count[s]
    for s in count:
        if known["G"].get(s, 0) < count[s]:
            g.wait_ge(T.sem[s], count[s])


def rank_program(g, core, T, topo):
    rank = T.rank_of(core)
    if rank is None:
        return
    pl = {"tasks": [], "last": {}, "rd": {}, "bias": 0.0}
    vec, sca, ten, syn = g.vector, g.scalar, g.tensor, g.sync
    cores = T.cores
    used = {}
    FF, GG, HOP = PRM["f"] * 0.83e-3, PRM["g"], PRM["hop"]
    C0 = [sum(PARTS[:h]) for h in range(NP)]
    LC = [slice(C0[h], C0[h] + PARTS[h]) for h in range(NP)]
    WC = [slice(16 * C0[h], 16 * (C0[h] + PARTS[h])) for h in range(NP)]

    def el(n, c=1.0):
        return max(64, n * c) * FF

    def ga(n):
        return 0.06 + n * GG * FF

    def pe(n, c=64):
        return n * c * PRM["pe"] * FF

    def take(kind):
        used[kind] = used.get(kind, -1) + 1
        return used[kind]

    def new(buf, h):
        n = take((buf, h))
        return (T[buf][:, NC * n + C0[h]:NC * n + C0[h] + PARTS[h]], "%s.%d.%d" % (buf, n, h))

    def rot(kind, h, n=2):
        b = kind + str(take((kind, h)) % n)
        return (T[b][:, WC[h]], "%s.%d" % (b, h), b)

    def part(buf, h, at=0):
        return (T[buf][:, NC * at + C0[h]:NC * at + C0[h] + PARTS[h]], buf)

    def vts(out, ok, in0, ik, s1, s2, op0, op1, cost=None, more=()):
        args = (out, in0, s1, s2, op0) if op1 is None else (out, in0, s1, s2, op0, op1)
        return add(pl, "V", cost or el(0), [ik] + list(more), [ok], lambda: [vec.tensor_scalar(*args)])

    def vtt(out, ok, a, ak, b, bk, op, cost=None):
        return add(pl, "V", cost or el(0), [ak, bk], [ok], lambda: [vec.tensor_tensor(out, a, b, op)])

    def vcp(out, ok, a, ak, cost=None):
        return add(pl, "V", cost or el(0), [ak], [ok], lambda: [vec.tensor_copy(out, a)])

    def act(out, ok, in_, reads, func, cost=None, **kw):
        return add(pl, "S", cost or el(100), reads, [ok], lambda: [sca.activation(out, in_, func, **kw)])

    def scan(out, ok, d0, d0k, d1, d1k, op0, op1, cost):
        return add(pl, "V", cost, [d0k, d1k], [ok], lambda: [vec.tensor_tensor_scan(out, d0, d1, 0.0, op0, op1)])

    def mm(group, reads, writes, cost):
        return add(pl, "P", cost, reads, writes, lambda: [ten.matmul(*x) for x in group])

    def lin(out, bank, terms):
        grp = [(out, T[m][:], l[0], i == 0, i == len(terms) - 1) for i, (m, l) in enumerate(terms)]
        cost = pe(sum(4 if m == "idf" else 1 for m, l in terms))
        return mm(grp, [m for m, l in terms] + [l[1] for m, l in terms], [bank], cost)

    def memset(ap, key, c, n=0):
        return add(pl, "V", el(n), [], [key], lambda: [vec.memset(ap, c)])

    def engines(dst, kind):
        en = topo.engines(core, dst)
        return {"all": en, "even": en[0::2], "odd": en[1::2], "lo": en[:len(en) // 2], "hi": en[len(en) // 2:],
                "q0": en[0::4], "q2": en[2::4]}[kind]

    def landing(i, sem, inc, keys, kind, rows, rb, pre, lat, rate=14.0):
        cls = {"all": (0, 1, 2, 3), "even": (0, 2), "odd": (1, 3), "q0": (0,), "q2": (2,), "q1": (1,), "q3": (3,)}[kind]
        dur = rows / (4.0 * len(cls)) * (PRM["row"] + rb * PRM["dma"] / (1000.0 * rate))
        j = add(pl, "R", dur, [], keys, None, sem=sem, inc=inc, after=[i], lat=lat)
        pl["tasks"][j]["cls"] = cls
        pl["tasks"][j]["pre"] = pre

    def send(trs, rb, name=None):
        made, tot, arr = [], 0, []
        for src, sk, kind, dsts in trs:
            en = engines(cores[dsts[0][0] % N], kind)
            sem = "r%d" % take("r")
            ids = [topo.addr(cores[to % N]) for to, _, _ in dsts]
            made.append((src, sem, ids, [o for _, o, _ in dsts], sum(1 << x for x in en)))
            tot += len(en)
            arr.append((sem, len(en) * len(dsts), [k for _, _, k in dsts], kind))

        def call():
            if len(made) == 1 and len(made[0][2]) == 1:
                src, sem, ids, outs, m = made[0]
                return [g.remote_dma(outs[0], src, T.sem[sem], T.sem.snt, ids[0][1], ids[0][0], m)]
            return [g.remote_dma_fused([RemoteDMATransfer(dst_ids=[DstId(rid=a[0], pnc=a[1]) for a in ids], dma_engine_mask=m,
                                                          remote_sem=T.sem[sem], srcs=[src], dsts=outs)
                                        for src, sem, ids, outs, m in made], local_sem=T.sem.snt)]
        keys = []
        for x in trs:
            keys += x[1] if isinstance(x[1], list) else [x[1]]
        i = add(pl, "G", PRM["issue"], keys, [], call, inc=tot, kind="r")
        pre = HOP - 0.7 + (3.5 if take("first") == 0 else 0.0)
        for sem, n, ks, kind in arr:
            landing(i, sem, n, ks, kind, 128 * len(ks), rb, pre, 0.25, 11.0 if kind == "all" else 13.0)
        event[name] = i
        return i

    def load(eng, out, in_, key, rows, rb, reads=()):
        qq = syn if eng == "Y" else sca
        sem = "ld%d" % take("ld")
        i = add(pl, eng, 0.1, list(reads), [], lambda: [qq.dma_start(out, in_)], sem=sem, kind="d", after=used.get(eng))
        pl["tasks"][i]["first"] = True
        used[eng] = [i]
        landing(i, sem, 16, [key], "all", rows, rb, 1.6, 0.0)

    def store(out, in_, reads, rb):
        sem = "st%d" % take("st")
        i = add(pl, "Y", 0.1, reads, [], lambda: [syn.dma_start(out, in_)], sem=sem, kind="d")
        landing(i, sem, 16, [], "all", 128, rb, 1.6, 0.0)

    def both(k):
        return ["%s.%d" % (k, h) for h in range(NP)]

    event = {}
    late = []

    def letters(eng, d, reads=()):
        s = (rank - d) % N
        load(eng, T.ltl[:, NC * d:NC * d + NC], T.lt[:, K * s:K * s + K], "ltl%d" % d, 128, 128, reads)
    JP = PRM["jp"]
    for eng, what, wait in PRM["loads"]:
        if isinstance(wait, tuple):
            late.append((len(pl["tasks"]), wait))
            wait = None
        wait = [wait] if wait else []
        if what == "sti":
            load(eng, T.sti[:], T.st[:], what, 128, 768, wait)
        elif what == "y0n":
            load(eng, T.y0n[:], T.y0[:], what, 16, 1024, wait)
        elif what == "ltn":
            load(eng, T.ltn[:], T.lt[:], what, 16, 4096, wait)
        elif what == "y0l":
            load(eng, T.y0l[:], T.y0[:], what, 128, 128, wait)
        elif what == "cst":
            load(eng, T.cst[:], T.cf[:, 4096:W], what, 128, 1024, wait)
        elif what[:2] == "cw":
            a, b = PRM["cp"][int(what[2])]
            load(eng, T.cw0[:, SH + a:SH + b], T.cf[:, a:b], "cwa" + what[2], 128, 2 * (b - a), wait)
        elif what[:3] == "ltl":
            letters(eng, int(what[3]), wait)
        else:
            a, b = JP[int(what[4])]
            load(eng, T.jint[:, a:b], T.jm[:, a:b], what, 128, 4 * (b - a), wait)

    def lic(i, b="li"):
        return T[b][:, NC * i:NC * i + NC]
    send([(T.ltl[:, NC:2 * NC], "ltl1", "even", [(rank - 1, lic(0), "li0")]),
          (T.ltl[:, 2 * NC:3 * NC], "ltl2", "odd", [(rank - 1, lic(1), "li1")])], 128)
    send([(T.ltl[:, 3 * NC:4 * NC], "ltl3", "all", [(rank - 1, lic(4), "li4")])], 128, "li")
    send([(T.ltl[:, 2 * NC:3 * NC], "ltl2", "even", [(rank - 2, lic(2), "li2")]),
          (T.ltl[:, 3 * NC:4 * NC], "ltl3", "odd", [(rank - 3, lic(3), "li3")])], 128, "lj")
    event["go"] = add(pl, "G", 0.02, [], ["go"], lambda: [g.sem_inc(T.sem.go, 1)], sem="go", kind="i", after=[event["li"]])
    vts(T.zi[:, 0:2 * NC], "zi0", T.li[:, 0:2 * NC], "li0", 15.5, -float(D), A.is_ge, A.mult, None, ["li1"])
    vts(T.zi[:, 2 * NC:4 * NC], "zi", T.li[:, 2 * NC:4 * NC], "li2", 15.5, -float(D), A.is_ge, A.mult, None, ["li3"])
    vts(lic(4, "zi"), "zi4", lic(4), "li4", 15.5, -float(D), A.is_ge, A.mult)
    vts(T.z0[:], "z0", T.ltl[:, 0:NC], "ltl0", 15.5, -float(D), A.is_ge, A.mult)
    if 0 in PRM["spec"]:
        vts(T.zo[:], "zo", T.ltl[:, NC:3 * NC], "ltl1", 15.5, -float(D), A.is_ge, A.mult, None, ["ltl2"])

    def gsel(ap, key, pat, op, base, cm):
        return add(pl, "G", 0.42, [key], [key], lambda: [g.affine_select(ap, ap, pat, op, 0.0, base, cm)])

    def giota(ap, key, pat, base, cm, n, fl=True):
        kw = {"allow_small_or_imprecise_dtypes": True} if fl else {}
        return add(pl, "G", 0.13 + 2 * n * FF, [], [key], lambda: [g.iota(ap, pat, base, cm, **kw)])
    memset(T.blk[:], "blk", 1.0)
    memset(T.bc8[:], "bc8", 1.0)
    memset(T.idb[:], "idb", 1.0)
    memset(T.eb[:], "eb", 0.0, 1024)
    giota(T.pidx[:], "pidx", [[1, 1]], 0, 1, 1, False)
    gsel(T.bc8[:], "bc8", [[-1, 8], [0, 16]], A.is_equal, 0, 1)
    gsel(T.blk[:], "blk", [[-16, 8], [0, 16]], A.is_ge, 0, 1)
    gsel(T.blk[:], "blk", [[16, 8], [0, 16]], A.is_ge, 15, -1)
    gsel(T.idb[:], "idb", [[-1, 128]], A.is_equal, 0, 1)
    giota(T.smi[:], "smi", [[16, 12], [0, 16]], 0, 1, 192, False)
    giota(T.jl0[:], "jl0", [[16, NC]], -PH, 0, NC)
    giota(T.pm0[:], "pm0", [[1, 16], [256, 4]], 0, 0, NC)
    JW = ["jwz", "jwu", "jwv"]
    nio = PRM["iota"]
    for a in range(0, nio, 1288):
        b = min(nio, a + 1288)
        giota(T.jw[:, D + a:D + b], "jwi%d" % a, [[1, b - a]], a - int(OFF), 0, b - a)
        JW.append("jwi%d" % a)
    for a in range(nio, D, 1288):
        act(T.jw[:, D + a:D + a + 1288], "jwi%d" % a, T.jw[:, D:D + 1288], ["jwi0"], F.Identity, el(1288), bias=float(a))
        JW.append("jwi%d" % a)

    add(pl, "V", el(0), ["pidx"], ["pxi"], lambda: [vec.tensor_scalar(T.pxi[:], T.pidx[:], 15, None, A.bitwise_and)])
    vcp(T.xcol[:], "xcol", T.pxi[:], "pxi")
    vts(T.x16[:], "x16", T.xcol[:], "xcol", 16.0, None, A.mult, None)
    vts(T.ecol[:], "ecol", T.xcol[:], "xcol", -1.0 / 16.0, 15.0 / 16.0, A.mult, A.add)
    vts(T.mb2[:], "mb2", T.xcol[:], "xcol", 14.5, 0.5, A.is_ge, A.mult)
    vtt(T.mb1[:], "mb1", T.xcol[:], "xcol", T.mb2[:], "mb2", A.add)
    vts(T.mb1[:], "mb1", T.mb1[:], "mb1", -1.0, None, A.mult, None)
    vts(T.mb2[:], "mb2", T.mb2[:], "mb2", 1.0, None, A.add, None)
    for h in range(NP):
        vts(T.jl[:, LC[h]], "jl", T.jl0[:, 0:PARTS[h]], "jl0", T.xcol[:, 0:1], None, A.add, None, more=["xcol"])
    vts(T.pm[:], "pm", T.pm0[:], "pm0", T.x16[:, 0:1], None, A.add, None, more=["x16"])
    add(pl, "S", 16 * el(80), ["blk"], ["eb"],
        lambda: [sca.activation(T.eb[:, 128 * x + x:128 * x + 128:16], T.blk[:, x:128:16], F.Copy) for x in range(16)])
    for m, c in (("idn", -1.0), ("idm", -0.5), ("idh", D / 2.0), ("idg", -D / 2.0), ("idf", 1.0), ("idw", PM / 2.0)):
        if m != "idf" or "S" in (PRM["xs"], PRM["xs3"]):
            act(T[m][:], m, T.idb[:], ["idb"], F.Copy, el(128), scale=c)
    memset(T.dl[:], "dl", 1.0 / 16.0, PM)
    memset(T.dl[:, 0:PM:16], "dl", -1000.0)
    memset(T.ha[:], "ha", 1.0, PM / 2)
    memset(T.ha[:, 0:PM:16], "ha", 0.0)
    add(pl, "V", el(512), [], both("bz"), lambda: [vec.memset(T.bz[:], 0.0)])
    memset(T.jw[:, 0:SH], "jwz", 0.0)
    memset(T.jw[:, SH + 4096:D], "jwv", 0.0, 1040)
    memset(T.cw0[:, 0:SH], "cwz", 0.0)
    memset(T.cw0[:, SH + 4096:WIN], "cwu", 0.0, 512)
    memset(T.stx[:, 0:16], "stx0", 0.0)
    memset(T.stx[:, 208:224], "stx1", 0.0)
    for t, d in PRM["remc"]:
        for h in range(NP if d == N - 1 or t not in PRM["spec"] else 0):
            a = 16 * C0[h] + SH * h
            memset(T["cg%d%d" % (t, d)][:, a:a + SH], "cgz%d%d.%d" % (t, d, h), 0.0)

    def onehot(rows, rk, c0, out, eng):
        for h in range(NP):
            bk = ("kt0", "kt1", "ms0", "ms1")[take("mb") % 4]
            n = PARTS[h]
            mm([(T[bk][:, r:16 * n:16], T.bc8[:], rows[:, c0 + NC * r + C0[h]:c0 + NC * r + C0[h] + n], True, True) for r in range(16)],
               ["bc8", rk], [bk], pe(16))
            o, ok = T[out][:, WC[h]], "%s.%d" % (out, h)
            if eng == "V":
                vts(o, ok, T[bk][:, 0:16 * n], bk, 15.0, T.xcol[:, 0:1], A.min, A.is_equal, el(16 * n), ["xcol"])
            else:
                mt = rot("gh", h)
                act(mt[0], mt[1], T[bk][:, 0:16 * n], [bk, "mb1"], F.Abs, el(16 * n), bias=T.mb1[:, 0:1])
                act(o, ok, mt[0], [mt[1], "mb2"], F.Relu, el(16 * n), bias=T.mb2[:, 0:1], scale=-1.0)
    onehot(T.y0n, "y0n", 0, "my0", PRM["my0"])
    for d in range(N):
        onehot(T.ltn, "ltn", K * ((rank - d) % N), "mk%d" % d, PRM["mk"][d])

    vts(T.sta[:], "sta", T.sti[:], "sti", 2.0, -4096.0, A.mult, A.add, el(192))
    vtt(T.stb[:], "stb", T.sti[:], "sti", T.sta[:], "sta", A.max, el(384))
    add(pl, "S", 12 * el(80), ["stb"], ["stx"],
        lambda: [sca.activation(T.stx[:, 16 + 16 * b:32 + 16 * b], T.stb[:, NC * (b // 4) + b % 4:NC * (b // 4) + NC:4], F.Copy) for b in range(12)])
    add(pl, "V", el(192), ["stx"], ["sty"], lambda: [vec.transpose(T.sty[:], T.stx[:, 16:208])])
    add(pl, "V", el(224), ["stx", "stx0", "stx1"], ["stz"], lambda: [vec.transpose(T.stz[:], T.stx[:])])
    add(pl, "V", el(192), ["smi"], ["smi"], lambda: [vec.tensor_scalar(T.smi[:], T.smi[:], 16, None, A.bitwise_and)])
    vts(T.smf[:], "smf", T.smi[:], "smi", 0.0, None, A.is_equal, None, el(192))
    vtt(T.sta[:], "sta", T.sty[:], "sty", T.stz[:, 16:208], "stz", A.subtract, el(384))
    vtt(T.sty[:], "sty", T.sta[:], "sta", T.smf[:], "smf", A.mult, el(384))
    vtt(T.sta[:], "sta", T.sty[:], "sty", T.stz[:, 16:208], "stz", A.add, el(384))
    vts(T.stu[:], "stu", T.sta[:], "sta", float(SH), None, A.add, None, el(192))

    for p, (a0, b0) in enumerate(JP):
        for a in range(a0, b0, 512):
            bk = ("xa0", "xa1", "xc0", "xc1")[take("jb") % 4]
            m = min(512, b0 - a)
            src, ik = T.jint[:, a:a + m], "jint%d" % p
            vts(T[bk][:, 0:m], bk, src, ik, 4096.0, -6144.0, A.max, A.add, el(m))
            if a < 4096:
                JW.append("jw%d" % a)
                vtt(T.jw[:, SH + a:SH + a + m], JW[-1], src, ik, T[bk][:, 0:m], bk, A.add, el(m))
            else:
                add(pl, "V", el(512), [ik, bk], ["jwu", "jwv"],
                    lambda src=src, bk=bk: [vec.tensor_tensor(T.jw[:, SH + 4096:WIN:2], src, T[bk][:], A.add)])
    act(T.cw0[:, SH + 4096:WIN:2], "cwu", T.cst[:], ["cst"], F.Copy, el(512))
    CW = ["cwz", "cwu"] + ["cwa%d" % k for k in range(len(PRM["cp"]))]
    CK = dict((d, []) for d in range(1, N))
    follow = []
    for k, (d, a, b, kind, ev) in enumerate(PRM["copies"]):
        rd = [x for x in CW if x == "cwz" and a < SH or x == "cwu" and b > SH + 4096]
        rd += ["cwa%d" % j for j, (p0, p1) in enumerate(PRM["cp"]) if SH + p0 < b and SH + p1 > a]
        CK[d].append("cw%d.%d" % (d, a))
        follow.append((send([(T.cw0[:, a:b], rd, kind, [(rank - d, T["cw%d" % d][:, a:b], CK[d][-1])])], 2 * (b - a), ("cw", k)), ev))

    ND = PRM["nd"]
    DP, DN, DC = ("idh", "idg", -D / 2.0) if ND == "S" else ("idb", "idn", 0.0)
    finals = {}

    def words(h):
        n, nw = PARTS[h], 16 * PARTS[h]
        xa, xc, kt, ms = ["%s%d" % (b, h % 2) for b in ("xa", "xc", "kt", "ms")]

        def tolist(x, xk, c=0.0):
            l = new("lu", h)
            vts(l[0], l[1], x, xk, OFF + c, 0.0, A.add, A.max)
            return l

        def summed(md, nxt):
            x = T[xa][:, 0:n]
            b, w0 = T[md[2]], 16 * C0[h]
            grp = [(x, T.idn[:], nxt[0], True, False)] if nxt else []
            grp += [(x, T.eb[:, 128 * r:128 * r + 128], b[:, w0 + r:w0 + nw:16], r == 0 and not nxt, r == 15) for r in range(16)]
            mm(grp, ["eb", md[1]] + (["idn", nxt[1]] if nxt else []), [xa], pe(17))
            return x

        def image(l, mask, nxt):
            md = rot("md", h)
            add(pl, "V", ga(nw), JW + [l[1], "%s.%d" % (mask, h)], [md[1]],
                lambda: [vec.tensor_tensor(md[0], T.jw[:].indirect(l[0]), T[mask][:, WC[h]], A.mult)])
            return summed(md, nxt)

        def keep(x, nxt, eng):
            if eng == "S":
                b = new("lf", h)
                act(b[0], b[1], x, [xa], F.Copy)
                return b, [("idf", b)] + ([("idb", nxt)] if nxt else [])
            b = new("lh", h)
            if nxt:
                vtt(b[0], b[1], x, xa, nxt[0], nxt[1], A.add)
            else:
                vcp(b[0], b[1], x, xa)
            return b, [("idb", b)]

        def gather_c(out, l):
            act(out[0], out[1], T.cw0[:].indirect(l[0]), CW + [l[1]], F.Identity, ga(nw))

        def letter(y, terms, c, at):
            q = T[ms][:, 0:n]
            lin(q, ms, [("idb", y)] + terms)
            o = (T.ol[:, NC * at + C0[h]:NC * at + C0[h] + n], "ol%d.%d" % (at, h)) if at is not None else new("lb", h)
            vts(o[0], o[1], q, ms, c, 16.0, A.add, A.min)
            return o

        def version(k):
            a = 6 * 16 * C0[h] + k * nw
            return (T.vw[:, a:a + nw], "vw%d.%d" % (k, h))

        def ahead(base, zn):
            u = T[ms][:, n:2 * n]
            lin(u, ms, base + ([("idb", zn)] if zn else []))
            return tolist(u, ms)

        def choice(deads):
            q = T[ms][:, 0:n]
            lin(q, ms, [("idb", part("jl", h))] + [("idw", x) for x in deads])
            return tolist(q, ms, -SH + nw + len(deads) * nw / 2.0)

        def chosen(l, m):
            v = rot("v", h, 3)
            a = 6 * 16 * C0[h]
            act(v[0], v[1], T.vw[:, a:a + (m + 1) * nw].indirect(l[0]), [version(k)[1] for k in range(m + 1)] + [l[1]], F.Identity, ga(nw))
            return v

        def vslot(v, base, zn, dead, win, wkeys, at, out):
            last = at == (TW - 1, N - 1)
            spec = at[0] in PRM["spec"] and at[1] < N - 1
            u = T[xc][:, 0:n]
            dt, dc = ([(DP, dead)], DC) if dead else ([], 0.0)
            if last:
                lc = letter(out[0], [("idn", zn)], 0.0, None)
                yc = letter(out[2], [(DN, dead)], -DC, None)
            if isinstance(base, tuple):
                l = base
            elif spec:
                l = ahead(base, zn) if base else None
            else:
                lin(u, xc, base + [("idb", zn)] + dt)
                l = tolist(u, xc, dc)
            how = "A" if last else PRM["sums"].get(at + (h,), PRM["sums"].get(at, PRM["sum0"]))
            if not base:
                how = "B" if how in "AB" else "C"
            if at in PRM["pair"] or held[0]:
                a = 32 * C0[h] + (nw if held[0] else 0)
                sg = (T.sp[:, a:a + nw], "sp%d.%d" % (1 if held[0] else 0, h))
            else:
                sg = rot("sg", h)
            nv = None if last else version(at[0] + at[1] + 1) if spec else rot("v", h, 3)
            if how in "BC":
                if base:
                    gh = rot("gh", h)
                    act(gh[0], gh[1], win.indirect(l[0]), wkeys + [l[1]], F.Identity, ga(nw))
                    gh = (gh[0], [gh[1]])
                else:
                    gh = (win, wkeys)
                src = (T[kt][:, 0:nw], kt)
                mm([(src[0], T.idb[:], v[0], True, False), (src[0], T.idb[:], gh[0], False, True)], ["idb", v[1]] + gh[1], [kt], pe(2, nw))
                cl = el(nw)
            else:
                src = (T.tmf[:, WC[h]], "tmf.%d" % h) if last else rot("tm", h)
                add(pl, "V", ga(nw), wkeys + [l[1], v[1]], [src[1]], lambda: [vec.tensor_tensor(src[0], win.indirect(l[0]), v[0], A.add)])
                cl = el(nw, 0.5)
            if how in "AB" and not (last and h == NP - 1):
                act(sg[0], sg[1], src[0], [src[1]], F.Sign, el(nw), bias=0.5)
            elif how != "C":
                vts(sg[0], sg[1], src[0], src[1], 0.0, 0.5, A.is_ge, A.subtract, el(nw, 0.5))
            if nv:
                vts(nv[0], nv[1], src[0], src[1], 255.0, -255.0, A.min, A.max, cl)
            if how == "C":
                vts(sg[0], sg[1], nv[0], nv[1], 0.0, 0.5, A.is_ge, A.subtract, el(nw, 0.5))
            if at in PRM["pair"]:
                held[0] = (zn, out, at, sg)
                return nv, dead, None
            if held[0]:
                z1, out1, at1, sg1 = held[0]
                held[0] = None
                o, a = T[xc][:, n:3 * n], 32 * C0[h]
                grp = [(o, T.eb[:, 128 * r:128 * r + 128], T.sp[:, a + r:a + 2 * nw:16], r == 0, False) for r in range(16)]
                for i, z in enumerate((z1, zn)):
                    if dead:
                        grp.append((T[xc][:, n + n * i:2 * n + n * i], T[DP][:], dead[0], False, False))
                    grp.append((T[xc][:, n + n * i:2 * n + n * i], T.idm[:], z[0], False, i == 1))
                mm(grp, ["idm", DP, z1[1], zn[1], "eb", sg1[1], sg[1]] + ([dead[1]] if dead else []), [xc], pe(len(grp)))
                i = take(("l2", h))
                a = 2 * (NC * i + C0[h])
                act(T.l2[:, a:a + 2 * n], "l2.%d.%d" % (i, h), o, [xc], F.Sign, bias=0.25 + dc)
                n1, nd = (T.l2[:, a:a + n], "l2.%d.%d" % (i, h)), new("lb", h)
                vtt(nd[0], nd[1], n1[0], n1[1], T.l2[:, a + n:a + 2 * n], n1[1], A.min)
                held[1] = (n1, after(z1, n1, dead, at1, out1))
                return nv, nd, after(zn, nd, n1, at, out)
            o = T[xc][:, n:2 * n]
            b, w0 = T[sg[2]], 16 * C0[h]
            grp = [(o, T.idm[:], zn[0], True, False)]
            if dead:
                grp.append((o, T[DN if last else DP][:], dead[0], False, False))
            grp += [(o, T.eb[:, 128 * r:128 * r + 128], b[:, w0 + r:w0 + nw:16], False, r == 15) for r in range(16)]
            mm(grp, ["idm", DP, DN, zn[1], "eb", sg[1]] + ([dead[1]] if dead else []), [xc], pe(18))
            if last:
                x = new("lb", h)
                vts(x[0], x[1], o, xc, -0.25 + dc, 16.0, A.is_le, A.mult)
                for a, i in ((lc, out[1]), (yc, out[3])):
                    vtt(T.ol[:, NC * i + C0[h]:NC * i + C0[h] + n], "ol%d.%d" % (i, h), x[0], x[1], a[0], a[1], A.max)
                return None, None, None
            nd = new("lb", h)
            if ND == "S":
                act(nd[0], nd[1], o, [xc], F.Sign, bias=0.25 + dc)
            else:
                vts(nd[0], nd[1], o, xc, -0.25, -float(D), A.is_le, A.mult)
            return nv, nd, after(zn, nd, dead, at, out)

        def after(zn, nd, dead, at, out):
            dt, dc = ([(DP, dead)], DC) if dead else ([], 0.0)
            if out:
                letter(out[0], [("idn", zn), (DN, nd)] + dt, dc - DC, out[1])
                return None
            if at[1] > 0:
                a = 3 * (NC * at[0] + C0[h]) + n * (at[1] - 1)
                nz = (T.zz[:, a:a + n], "zz%d%d.%d" % (at[0], at[1], h))
            else:
                nz = new("lb", h)
            q = T[ms][:, 0:n]
            lin(q, ms, [("idb", zn), (DP, nd)] + ([(DN, dead)] if dead else []))
            act(nz[0], nz[1], q, [ms], F.Identity, bias=DC - dc)
            return nz

        held = [None, None]

        zn = [part("z0", h), (part("zi", h)[0], "zi0")] + [part("zi", h, d) for d in range(2, N)]
        nf = [None, (part("zi", h, 1)[0], "zi0"), (part("zi", h, 4)[0], "zi4"), None]
        of = [None, part("zo", h, 0), part("zo", h, 1), None]
        lts = [(T.ltl[:, LC[h]], "ltl0")] + [(T.li[:, NC * i + C0[h]:NC * i + C0[h] + n], "li%d" % i) for i in (0, 2, 3)]
        res = []
        ys = [part("y0l", h)]

        def note(deads, dead, j, nz):
            deads.append(dead)
            both_ = [(j, nz)]
            if held[1]:
                deads[-2] = held[1][0]
                both_.append((j - 1, held[1][1]))
                held[1] = None
            for a, z in both_:
                if a < 0:
                    res[-1 - a] = z
                else:
                    zn[a] = z
        for t in range(TW):
            le = "all" if t in PRM["lists16"] else "even"
            if PRM.get("lags"):
                pl["bias"] = PRM["lags"][t] * (NP - 1 - h)
            todo = [("my%d" % i, res[i], (ys[i], 4 + i)) for i in range(t - 1, -1, -1)] + [("mk0", zn[0], (lts[0], 0))]
            stl = (T.stu[:, NC * t + C0[h]:NC * t + C0[h] + n], "stu")
            if t == 0 or PRM["start"] == "G":
                x = image(stl, "my%d" % t, todo[0][1])
            else:
                md = rot("md", h)
                vtt(md[0], md[1], T["js%d" % t][:, WC[h]], "js%d.%d" % (t, h), T[kt][:, 0:nw], kt, A.mult, el(nw))
                x = summed(md, todo[0][1])
                if t < TW - 1:
                    act(T["my%d" % t][:, WC[h]], "my%d.%d" % (t, h), T[kt][:, 0:nw], [kt], F.Copy, el(nw))
                else:
                    act(T.ym[:, WC[h]], "ym.%d" % h, T[kt][:, 0:nw], [kt, "xcol"], F.Copy, el(nw), scale=T.xcol[:, 0:1])
            l = tolist(x, xa)
            spec = t in PRM["spec"]

            def clist(x, nxt, z):
                if spec and PRM["hdirect"]:
                    zz, b = nxt, new("lf", h)
                    if z:
                        zz = new("lb", h)
                        if PRM["hdirect"] in "VS":
                            vtt(zz[0], zz[1], z[0], z[1], nxt[0], nxt[1], A.add)
                        else:
                            q = T[ms][:, 0:n]
                            lin(q, ms, [("idb", z), ("idb", nxt)])
                            act(zz[0], zz[1], q, [ms], F.Copy)
                    if PRM["hdirect"] == "S":
                        act(b[0], b[1], x, [xa], F.Copy)
                        vtt(b[0], b[1], b[0], b[1], zz[0], zz[1], A.add)
                    else:
                        vtt(b[0], b[1], x, xa, zz[0], zz[1], A.add)
                    return tolist(b[0], b[1])
                terms = keep(x, nxt, PRM["xs"])[1]
                return ahead(terms, z) if spec else terms
            chain = [clist(x, todo[0][1], None)]
            for j in range(len(todo)):
                nxt = todo[j + 1][1] if j < t else zn[1]
                x = image(l, todo[j][0], nxt)
                l = tolist(x, xa)
                chain.append(clist(x, nxt, todo[j][1]))
            br = new("ru", h)
            send([(l[0], l[1], le, [(rank + 1, br[0], br[1])])], 2 * n, ("br", t, 1, h))
            if t:
                q, w0 = T[ms][:, 0:n], 16 * C0[h]
                yk = "ym.%d" % h
                if t < TW - 1 or PRM["start"] == "G":
                    act(T.ym[:, WC[h]], yk, T["my%d" % t][:, WC[h]], ["my%d.%d" % (t, h), "xcol"], F.Copy, el(nw), scale=T.xcol[:, 0:1])
                mm([(q, T.eb[:, 128 * r:128 * r + 128], T.ym[:, w0 + r:w0 + nw:16], r == 0, r == 15) for r in range(16)],
                   ["eb", yk], [ms], pe(16))
                y = new("lb", h)
                act(y[0], y[1], q, [ms], F.Copy)
                ys.append(y)
            if t + 1 < TW and PRM["start"] != "G":
                c = NC * (t + 1) + C0[h]
                act(T["js%d" % (t + 1)][:, WC[h]], "js%d.%d" % (t + 1, h), T.jw[:].indirect(T.stu[:, c:c + n]), JW + ["stu"], F.Identity, ga(nw))
            home = {}
            cgk = {}
            for d in range(1, N):
                x = image(br, "mk%d" % d, nf[d])
                rem = (t, d) in PRM["remc"]
                if d < N - 1:
                    l = tolist(x, xa)
                    br = new("ru", h)
                    to = [(rank + 1, br[0], br[1])]
                    if PRM["dual"] and not rem:
                        a, b = new("ru", h), new("lf", h)
                        to.append((rank - d, a[0], a[1]))
                    send([(l[0], l[1], le, to)], 2 * n, ("br", t, d + 1, h))
                    if PRM["dual"] and not rem:
                        vts(b[0], b[1], a[0], a[1], -OFF, None, A.add, None)
                        home[d] = [("idf", b), ("idb", zn[d + 1])]
                        continue
                if rem:
                    if d == N - 1:
                        l = tolist(x, xa)
                    elif spec and PRM["direct"]:
                        zz, b = new("lb", h), new("lf", h)
                        vtt(zz[0], zz[1], of[d][0], of[d][1], nf[d][0], nf[d][1], A.add)
                        vtt(b[0], b[1], x, xa, zz[0], zz[1], A.add)
                        l = tolist(b[0], b[1])
                    else:
                        b, terms = keep(x, nf[d], PRM["xs"])
                        u = T[xa][:, n:2 * n]
                        lin(u, xa, terms + ([("idb", of[d])] if spec and of[d] else []))
                        l = tolist(u, xa)
                    nm = "%d%d" % (t, d)
                    k = 2 if (t, d) in PRM["half"] else 1
                    num = int(l[1].split(".")[1])
                    for i in range(k):
                        w0, w1 = 16 * C0[h] + i * nw // k, 16 * C0[h] + (i + 1) * nw // k
                        cs = (T["cs" + nm][:, w0:w1], "cs%s.%d.%d" % (nm, h, i))
                        li = T.lu[:, NC * num + w0 // 16:NC * num + w1 // 16]
                        act(cs[0], cs[1], T.cw0[:].indirect(li), CW + [l[1]], F.Identity, ga(nw // k))
                        a = SH * (h + 1)
                        send([(cs[0], cs[1], PRM["cge"].get((t, d, h), "odd"),
                               [(rank - d, T["cg" + nm][:, a + w0:a + w1], "cg%s.%d.%d" % (nm, h, i))])], 2 * nw // k, ("cg", t, d, h))
                    cgk[d] = ["cg%s.%d.%d" % (nm, h, i) for i in range(k)]
                else:
                    b, terms = keep(x, nf[d], PRM["xs"] if d < N - 1 else PRM.get("xs3", PRM["xs"]))
                    a = new("rf" if terms[0][0] == "idf" else "rh", h)
                    send([(b[0], b[1], le if d == N - 1 else PRM["bhe"][t], [(rank - d, a[0], a[1])])],
                         (4 if terms[0][0] == "idf" else 2) * n, ("bh", t, d, h))
                    home[d] = [(terms[0][0], a)] + ([("idb", zn[d + 1])] if len(terms) > 1 else [])
            if spec:
                l, v = chain[0], version(0)
            else:
                u = T[xc][:, 0:n]
                lin(u, xc, chain[0])
                l = tolist(u, xc)
                v = rot("v", h, 3)
            gather_c(v, l)
            dead = None
            deads = []
            fin = t == TW - 1
            for j in range(len(todo)):
                v, dead, nz = vslot(v, chain[j + 1], todo[j][1], dead, T.cw0[:], CW, (t, j - t), todo[j][2] if fin else None)
                note(deads, dead, j - t, nz)
            for d in range(1, N):
                out = ((lts[d], d) + ((ys[t], 4 + t) if d == N - 1 else ())) if fin else None
                if spec and d == N - 2:
                    pick = choice(deads)
                if spec and d == N - 1:
                    v = chosen(pick, len(deads))
                nm = "%d%d" % (t, d)
                a = 16 * C0[h] + SH * h
                if d in home:
                    v, dead, nz = vslot(v, home[d], zn[d], dead, T["cw%d" % d][:], CK[d], (t, d), out)
                elif spec and d < N - 1:
                    v, dead, nz = vslot(v, None, zn[d], dead, T["cg" + nm][:, a + SH:a + SH + nw], cgk[d], (t, d), out)
                else:
                    v, dead, nz = vslot(v, [("idb", part("jl", h))], zn[d], dead, T["cg" + nm][:, a:a + SH + nw],
                                        ["cgz%s.%d" % (nm, h)] + cgk[d], (t, d), out)
                note(deads, dead, d, nz)
            if fin:
                break
            a = 3 * (NC * t + C0[h])
            b = 4 * (NC * t + C0[h])
            of = [None] + [(T.rb[:, b + 2 * n * i:b + 2 * n * i + n], "rb%d%d.%d" % (t, i, h)) for i in range(2)] + [None]
            nf = [None] + [(T.rb[:, b + 2 * n * i + n:b + 2 * n * i + 2 * n], "rb%d%d.%d" % (t, i, h)) for i in range(2)] + [None]
            if t + 1 in PRM["spec"] and ((t + 1, 1) in PRM["remc"] or (t + 1, 2) in PRM["remc"]):
                send([(T.zz[:, a + n * i:a + n * i + 2 * n], [zn[i + 1][1], zn[i + 2][1]], PRM["nfe"][t][i],
                       [(rank + 1 + i, T.rb[:, b + 2 * n * i:b + 2 * n * i + 2 * n], nf[i + 1][1])]) for i in range(2)], 4 * n, ("nf", t, h))
            else:
                send([(zn[i + 2][0], zn[i + 2][1], PRM["nfe"][t][i], [(rank + 1 + i, nf[i + 1][0], nf[i + 1][1])]) for i in range(2)],
                     2 * n, ("nf", t, h))
            if ND == "S":
                r = new("lb", h)
                act(r[0], r[1], dead[0], [dead[1]], F.Identity, scale=D / 2.0, bias=DC)
                res.append(r)
            else:
                res.append(dead)
            w0, nb = 16 * C0[h], nw // 128
            vb = T[v[2]]
            ru, rk, bzk, hsk = T.run[:, WC[h]], "run.%d" % h, "bz.%d" % h, "hs.%d" % h
            mm([(T[kt][:, 128 * k:128 * k + 128], vb[:, w0 + 128 * k:w0 + 128 * k + 128], T.idb[:], True, True) for k in range(nb)],
               [v[1], "idb"], [kt], pe(nb, 128))
            scan(ru, rk, T.dl[:, 0:nw], "dl", T[kt][:, 0:nw], kt, A.add, A.max, el(nw))
            mi, mk_ = T.mi[:, NC * t + C0[h]:NC * t + C0[h] + n], "mi%d.%d" % (t, h)
            top = T.run[:, w0 + 15:w0 + nw:16]
            vts(mi, mk_, top, rk, -15.0 / 32.0, None, A.add, None)
            vtt(T.bz[:, w0:w0 + nw:16], bzk, top, rk, mi, mk_, A.subtract)
            scan(T.hs[:, WC[h]], hsk, T.ha[:, 0:nw], "ha", T.bz[:, WC[h]], bzk, A.mult, A.add, el(nw, 0.5))
            mm([(T[kt][:, 128 * k:128 * k + 128], T.hs[:, w0 + 128 * k:w0 + 128 * k + 128], T.idb[:], True, True) for k in range(nb)],
               [hsk, "idb"], [kt], pe(nb, 128))
            if PRM["start"] == "G":
                vts(T["my%d" % (t + 1)][:, WC[h]], "my%d.%d" % (t + 1, h), T[kt][:, 0:nw], kt, T.ecol[:, 0:1], None, A.is_equal, None, el(nw), ["ecol"])
            else:
                vts(T[kt][:, 0:nw], kt, T[kt][:, 0:nw], kt, T.ecol[:, 0:1], None, A.is_equal, None, el(nw), ["ecol"])

    for h in range(NP):
        pl["bias"] = PRM["lag"] * (NP - 1 - h)
        words(h)
    pl["bias"] = 0.0
    for i, ev in follow + [(event["li"], PRM["liafter"]), (event["lj"], PRM["ljafter"])]:
        if ev:
            pl["tasks"][i]["tdeps"].append(event[ev])
    for i, ev in late:
        for k in ("deps", "tdeps"):
            pl["tasks"][i][k].append(event["go"] if ev == ("go",) else event[ev] + 1)

    def olc(b, i):
        return T[b][:, NC * i:NC * i + NC]
    for k in range(2):
        add(pl, "V", ga(K // 2), both("tmf") + (both("ol3") if k else []) + ["pm"], ["vo%d" % k],
            lambda k=k: [vec.tensor_scalar(T.vo[:, 512 * k:512 * k + 512], T.tmf[:].indirect(T.pm[:, 32 * k:32 * k + 32]), 255.0, -255.0, A.min, A.max)])
    store(T.yv[:], T.vo[:], ["vo0", "vo1"], 2048)
    for d in range(1, N):
        send([(olc("ol", d), both("ol%d" % d), "all", [(rank + d, olc("lo", d - 1), "lo%d" % d)])], 128)
    for t in range(TW):
        store(T.yi[:, K * t:K * t + K], olc("ol", 4 + t), both("ol%d" % (4 + t)) + (["vo1"] if t == TW - 1 else []), 128)
    store(T.yl[:, K * rank:K * rank + K], olc("ol", 0), both("ol0"), 128)
    for d in range(1, N):
        s = (rank - d) % N
        store(T.yl[:, K * s:K * s + K], olc("lo", d - 1), ["lo%d" % d], 128)
    emit(g, T, pl["tasks"])
